import numpy as np
import ml_dtypes


def mxq(x, axis, fmt="e4m3"):
    dtype, down = {"e4m3": (ml_dtypes.float8_e4m3fn, 7), "e5m2": (ml_dtypes.float8_e5m2, 14)}[fmt]
    v = np.moveaxis(np.asarray(x, np.float32).astype(ml_dtypes.bfloat16).astype(np.float64), axis, -1)
    blocks = v.reshape(v.shape[:-1] + (-1, 32))
    amax = np.abs(blocks).max(-1, keepdims=True)
    byte = np.maximum(np.where(amax > 0, np.frexp(amax)[1] - 1 + 127, 0) - down, 1)
    scale = np.exp2(byte - 127.0)
    codes = (blocks / scale).astype(np.float32).astype(dtype).astype(np.float64)
    return np.moveaxis((codes * scale).reshape(v.shape), -1, axis)


WIDE = False


def mx_kscale(k):
    if not WIDE:
        return np.ones(k)
    levels = np.array([10, -10, 5, -5, 0])
    if k % 512:
        return np.exp2(np.random.permutation(np.resize(levels, k // 32))).repeat(32)
    a = np.empty((k // 512, 16))
    for p in range(k // 512):
        a[p, :8] = np.random.permutation(np.resize(levels, 8))
        for g in range(8):
            far = levels[np.abs(levels - a[p, g]) >= 10]
            a[p, g + 8] = far[np.random.randint(len(far))]
    return np.exp2(a.ravel()).repeat(32)


def f64(x):
    return np.asarray(x).astype(np.float64)


def striped(idx):
    return np.tile(idx.reshape(-1, 16).T, (8, 1)).astype(np.uint16)


def unstriped(offs):
    return offs[:16].T.reshape(-1).astype(np.int64)


K, T, E, C, N = 128, 1024, 8, 128, 1536


def by_expert(wq, xq):
    return np.concatenate([wq[e].T @ xq[:, e * C:(e + 1) * C] for e in range(E)], axis=1)


def setup_inputs():
    n = np.random.standard_normal
    s = mx_kscale(N)[:, None]
    return {
        "dyT": (n((N, T)) * s).astype(np.float32),
        "w": (n((E, N, K)) / np.sqrt(N) / s[None]).astype(np.float32),
        "gate": np.tile(np.random.uniform(0.2, 1.0, E * C), (N, 1)).astype(np.float32),
        "offs": striped(np.random.permutation(T)[:E * C]),
    }


def reference(dyT, w, gate, offs):
    idx = unstriped(offs)
    gq = mxq(f64(gate) * f64(dyT)[:, idx], 0, "e4m3")
    dx = by_expert(mxq(f64(w), 1, "e4m3"), gq)
    out = np.zeros((K, T))
    out[:, idx] = dx
    return out

@@ -1,0 +1,228 @@
+from contextlib import ExitStack
+
+import concourse.mybir as mybir
+
+F32 = mybir.dt.float32
+BF16 = mybir.dt.bfloat16
+U32 = mybir.dt.uint32
+U16 = mybir.dt.uint16
+U8 = mybir.dt.uint8
+FP8X4 = mybir.dt.float8_e4m3fn_x4
+MULT = mybir.AluOpType.mult
+
+K, T, E, C, N = 128, 1024, 8, 128, 1536
+S = E * C
+P = 128
+PACK = 4
+K_PASS = P * PACK
+PASSES = N // K_PASS
+PAD = 32
+RUN = 4
+LOADS = [(x[0], int(x[1]), int(x[2])) for x in "y01 y02 w00 w01 y03 y10 w02 y11 w03 w10 y12 y13 w11 w12 w13 y20 y21 y22 y23 w20 w21 w22 w23".split(" ")]
+
+FLOPS = 2 * K * N * S
+BYTES = 4 * (N * T + E * N * K + K * T + S) + 2 * S
+
+
+def tile_moe_bdx_lin_none_kernel(tc, dyT, w, gate, offs, out):
+    nc = tc.nc
+    with ExitStack() as ctx:
+        keep = ctx.enter_context(tc.tile_pool(name="keep", bufs=1))
+        stage = ctx.enter_context(tc.tile_pool(name="stage", bufs=2))
+        psum = ctx.enter_context(tc.psum_pool(name="psum", bufs=1))
+
+        offsets = keep.tile([P, S // 16], U16, name="offsets")
+        gates = keep.tile([P, S], F32, name="gates")
+        windows = {}
+        w_raw = {}
+        for c in range(PASSES):
+            for t in range(PACK):
+                width = T + PAD if c < 2 else T
+                windows[c, t] = keep.tile([P, width], F32, name=f"win{c}{t}")
+                if c < 2:
+                    nc.gpsimd.memset(windows[c, t][:, T:width], 0.0)
+            for h in range(2):
+                w_raw[c, h] = keep.tile([P, 4, PACK, K], F32, name=f"wraw{c}{h}")
+        g_codes = keep.tile([P, PASSES, S], U32, align_bytes=64, name="g_codes")
+        g_scales = keep.tile([P, PASSES, S], U8, align_bytes=64, name="g_scales")
+        w_codes = keep.tile([P, PASSES, E * K], U32, align_bytes=64, name="w_codes")
+        w_scales = keep.tile([P, PASSES, E * K], U8, align_bytes=64, name="w_scales")
+        result = keep.tile([P, T], F32, name="result")
+        slots = keep.tile([P, S], F32, name="slots")
+        acc = [psum.tile([P, 2 * C], F32, name=f"acc{b}") for b in range(E // 2)]
+
+        dy_rows = dyT.rearrange("(c p j) t -> c p j t", p=P, j=PACK)
+        w_rows = w.rearrange("e (c p j) k -> c p e (j k)", p=P, j=PACK)
+
+        def load_window(c, t):
+            nc.sync.dma_start(out=windows[c, t][:, 0:T], in_=dy_rows[c, :, t, :])
+
+        def load_w(c, h):
+            nc.sync.dma_start(
+                out=w_raw[c, h // 2][:, 2 * (h % 2) : 2 * (h % 2) + 2].rearrange("p e j k -> p e (j k)"),
+                in_=w_rows[c, :, 2 * h : 2 * h + 2, :],
+            )
+
+        def load_gates(s0, s1):
+            nc.sync.dma_start(out=gates[:, s0:s1], in_=gate[0:P, s0:s1])
+
+        gathered = {}
+
+        def new_gathered(c, q, n):
+            gathered[c, q] = stage.tile([P, PACK, n], F32, tag="gathered", bufs=2, name=f"gathered{c}{q}")
+
+        def gather(c, q, t, s0, n):
+            nc.vector.tensor_tensor(
+                gathered[c, q][:, t, :],
+                windows[c, t][:].indirect(offsets[:, s0 // 16 : (s0 + n) // 16]),
+                gates[:, s0 : s0 + n],
+                MULT,
+            )
+
+        mixed = {}
+
+        def new_mixed(c, q, n):
+            mixed[c, q] = stage.tile([P, n, PACK], BF16, align_bytes=64, tag=f"mixed{n}", bufs=2, name=f"mixed{c}{q}")
+
+        def mix(dst, src):
+            nc.scalar.copy(
+                out=dst.rearrange("p (n i) t -> p n t i", i=RUN),
+                in_=src.rearrange("p t (n i) -> p n t i", i=RUN),
+            )
+
+        def quant_g(c, q, s0, n):
+            nc.vector.quantize_mx(
+                out=g_codes[:, c, s0 : s0 + n].bitcast(FP8X4),
+                scales=g_scales[:, c, s0 : s0 + n],
+                in_=mixed[c, q][:].rearrange("p n t -> p (n t)"),
+            )
+
+        wmixed = {}
+
+        def mix_w(c, q):
+            wmixed[c, q] = stage.tile([P, 4, K, PACK], BF16, align_bytes=64, tag="wmix", bufs=4, name=f"wmix{c}{q}")
+            nc.scalar.copy(
+                out=wmixed[c, q][:].rearrange("p e (k i) j -> p e k j i", i=RUN),
+                in_=w_raw[c, q][:].rearrange("p e j (k i) -> p e k j i", i=RUN),
+            )
+
+        def quant_w(c, q):
+            cols = slice(q * 4 * K, (q + 1) * 4 * K)
+            nc.vector.quantize_mx(
+                out=w_codes[:, c, cols].bitcast(FP8X4),
+                scales=w_scales[:, c, cols],
+                in_=wmixed[c, q][:].rearrange("p e k j -> p (e k j)"),
+            )
+
+        def multiply(c, e):
+            cols = slice(e * C, (e + 1) * C)
+            half = (e % 2) * C
+            nc.tensor.matmul_mx(
+                out=acc[e // 2][:, half : half + C],
+                lhsT=w_codes[:, c, cols].bitcast(FP8X4),
+                lhsT_scale=w_scales[:, c, cols],
+                rhs=g_codes[:, c, cols].bitcast(FP8X4),
+                rhs_scale=g_scales[:, c, cols],
+                start=(c == 0),
+                stop=(c == PASSES - 1),
+            )
+
+        def finish(b):
+            multiply(2, 2 * b)
+            for c in range(PASSES):
+                multiply(c, 2 * b + 1)
+            nc.scalar.copy(out=slots[:, 2 * b * C : 2 * (b + 1) * C], in_=acc[b][:])
+
+        def scatter(s0, n):
+            nc.vector.tensor_copy(
+                out=result[:].indirect(offsets[:, s0 // 16 : (s0 + n) // 16]), in_=slots[:, s0 : s0 + n]
+            )
+
+        nc.sync.dma_start(offsets[:], offs)
+        load_window(0, 0)
+        load_gates(0, 256)
+        load_gates(256, 1024)
+        for kind, c, i in LOADS:
+            (load_window if kind == "y" else load_w)(c, i)
+
+        def g01(c, t):
+            if t == 0:
+                new_gathered(c, 0, S)
+            for s0, n in ((0, 256), (256, 768)) if (c, t) == (0, 0) else ((0, S),):
+                nc.vector.tensor_tensor(
+                    gathered[c, 0][:, t, s0 : s0 + n],
+                    windows[c, t][:].indirect(offsets[:, s0 // 16 : (s0 + n) // 16]),
+                    gates[:, s0 : s0 + n],
+                    MULT,
+                )
+
+        def g2(q, t):
+            if t == 0:
+                new_gathered(2, q, 512)
+            gather(2, q, t, 512 * q, 512)
+
+        def m01(c):
+            new_mixed(c, 0, S)
+            mix(mixed[c, 0][:], gathered[c, 0][:])
+
+        def m2(i):
+            n = (512, 256, 256)[i]
+            new_mixed(2, i, n)
+            src = gathered[2, 0][:] if i == 0 else gathered[2, 1][:, :, 256 * i - 256 : 256 * i]
+            mix(mixed[2, i][:], src)
+
+        g01(0, 0)
+        mix_w(0, 0)
+        mix_w(0, 1)
+        g01(0, 1)
+        g01(0, 2)
+        g01(0, 3)
+        g01(1, 0)
+        mix_w(1, 0)
+        m01(0)
+        g01(1, 1)
+        g01(1, 2)
+        g01(1, 3)
+        g2(0, 0)
+        quant_w(0, 0)
+        g2(0, 1)
+        quant_g(0, 0, 0, 1024)
+        multiply(0, 0)
+        multiply(0, 2)
+        mix_w(1, 1)
+        mix_w(2, 0)
+        m01(1)
+        g2(0, 2)
+        quant_g(1, 0, 0, 1024)
+        quant_w(0, 1)
+        multiply(0, 4)
+        multiply(0, 6)
+        g2(0, 3)
+        g2(1, 0)
+        g2(1, 1)
+        m2(0)
+        quant_w(1, 0)
+        multiply(1, 0)
+        multiply(1, 2)
+        g2(1, 2)
+        mix_w(2, 1)
+        g2(1, 3)
+        quant_g(2, 0, 0, 512)
+        quant_w(1, 1)
+        multiply(1, 4)
+        multiply(1, 6)
+        m2(1)
+        quant_w(2, 0)
+        quant_g(2, 1, 512, 256)
+        finish(0)
+        m2(2)
+        scatter(0, 256)
+        finish(1)
+        scatter(256, 256)
+        quant_w(2, 1)
+        finish(2)
+        quant_g(2, 2, 768, 256)
+        scatter(512, 256)
+        finish(3)
+        scatter(768, 256)
+        nc.sync.dma_start(out=out, in_=result[:])

@@ -17,7 +17,7 @@ PACK = 4
 K_PASS = P * PACK
 PASSES = N // K_PASS
 PAD = 32
-RUN = 4
+RUN = 2
 LOADS = [(x[0], int(x[1]), int(x[2])) for x in "y01 y02 w00 w01 y03 y10 w02 y11 w03 w10 y12 y13 w11 w12 w13 y20 y21 y22 y23 w20 w21 w22 w23".split(" ")]
 
 FLOPS = 2 * K * N * S

@@ -16,9 +16,22 @@ P = 128
 PACK = 4
 K_PASS = P * PACK
 PASSES = N // K_PASS
+LAST = PASSES - 1
+HALF = S // 2
+EH = E // 2
 PAD = 32
 RUN = 2
-LOADS = [(x[0], int(x[1]), int(x[2])) for x in "y01 y02 w00 w01 y03 y10 w02 y11 w03 w10 y12 y13 w11 w12 w13 y20 y21 y22 y23 w20 w21 w22 w23".split(" ")]
+HEAD = 256
+
+GROUPS = {
+    "w0": [("w", 0, 0), ("w", 0, 1)],
+    "g0": [("g", 0, 0), ("g", 0, 1)],
+    "wa": [("w", 1, 0), ("w", 2, 0)],
+    "g1": [("g", 1, 0), ("g", 1, 1)],
+    "wb": [("w", 1, 1), ("w", 2, 1)],
+    "ga": [("g", 2, 0)],
+    "gb": [("g", 2, 1)],
+}
 
 FLOPS = 2 * K * N * S
 BYTES = 4 * (N * T + E * N * K + K * T + S) + 2 * S
@@ -28,28 +41,30 @@ def tile_moe_bdx_lin_none_kernel(tc, dyT, w, gate, offs, out):
     nc = tc.nc
     with ExitStack() as ctx:
         keep = ctx.enter_context(tc.tile_pool(name="keep", bufs=1))
-        stage = ctx.enter_context(tc.tile_pool(name="stage", bufs=2))
         psum = ctx.enter_context(tc.psum_pool(name="psum", bufs=1))
 
         offsets = keep.tile([P, S // 16], U16, name="offsets")
         gates = keep.tile([P, S], F32, name="gates")
         windows = {}
-        w_raw = {}
         for c in range(PASSES):
             for t in range(PACK):
-                width = T + PAD if c < 2 else T
-                windows[c, t] = keep.tile([P, width], F32, name=f"win{c}{t}")
-                if c < 2:
+                width = T + PAD if c < LAST else T
+                windows[c, t] = keep.tile([P, width], F32, name=f"win{c}{t}", tag=f"win{c}{t}")
+                if c < LAST:
                     nc.gpsimd.memset(windows[c, t][:, T:width], 0.0)
-            for h in range(2):
-                w_raw[c, h] = keep.tile([P, 4, PACK, K], F32, name=f"wraw{c}{h}")
-        g_codes = keep.tile([P, PASSES, S], U32, align_bytes=64, name="g_codes")
-        g_scales = keep.tile([P, PASSES, S], U8, align_bytes=64, name="g_scales")
-        w_codes = keep.tile([P, PASSES, E * K], U32, align_bytes=64, name="w_codes")
-        w_scales = keep.tile([P, PASSES, E * K], U8, align_bytes=64, name="w_scales")
+        w_raw = {(c, h): keep.tile([P, EH, PACK, K], F32, name=f"wraw{c}{h}", tag=f"wraw{c}{h}") for c in range(PASSES) for h in range(2)}
+        place = {}
+        mixed, codes, scales = {}, {}, {}
+        for name, parts in GROUPS.items():
+            mixed[name] = keep.tile([P, len(parts), HALF, PACK], BF16, align_bytes=64, name=f"mixed_{name}")
+            codes[name] = keep.tile([P, len(parts) * HALF], U32, align_bytes=64, name=f"codes_{name}")
+            scales[name] = keep.tile([P, len(parts) * HALF], U8, align_bytes=64, name=f"scales_{name}")
+            for i, part in enumerate(parts):
+                place[part] = (name, i)
+        gathered = {}
         result = keep.tile([P, T], F32, name="result")
         slots = keep.tile([P, S], F32, name="slots")
-        acc = [psum.tile([P, 2 * C], F32, name=f"acc{b}") for b in range(E // 2)]
+        acc = [psum.tile([P, 1 * C], F32, name=f"acc{b}") for b in range(E // 1)]
 
         dy_rows = dyT.rearrange("(c p j) t -> c p j t", p=P, j=PACK)
         w_rows = w.rearrange("e (c p j) k -> c p e (j k)", p=P, j=PACK)
@@ -57,81 +72,81 @@ def tile_moe_bdx_lin_none_kernel(tc, dyT, w, gate, offs, out):
         def load_window(c, t):
             nc.sync.dma_start(out=windows[c, t][:, 0:T], in_=dy_rows[c, :, t, :])
 
-        def load_w(c, h):
+        def load_w(c, q):
             nc.sync.dma_start(
-                out=w_raw[c, h // 2][:, 2 * (h % 2) : 2 * (h % 2) + 2].rearrange("p e j k -> p e (j k)"),
-                in_=w_rows[c, :, 2 * h : 2 * h + 2, :],
+                out=w_raw[c, q // 2][:, 2 * (q % 2) : 2 * (q % 2) + 2].rearrange("p e j k -> p e (j k)"),
+                in_=w_rows[c, :, 2 * q : 2 * q + 2, :],
             )
 
-        def load_gates(s0, s1):
-            nc.sync.dma_start(out=gates[:, s0:s1], in_=gate[0:P, s0:s1])
-
-        gathered = {}
-
-        def new_gathered(c, q, n):
-            gathered[c, q] = stage.tile([P, PACK, n], F32, tag="gathered", bufs=2, name=f"gathered{c}{q}")
-
-        def gather(c, q, t, s0, n):
+        def gather(dst, c, t, s0, n):
             nc.vector.tensor_tensor(
-                gathered[c, q][:, t, :],
-                windows[c, t][:].indirect(offsets[:, s0 // 16 : (s0 + n) // 16]),
-                gates[:, s0 : s0 + n],
-                MULT,
+                dst, windows[c, t][:].indirect(offsets[:, s0 // 16 : (s0 + n) // 16]), gates[:, s0 : s0 + n], MULT
             )
 
-        mixed = {}
+        def g_full(c, t):
+            if t == 0:
+                gathered[c] = keep.tile([P, PACK, S], F32, tag=f"gath{c}", name=f"gath{c}")
+            for s0, n in ((0, HEAD), (HEAD, S - HEAD)) if (c, t) == (0, 0) else ((0, S),):
+                gather(gathered[c][:, t, s0 : s0 + n], c, t, s0, n)
 
-        def new_mixed(c, q, n):
-            mixed[c, q] = stage.tile([P, n, PACK], BF16, align_bytes=64, tag=f"mixed{n}", bufs=2, name=f"mixed{c}{q}")
+        def g_half(h, t):
+            if t == 0:
+                gathered[LAST, h] = keep.tile([P, PACK, HALF], F32, tag=f"gath{h}", name=f"gath2{h}")
+            gather(gathered[LAST, h][:, t, :], LAST, t, h * HALF, HALF)
 
-        def mix(dst, src):
+        def mix_g(c, h):
+            src = gathered[c][:, :, h * HALF : (h + 1) * HALF] if c < LAST else gathered[c, h][:]
             nc.scalar.copy(
-                out=dst.rearrange("p (n i) t -> p n t i", i=RUN),
+                out=mixed[place["g", c, h][0]][:, place["g", c, h][1]].rearrange("p (n i) t -> p n t i", i=RUN),
                 in_=src.rearrange("p t (n i) -> p n t i", i=RUN),
             )
 
-        def quant_g(c, q, s0, n):
-            nc.vector.quantize_mx(
-                out=g_codes[:, c, s0 : s0 + n].bitcast(FP8X4),
-                scales=g_scales[:, c, s0 : s0 + n],
-                in_=mixed[c, q][:].rearrange("p n t -> p (n t)"),
-            )
-
-        wmixed = {}
-
-        def mix_w(c, q):
-            wmixed[c, q] = stage.tile([P, 4, K, PACK], BF16, align_bytes=64, tag="wmix", bufs=4, name=f"wmix{c}{q}")
+        def mix_w(c, h, e0=0, ne=EH):
             nc.scalar.copy(
-                out=wmixed[c, q][:].rearrange("p e (k i) j -> p e k j i", i=RUN),
-                in_=w_raw[c, q][:].rearrange("p e j (k i) -> p e k j i", i=RUN),
+                out=mixed[place["w", c, h][0]][:, place["w", c, h][1], e0 * K : (e0 + ne) * K].rearrange("p (e k i) j -> p e k j i", i=RUN, e=ne),
+                in_=w_raw[c, h][:, e0 : e0 + ne].rearrange("p e j (k i) -> p e k j i", i=RUN),
             )
 
-        def quant_w(c, q):
-            cols = slice(q * 4 * K, (q + 1) * 4 * K)
+        def mix_w2(c, h):
+            mix_w(c, h, 0, 2)
+            mix_w(c, h, 2, 2)
+
+        def quant(name):
             nc.vector.quantize_mx(
-                out=w_codes[:, c, cols].bitcast(FP8X4),
-                scales=w_scales[:, c, cols],
-                in_=wmixed[c, q][:].rearrange("p e k j -> p (e k j)"),
+                out=codes[name][:].bitcast(FP8X4),
+                scales=scales[name][:],
+                in_=mixed[name][:].rearrange("p o n t -> p (o n t)"),
             )
 
         def multiply(c, e):
-            cols = slice(e * C, (e + 1) * C)
-            half = (e % 2) * C
+            h, i = divmod(e, EH)
+            wn, wi = place["w", c, h]
+            gn, gi = place["g", c, h]
+            wc = slice(wi * HALF + i * K, wi * HALF + (i + 1) * K)
+            gc = slice(gi * HALF + i * C, gi * HALF + (i + 1) * C)
+            col = (e % 1) * C
             nc.tensor.matmul_mx(
-                out=acc[e // 2][:, half : half + C],
-                lhsT=w_codes[:, c, cols].bitcast(FP8X4),
-                lhsT_scale=w_scales[:, c, cols],
-                rhs=g_codes[:, c, cols].bitcast(FP8X4),
-                rhs_scale=g_scales[:, c, cols],
+                out=acc[e // 1][:, col : col + C],
+                lhsT=codes[wn][:, wc].bitcast(FP8X4),
+                lhsT_scale=scales[wn][:, wc],
+                rhs=codes[gn][:, gc].bitcast(FP8X4),
+                rhs_scale=scales[gn][:, gc],
                 start=(c == 0),
-                stop=(c == PASSES - 1),
+                stop=(c == LAST),
             )
 
-        def finish(b):
-            multiply(2, 2 * b)
-            for c in range(PASSES):
-                multiply(c, 2 * b + 1)
-            nc.scalar.copy(out=slots[:, 2 * b * C : 2 * (b + 1) * C], in_=acc[b][:])
+        def products(h):
+            first = [e for e in range(h * EH, (h + 1) * EH) if e % 1 == 0]
+            for c in range(LAST):
+                for e in first:
+                    multiply(c, e)
+            for e0 in first:
+                multiply(LAST, e0)
+                for e in range(e0 + 1, e0 + 1):
+                    for c in range(PASSES):
+                        multiply(c, e)
+                b = e0 // 1
+                nc.scalar.copy(out=slots[:, e0 * C : (e0 + 1) * C], in_=acc[b][:])
 
         def scatter(s0, n):
             nc.vector.tensor_copy(
@@ -140,89 +155,40 @@ def tile_moe_bdx_lin_none_kernel(tc, dyT, w, gate, offs, out):
 
         nc.sync.dma_start(offsets[:], offs)
         load_window(0, 0)
-        load_gates(0, 256)
-        load_gates(256, 1024)
-        for kind, c, i in LOADS:
-            (load_window if kind == "y" else load_w)(c, i)
+        nc.sync.dma_start(out=gates[:, 0:HEAD], in_=gate[0:P, 0:HEAD])
+        nc.sync.dma_start(out=gates[:, HEAD:S], in_=gate[0:P, HEAD:S])
+        for x in "y01 w00 y02 w01 y03 w02 y10 w03 y11 w10 w11 w12 y12 w13 w20 y13 w21 y20 y21 y22 y23 w22 w23".split(" "):
+            (load_window if x[0] == "y" else load_w)(int(x[1]), int(x[2]))
 
-        def g01(c, t):
-            if t == 0:
-                new_gathered(c, 0, S)
-            for s0, n in ((0, 256), (256, 768)) if (c, t) == (0, 0) else ((0, S),):
-                nc.vector.tensor_tensor(
-                    gathered[c, 0][:, t, s0 : s0 + n],
-                    windows[c, t][:].indirect(offsets[:, s0 // 16 : (s0 + n) // 16]),
-                    gates[:, s0 : s0 + n],
-                    MULT,
-                )
-
-        def g2(q, t):
-            if t == 0:
-                new_gathered(2, q, 512)
-            gather(2, q, t, 512 * q, 512)
-
-        def m01(c):
-            new_mixed(c, 0, S)
-            mix(mixed[c, 0][:], gathered[c, 0][:])
-
-        def m2(i):
-            n = (512, 256, 256)[i]
-            new_mixed(2, i, n)
-            src = gathered[2, 0][:] if i == 0 else gathered[2, 1][:, :, 256 * i - 256 : 256 * i]
-            mix(mixed[2, i][:], src)
-
-        g01(0, 0)
-        mix_w(0, 0)
-        mix_w(0, 1)
-        g01(0, 1)
-        g01(0, 2)
-        g01(0, 3)
-        g01(1, 0)
+        for t in range(PACK):
+            g_full(0, t)
+        mix_w2(0, 0)
+        mix_w2(0, 1)
+        mix_g(0, 0)
+        mix_g(0, 1)
+        for t in range(PACK):
+            g_full(1, t)
+        quant("w0")
+        quant("g0")
         mix_w(1, 0)
-        m01(0)
-        g01(1, 1)
-        g01(1, 2)
-        g01(1, 3)
-        g2(0, 0)
-        quant_w(0, 0)
-        g2(0, 1)
-        quant_g(0, 0, 0, 1024)
-        multiply(0, 0)
-        multiply(0, 2)
-        mix_w(1, 1)
-        mix_w(2, 0)
-        m01(1)
-        g2(0, 2)
-        quant_g(1, 0, 0, 1024)
-        quant_w(0, 1)
-        multiply(0, 4)
-        multiply(0, 6)
-        g2(0, 3)
-        g2(1, 0)
-        g2(1, 1)
-        m2(0)
-        quant_w(1, 0)
-        multiply(1, 0)
-        multiply(1, 2)
-        g2(1, 2)
+        mix_w2(1, 1)
+        mix_w2(2, 0)
+        mix_g(1, 0)
+        mix_g(1, 1)
+        for t in range(PACK):
+            g_half(0, t)
+        quant("wa")
+        mix_g(2, 0)
+        for t in range(PACK):
+            g_half(1, t)
         mix_w(2, 1)
-        g2(1, 3)
-        quant_g(2, 0, 0, 512)
-        quant_w(1, 1)
-        multiply(1, 4)
-        multiply(1, 6)
-        m2(1)
-        quant_w(2, 0)
-        quant_g(2, 1, 512, 256)
-        finish(0)
-        m2(2)
-        scatter(0, 256)
-        finish(1)
-        scatter(256, 256)
-        quant_w(2, 1)
-        finish(2)
-        quant_g(2, 2, 768, 256)
-        scatter(512, 256)
-        finish(3)
-        scatter(768, 256)
+        mix_g(2, 1)
+        quant("g1")
+        quant("ga")
+        quant("wb")
+        quant("gb")
+        products(0)
+        products(1)
+        scatter(0, HALF)
+        scatter(HALF, HALF)
         nc.sync.dma_start(out=out, in_=result[:])

@@ -21,7 +21,7 @@ HALF = S // 2
 EH = E // 2
 PAD = 32
 RUN = 2
-HEAD = 256
+HEAD = ((0, 128), (128, 384), (512, 512))
 
 GROUPS = {
     "w0": [("w", 0, 0), ("w", 0, 1)],
@@ -86,7 +86,7 @@ def tile_moe_bdx_lin_none_kernel(tc, dyT, w, gate, offs, out):
         def g_full(c, t):
             if t == 0:
                 gathered[c] = keep.tile([P, PACK, S], F32, tag=f"gath{c}", name=f"gath{c}")
-            for s0, n in ((0, HEAD), (HEAD, S - HEAD)) if (c, t) == (0, 0) else ((0, S),):
+            for s0, n in HEAD if (c, t) == (0, 0) else ((0, S),):
                 gather(gathered[c][:, t, s0 : s0 + n], c, t, s0, n)
 
         def g_half(h, t):
@@ -153,10 +153,10 @@ def tile_moe_bdx_lin_none_kernel(tc, dyT, w, gate, offs, out):
                 out=result[:].indirect(offsets[:, s0 // 16 : (s0 + n) // 16]), in_=slots[:, s0 : s0 + n]
             )
 
-        nc.sync.dma_start(offsets[:], offs)
         load_window(0, 0)
-        nc.sync.dma_start(out=gates[:, 0:HEAD], in_=gate[0:P, 0:HEAD])
-        nc.sync.dma_start(out=gates[:, HEAD:S], in_=gate[0:P, HEAD:S])
+        nc.sync.dma_start(offsets[:], offs)
+        for s0, n in HEAD:
+            nc.sync.dma_start(out=gates[:, s0 : s0 + n], in_=gate[0:P, s0 : s0 + n])
         for x in "y01 w00 y02 w01 y03 w02 y10 w03 y11 w10 w11 w12 y12 w13 w20 y13 w21 y20 y21 y22 y23 w22 w23".split(" "):
             (load_window if x[0] == "y" else load_w)(int(x[1]), int(x[2]))
 

@@ -50,8 +50,9 @@ def tile_moe_bdx_lin_none_kernel(tc, dyT, w, gate, offs, out):
             for t in range(PACK):
                 width = T + PAD if c < LAST else T
                 windows[c, t] = keep.tile([P, width], F32, name=f"win{c}{t}", tag=f"win{c}{t}")
-                if c < LAST:
-                    nc.gpsimd.memset(windows[c, t][:, T:width], 0.0)
+        for c in reversed(range(LAST)):
+            for t in reversed(range(PACK)):
+                nc.gpsimd.memset(windows[c, t][:, T : T + PAD], 0.0)
         w_raw = {(c, h): keep.tile([P, EH, PACK, K], F32, name=f"wraw{c}{h}", tag=f"wraw{c}{h}") for c in range(PASSES) for h in range(2)}
         place = {}
         mixed, codes, scales = {}, {}, {}

@@ -74,6 +74,10 @@ def tile_moe_bdx_lin_none_kernel(tc, dyT, w, gate, offs, out):
             nc.sync.dma_start(out=windows[c, t][:, 0:T], in_=dy_rows[c, :, t, :])
 
         def load_w(c, q):
+            if c == LAST and q > 0:
+                for e in (2 * q, 2 * q + 1):
+                    nc.sync.dma_start(out=w_raw[c, e // EH][:, e % EH].rearrange("p j k -> p (j k)"), in_=w_rows[c, :, e, :])
+                return
             nc.sync.dma_start(
                 out=w_raw[c, q // 2][:, 2 * (q % 2) : 2 * (q % 2) + 2].rearrange("p e j k -> p e (j k)"),
                 in_=w_rows[c, :, 2 * q : 2 * q + 2, :],

@@ -19,18 +19,24 @@ PASSES = N // K_PASS
 LAST = PASSES - 1
 HALF = S // 2
 EH = E // 2
+PAIRS = E // 2
+LIST_ROWS = 16
+ALIGN = 256
+
 PAD = 32
 RUN = 2
 HEAD = ((0, 128), (128, 384), (512, 512))
+EXTRA_PAIRS = {(1, 1): 2, (1, 2): 1}
+PAIRS_BY_EXPERT = 3
 
 GROUPS = {
-    "w0": [("w", 0, 0), ("w", 0, 1)],
-    "g0": [("g", 0, 0), ("g", 0, 1)],
-    "wa": [("w", 1, 0), ("w", 2, 0)],
-    "g1": [("g", 1, 0), ("g", 1, 1)],
-    "wb": [("w", 1, 1), ("w", 2, 1)],
-    "ga": [("g", 2, 0)],
-    "gb": [("g", 2, 1)],
+    "w_pass0": [("w", 0, 0), ("w", 0, 1)],
+    "g_pass0": [("g", 0, 0), ("g", 0, 1)],
+    "w_half0": [("w", 1, 0), ("w", 2, 0)],
+    "g_pass1": [("g", 1, 0), ("g", 1, 1)],
+    "w_half1": [("w", 1, 1), ("w", 2, 1)],
+    "g_last0": [("g", 2, 0)],
+    "g_last1": [("g", 2, 1)],
 }
 
 FLOPS = 2 * K * N * S
@@ -43,157 +49,167 @@ def tile_moe_bdx_lin_none_kernel(tc, dyT, w, gate, offs, out):
         keep = ctx.enter_context(tc.tile_pool(name="keep", bufs=1))
         psum = ctx.enter_context(tc.psum_pool(name="psum", bufs=1))
 
-        offsets = keep.tile([P, S // 16], U16, name="offsets")
-        gates = keep.tile([P, S], F32, name="gates")
+        offsets = keep.tile([P, S // LIST_ROWS], U16, name="offsets")
+        gates = keep.tile([P, S], F32, align_bytes=ALIGN, name="gates")
         windows = {}
         for c in range(PASSES):
             for t in range(PACK):
                 width = T + PAD if c < LAST else T
-                windows[c, t] = keep.tile([P, width], F32, name=f"win{c}{t}", tag=f"win{c}{t}")
+                windows[c, t] = keep.tile([P, width], F32, align_bytes=ALIGN, name=f"win{c}{t}")
         for c in reversed(range(LAST)):
             for t in reversed(range(PACK)):
                 nc.gpsimd.memset(windows[c, t][:, T : T + PAD], 0.0)
-        w_raw = {(c, h): keep.tile([P, EH, PACK, K], F32, name=f"wraw{c}{h}", tag=f"wraw{c}{h}") for c in range(PASSES) for h in range(2)}
+        w_raw = {}
+        for c in range(PASSES):
+            for h in range(2):
+                w_raw[c, h] = keep.tile([P, EH, PACK, K], F32, align_bytes=ALIGN, name=f"wraw{c}{h}")
         place = {}
         mixed, codes, scales = {}, {}, {}
-        for name, parts in GROUPS.items():
-            mixed[name] = keep.tile([P, len(parts), HALF, PACK], BF16, align_bytes=64, name=f"mixed_{name}")
-            codes[name] = keep.tile([P, len(parts) * HALF], U32, align_bytes=64, name=f"codes_{name}")
-            scales[name] = keep.tile([P, len(parts) * HALF], U8, align_bytes=64, name=f"scales_{name}")
+        for group, parts in GROUPS.items():
+            mixed[group] = keep.tile([P, len(parts), HALF, PACK], BF16, align_bytes=ALIGN, name=f"mixed_{group}")
+            codes[group] = keep.tile([P, len(parts) * HALF], U32, align_bytes=ALIGN, name=f"codes_{group}")
+            scales[group] = keep.tile([P, len(parts) * HALF], U8, align_bytes=ALIGN, name=f"scales_{group}")
             for i, part in enumerate(parts):
-                place[part] = (name, i)
+                place[part] = (group, i)
         gathered = {}
-        result = keep.tile([P, T], F32, name="result")
-        slots = keep.tile([P, S], F32, name="slots")
-        acc = [psum.tile([P, 1 * C], F32, name=f"acc{b}") for b in range(E // 1)]
+        result = keep.tile([P, T], F32, align_bytes=ALIGN, name="result")
+        slots = keep.tile([P, S], F32, align_bytes=ALIGN, name="slots")
+        acc = [psum.tile([P, C], F32, name=f"acc{e}") for e in range(E)]
 
-        dy_rows = dyT.rearrange("(c p j) t -> c p j t", p=P, j=PACK)
-        w_rows = w.rearrange("e (c p j) k -> c p e (j k)", p=P, j=PACK)
+        dy_rows = dyT.rearrange("(c p t) x -> c p t x", p=P, t=PACK)
+        w_rows = w.rearrange("e (c p t) k -> c p e (t k)", p=P, t=PACK)
 
         def load_window(c, t):
             nc.sync.dma_start(out=windows[c, t][:, 0:T], in_=dy_rows[c, :, t, :])
 
-        def load_w(c, q):
-            if c == LAST and q > 0:
-                for e in (2 * q, 2 * q + 1):
-                    nc.sync.dma_start(out=w_raw[c, e // EH][:, e % EH].rearrange("p j k -> p (j k)"), in_=w_rows[c, :, e, :])
-                return
-            nc.sync.dma_start(
-                out=w_raw[c, q // 2][:, 2 * (q % 2) : 2 * (q % 2) + 2].rearrange("p e j k -> p e (j k)"),
-                in_=w_rows[c, :, 2 * q : 2 * q + 2, :],
-            )
+        def load_pair(c, q):
+            h, i = divmod(2 * q, EH)
+            if c == LAST and q >= PAIRS - PAIRS_BY_EXPERT:
+                for j in range(2):
+                    nc.sync.dma_start(
+                        out=w_raw[c, h][:, i + j].rearrange("p t k -> p (t k)"), in_=w_rows[c, :, 2 * q + j, :]
+                    )
+            else:
+                nc.sync.dma_start(
+                    out=w_raw[c, h][:, i : i + 2].rearrange("p e t k -> p e (t k)"),
+                    in_=w_rows[c, :, 2 * q : 2 * q + 2, :],
+                )
+
+        def listed(s0, n):
+            return offsets[:, s0 // LIST_ROWS : (s0 + n) // LIST_ROWS]
 
         def gather(dst, c, t, s0, n):
-            nc.vector.tensor_tensor(
-                dst, windows[c, t][:].indirect(offsets[:, s0 // 16 : (s0 + n) // 16]), gates[:, s0 : s0 + n], MULT
-            )
+            nc.vector.tensor_tensor(dst, windows[c, t][:].indirect(listed(s0, n)), gates[:, s0 : s0 + n], MULT)
 
-        def g_full(c, t):
-            if t == 0:
-                gathered[c] = keep.tile([P, PACK, S], F32, tag=f"gath{c}", name=f"gath{c}")
-            for s0, n in HEAD if (c, t) == (0, 0) else ((0, S),):
-                gather(gathered[c][:, t, s0 : s0 + n], c, t, s0, n)
+        def gather_pass(c):
+            gathered[c] = keep.tile([P, PACK, S], F32, align_bytes=ALIGN, tag=f"gath{c}", name=f"gath{c}")
+            for t in range(PACK):
+                for s0, n in HEAD if (c, t) == (0, 0) else ((0, S),):
+                    gather(gathered[c][:, t, s0 : s0 + n], c, t, s0, n)
 
-        def g_half(h, t):
-            if t == 0:
-                gathered[LAST, h] = keep.tile([P, PACK, HALF], F32, tag=f"gath{h}", name=f"gath2{h}")
-            gather(gathered[LAST, h][:, t, :], LAST, t, h * HALF, HALF)
+        def gather_last(h):
+            gathered[LAST, h] = keep.tile([P, PACK, HALF], F32, align_bytes=ALIGN, tag=f"gath{h}", name=f"gath_last{h}")
+            for t in range(PACK):
+                gather(gathered[LAST, h][:, t, :], LAST, t, h * HALF, HALF)
 
         def mix_g(c, h):
             src = gathered[c][:, :, h * HALF : (h + 1) * HALF] if c < LAST else gathered[c, h][:]
+            group, i = place["g", c, h]
             nc.scalar.copy(
-                out=mixed[place["g", c, h][0]][:, place["g", c, h][1]].rearrange("p (n i) t -> p n t i", i=RUN),
-                in_=src.rearrange("p t (n i) -> p n t i", i=RUN),
+                out=mixed[group][:, i].rearrange("p (x r) t -> p x t r", r=RUN),
+                in_=src.rearrange("p t (x r) -> p x t r", r=RUN),
             )
 
-        def mix_w(c, h, e0=0, ne=EH):
-            nc.scalar.copy(
-                out=mixed[place["w", c, h][0]][:, place["w", c, h][1], e0 * K : (e0 + ne) * K].rearrange("p (e k i) j -> p e k j i", i=RUN, e=ne),
-                in_=w_raw[c, h][:, e0 : e0 + ne].rearrange("p e j (k i) -> p e k j i", i=RUN),
-            )
+        def mix_w(c, h, experts):
+            group, i = place["w", c, h]
+            for e0 in range(0, EH, experts):
+                nc.scalar.copy(
+                    out=mixed[group][:, i, e0 * K : (e0 + experts) * K].rearrange(
+                        "p (e x r) t -> p e x t r", r=RUN, e=experts
+                    ),
+                    in_=w_raw[c, h][:, e0 : e0 + experts].rearrange("p e t (x r) -> p e x t r", r=RUN),
+                )
 
-        def mix_w2(c, h):
-            mix_w(c, h, 0, 2)
-            mix_w(c, h, 2, 2)
-
-        def quant(name):
+        def quantise(group):
             nc.vector.quantize_mx(
-                out=codes[name][:].bitcast(FP8X4),
-                scales=scales[name][:],
-                in_=mixed[name][:].rearrange("p o n t -> p (o n t)"),
+                out=codes[group][:].bitcast(FP8X4),
+                scales=scales[group][:],
+                in_=mixed[group][:].rearrange("p i x t -> p (i x t)"),
             )
 
         def multiply(c, e):
             h, i = divmod(e, EH)
-            wn, wi = place["w", c, h]
-            gn, gi = place["g", c, h]
-            wc = slice(wi * HALF + i * K, wi * HALF + (i + 1) * K)
-            gc = slice(gi * HALF + i * C, gi * HALF + (i + 1) * C)
-            col = (e % 1) * C
+            w_group, w_place = place["w", c, h]
+            g_group, g_place = place["g", c, h]
+            w_cols = slice(w_place * HALF + i * K, w_place * HALF + (i + 1) * K)
+            g_cols = slice(g_place * HALF + i * C, g_place * HALF + (i + 1) * C)
             nc.tensor.matmul_mx(
-                out=acc[e // 1][:, col : col + C],
-                lhsT=codes[wn][:, wc].bitcast(FP8X4),
-                lhsT_scale=scales[wn][:, wc],
-                rhs=codes[gn][:, gc].bitcast(FP8X4),
-                rhs_scale=scales[gn][:, gc],
+                out=acc[e][:],
+                lhsT=codes[w_group][:, w_cols].bitcast(FP8X4),
+                lhsT_scale=scales[w_group][:, w_cols],
+                rhs=codes[g_group][:, g_cols].bitcast(FP8X4),
+                rhs_scale=scales[g_group][:, g_cols],
                 start=(c == 0),
                 stop=(c == LAST),
             )
 
         def products(h):
-            first = [e for e in range(h * EH, (h + 1) * EH) if e % 1 == 0]
+            experts = range(h * EH, (h + 1) * EH)
             for c in range(LAST):
-                for e in first:
+                for e in experts:
                     multiply(c, e)
-            for e0 in first:
-                multiply(LAST, e0)
-                for e in range(e0 + 1, e0 + 1):
-                    for c in range(PASSES):
-                        multiply(c, e)
-                b = e0 // 1
-                nc.scalar.copy(out=slots[:, e0 * C : (e0 + 1) * C], in_=acc[b][:])
+            for e in experts:
+                multiply(LAST, e)
+                nc.scalar.copy(out=slots[:, e * C : (e + 1) * C], in_=acc[e][:])
 
-        def scatter(s0, n):
+        def scatter(h):
             nc.vector.tensor_copy(
-                out=result[:].indirect(offsets[:, s0 // 16 : (s0 + n) // 16]), in_=slots[:, s0 : s0 + n]
+                out=result[:].indirect(listed(h * HALF, HALF)), in_=slots[:, h * HALF : (h + 1) * HALF]
             )
 
         load_window(0, 0)
         nc.sync.dma_start(offsets[:], offs)
         for s0, n in HEAD:
             nc.sync.dma_start(out=gates[:, s0 : s0 + n], in_=gate[0:P, s0 : s0 + n])
-        for x in "y01 w00 y02 w01 y03 w02 y10 w03 y11 w10 w11 w12 y12 w13 w20 y13 w21 y20 y21 y22 y23 w22 w23".split(" "):
-            (load_window if x[0] == "y" else load_w)(int(x[1]), int(x[2]))
+        pairs = [(c, q) for c in range(PASSES) for q in range(PAIRS)]
+        loaded = 0
+        for c in range(PASSES):
+            for t in range(PACK):
+                if (c, t) == (0, 0):
+                    continue
+                load_window(c, t)
+                behind = 1 + EXTRA_PAIRS.get((c, t), 0) if c < LAST else 0
+                for pair in pairs[loaded : loaded + behind]:
+                    load_pair(*pair)
+                loaded = loaded + behind
+        for pair in pairs[loaded:]:
+            load_pair(*pair)
 
-        for t in range(PACK):
-            g_full(0, t)
-        mix_w2(0, 0)
-        mix_w2(0, 1)
+        gather_pass(0)
+        mix_w(0, 0, 2)
+        mix_w(0, 1, 2)
         mix_g(0, 0)
         mix_g(0, 1)
-        for t in range(PACK):
-            g_full(1, t)
-        quant("w0")
-        quant("g0")
-        mix_w(1, 0)
-        mix_w2(1, 1)
-        mix_w2(2, 0)
+        gather_pass(1)
+        quantise("w_pass0")
+        quantise("g_pass0")
+        mix_w(1, 0, EH)
+        mix_w(1, 1, 2)
+        mix_w(LAST, 0, 2)
         mix_g(1, 0)
         mix_g(1, 1)
-        for t in range(PACK):
-            g_half(0, t)
-        quant("wa")
-        mix_g(2, 0)
-        for t in range(PACK):
-            g_half(1, t)
-        mix_w(2, 1)
-        mix_g(2, 1)
-        quant("g1")
-        quant("ga")
-        quant("wb")
-        quant("gb")
+        gather_last(0)
+        quantise("w_half0")
+        mix_g(LAST, 0)
+        gather_last(1)
+        mix_w(LAST, 1, EH)
+        mix_g(LAST, 1)
+        quantise("g_pass1")
+        quantise("g_last0")
+        quantise("w_half1")
+        quantise("g_last1")
         products(0)
         products(1)
-        scatter(0, HALF)
-        scatter(HALF, HALF)
+        scatter(0)
+        scatter(1)
         nc.sync.dma_start(out=out, in_=result[:])

@@ -51,14 +51,14 @@ def tile_moe_bdx_lin_none_kernel(tc, dyT, w, gate, offs, out):
 
         offsets = keep.tile([P, S // LIST_ROWS], U16, name="offsets")
         gates = keep.tile([P, S], F32, align_bytes=ALIGN, name="gates")
+        padded = [(c, t) for c in range(LAST) for t in range(PACK) if (c, t) != (0, 0)]
         windows = {}
         for c in range(PASSES):
             for t in range(PACK):
-                width = T + PAD if c < LAST else T
+                width = T + PAD if (c, t) in padded else T
                 windows[c, t] = keep.tile([P, width], F32, align_bytes=ALIGN, name=f"win{c}{t}")
-        for c in reversed(range(LAST)):
-            for t in reversed(range(PACK)):
-                nc.gpsimd.memset(windows[c, t][:, T : T + PAD], 0.0)
+        for c, t in reversed(padded):
+            nc.gpsimd.memset(windows[c, t][:, T : T + PAD], 0.0)
         w_raw = {}
         for c in range(PASSES):
             for h in range(2):

@@ -1,6 +1,7 @@
 from contextlib import ExitStack
 
 import concourse.mybir as mybir
+from concourse.masks import make_identity
 
 F32 = mybir.dt.float32
 BF16 = mybir.dt.bfloat16
@@ -9,6 +10,7 @@ U16 = mybir.dt.uint16
 U8 = mybir.dt.uint8
 FP8X4 = mybir.dt.float8_e4m3fn_x4
 MULT = mybir.AluOpType.mult
+COPY = mybir.ActivationFunctionType.Copy
 
 K, T, E, C, N = 128, 1024, 8, 128, 1536
 S = E * C
@@ -19,25 +21,11 @@ PASSES = N // K_PASS
 LAST = PASSES - 1
 HALF = S // 2
 EH = E // 2
-PAIRS = E // 2
 LIST_ROWS = 16
 ALIGN = 256
-
-PAD = 32
 RUN = 2
-HEAD = ((0, 128), (128, 384), (512, 512))
-EXTRA_PAIRS = {(1, 1): 2, (1, 2): 1}
-PAIRS_BY_EXPERT = 3
-
-GROUPS = {
-    "w_pass0": [("w", 0, 0), ("w", 0, 1)],
-    "g_pass0": [("g", 0, 0), ("g", 0, 1)],
-    "w_half0": [("w", 1, 0), ("w", 2, 0)],
-    "g_pass1": [("g", 1, 0), ("g", 1, 1)],
-    "w_half1": [("w", 1, 1), ("w", 2, 1)],
-    "g_last0": [("g", 2, 0)],
-    "g_last1": [("g", 2, 1)],
-}
+PLANES = PACK * HALF
+SCATTERS = ((0, 2), (2, 2), (4, 1), (5, 1), (6, 1), (7, 1))
 
 FLOPS = 2 * K * N * S
 BYTES = 4 * (N * T + E * N * K + K * T + S) + 2 * S
@@ -50,166 +38,170 @@ def tile_moe_bdx_lin_none_kernel(tc, dyT, w, gate, offs, out):
         psum = ctx.enter_context(tc.psum_pool(name="psum", bufs=1))
 
         offsets = keep.tile([P, S // LIST_ROWS], U16, name="offsets")
-        gates = keep.tile([P, S], F32, align_bytes=ALIGN, name="gates")
-        padded = [(c, t) for c in range(LAST) for t in range(PACK) if (c, t) != (0, 0)]
-        windows = {}
+        identity = keep.tile([P, P], F32, align_bytes=ALIGN, name="identity")
+        zero = keep.tile([P, 1], F32, name="zero")
+        gate_cols = keep.tile([P, 2, PACK], F32, align_bytes=ALIGN, name="gate_cols")
+        gates = [psum.tile([P, HALF], F32, name=f"gates{h}") for h in range(2)]
+        windows, gathered = {}, {}
         for c in range(PASSES):
             for t in range(PACK):
-                width = T + PAD if (c, t) in padded else T
-                windows[c, t] = keep.tile([P, width], F32, align_bytes=ALIGN, name=f"win{c}{t}")
-        for c, t in reversed(padded):
-            nc.gpsimd.memset(windows[c, t][:, T : T + PAD], 0.0)
-        w_raw = {}
-        for c in range(PASSES):
-            for h in range(2):
-                w_raw[c, h] = keep.tile([P, EH, PACK, K], F32, align_bytes=ALIGN, name=f"wraw{c}{h}")
-        place = {}
-        mixed, codes, scales = {}, {}, {}
-        for group, parts in GROUPS.items():
-            mixed[group] = keep.tile([P, len(parts), HALF, PACK], BF16, align_bytes=ALIGN, name=f"mixed_{group}")
-            codes[group] = keep.tile([P, len(parts) * HALF], U32, align_bytes=ALIGN, name=f"codes_{group}")
-            scales[group] = keep.tile([P, len(parts) * HALF], U8, align_bytes=ALIGN, name=f"scales_{group}")
-            for i, part in enumerate(parts):
-                place[part] = (group, i)
-        gathered = {}
+                if c > 0 and t == PACK - 1:
+                    wide = keep.tile([P, T + PLANES], F32, align_bytes=ALIGN, name=f"win{c}{t}")
+                    windows[c, t] = wide[:, 0:T]
+                    windows[c, "wide"] = wide[:]
+                    gathered[0, c - 1] = wide[:, T : T + PLANES]
+                    gathered[c, 1] = wide[:, T : T + PLANES]
+                else:
+                    win = keep.tile([P, T], F32, align_bytes=ALIGN, name=f"win{c}{t}")
+                    windows[c, t] = win[:]
+            if c > 0:
+                first = keep.tile([P, PLANES], F32, align_bytes=ALIGN, name=f"gath{c}")
+                gathered[c, 0] = first[:]
+        w_raw = [keep.tile([P, PASSES, K_PASS], F32, align_bytes=ALIGN, name=f"wraw{e}") for e in range(E)]
+        w_mixed = [keep.tile([P, PASSES * K_PASS], BF16, align_bytes=ALIGN, name=f"wmixed{e}") for e in range(E)]
+        w_codes = [keep.tile([P, PASSES * K], U32, align_bytes=ALIGN, name=f"wcodes{e}") for e in range(E)]
+        w_scales = [keep.tile([P, PASSES * K], U8, align_bytes=ALIGN, name=f"wscales{e}") for e in range(E)]
+        g_mixed = [keep.tile([P, 2 * PLANES], BF16, align_bytes=ALIGN, name=f"gmixed{c}") for c in range(PASSES)]
+        g_codes = [keep.tile([P, S], U32, align_bytes=ALIGN, name=f"gcodes{c}") for c in range(PASSES)]
+        g_scales = [keep.tile([P, S], U8, align_bytes=ALIGN, name=f"gscales{c}") for c in range(PASSES)]
         result = keep.tile([P, T], F32, align_bytes=ALIGN, name="result")
         slots = keep.tile([P, S], F32, align_bytes=ALIGN, name="slots")
-        acc = [psum.tile([P, C], F32, name=f"acc{e}") for e in range(E)]
+        acc = {}
 
         dy_rows = dyT.rearrange("(c p t) x -> c p t x", p=P, t=PACK)
-        w_rows = w.rearrange("e (c p t) k -> c p e (t k)", p=P, t=PACK)
+        w_rows = w.rearrange("e (c p t) k -> e p c (t k)", p=P, t=PACK)
 
         def load_window(c, t):
-            nc.sync.dma_start(out=windows[c, t][:, 0:T], in_=dy_rows[c, :, t, :])
+            nc.sync.dma_start(out=windows[c, t], in_=dy_rows[c, :, t, :])
 
-        def load_pair(c, q):
-            h, i = divmod(2 * q, EH)
-            if c == LAST and q >= PAIRS - PAIRS_BY_EXPERT:
-                for j in range(2):
-                    nc.sync.dma_start(
-                        out=w_raw[c, h][:, i + j].rearrange("p t k -> p (t k)"), in_=w_rows[c, :, 2 * q + j, :]
-                    )
-            else:
-                nc.sync.dma_start(
-                    out=w_raw[c, h][:, i : i + 2].rearrange("p e t k -> p e (t k)"),
-                    in_=w_rows[c, :, 2 * q : 2 * q + 2, :],
-                )
+        def spread_gates():
+            nc.vector.memset(zero[:], 0.0)
+            nc.scalar.activation(identity[:], zero[:].to_broadcast([P, P]), COPY)
+            make_identity(nc, identity[:], nomemset=True)
+            for h in (1, 0):
+                for j in range(PACK):
+                    nc.tensor.transpose(gates[h][:, j::PACK], gate_cols[:, h, j : j + 1].to_broadcast([P, P]), identity[:])
+
+        def load_expert(e):
+            nc.sync.dma_start(out=w_raw[e][:], in_=w_rows[e])
 
         def listed(s0, n):
             return offsets[:, s0 // LIST_ROWS : (s0 + n) // LIST_ROWS]
 
-        def gather(dst, c, t, s0, n):
-            nc.vector.tensor_tensor(dst, windows[c, t][:].indirect(listed(s0, n)), gates[:, s0 : s0 + n], MULT)
+        def plane(c, h, t):
+            return gathered[c, h][:, t * HALF : (t + 1) * HALF]
 
-        def gather_pass(c):
-            gathered[c] = keep.tile([P, PACK, S], F32, align_bytes=ALIGN, tag=f"gath{c}", name=f"gath{c}")
+        def gather_scalar(c, h):
             for t in range(PACK):
-                for s0, n in HEAD if (c, t) == (0, 0) else ((0, S),):
-                    gather(gathered[c][:, t, s0 : s0 + n], c, t, s0, n)
+                win = windows[c, "wide"] if (c > 0 and h == 0 and t == PACK - 1) else windows[c, t]
+                nc.scalar.activation(plane(c, h, t), win.indirect(listed(h * HALF, HALF)), COPY)
 
-        def gather_last(h):
-            gathered[LAST, h] = keep.tile([P, PACK, HALF], F32, align_bytes=ALIGN, tag=f"gath{h}", name=f"gath_last{h}")
+        def gather_vector(c, h):
             for t in range(PACK):
-                gather(gathered[LAST, h][:, t, :], LAST, t, h * HALF, HALF)
+                nc.vector.tensor_copy(plane(c, h, t), windows[c, t].indirect(listed(h * HALF, HALF)))
 
-        def mix_g(c, h):
-            src = gathered[c][:, :, h * HALF : (h + 1) * HALF] if c < LAST else gathered[c, h][:]
-            group, i = place["g", c, h]
-            nc.scalar.copy(
-                out=mixed[group][:, i].rearrange("p (x r) t -> p x t r", r=RUN),
-                in_=src.rearrange("p t (x r) -> p x t r", r=RUN),
-            )
+        def g_views(c, h):
+            dst = g_mixed[c][:, h * PLANES : (h + 1) * PLANES].rearrange("p (x r t) -> p x t r", r=RUN, t=PACK)
+            src = gathered[c, h].rearrange("p (t x r) -> p x t r", r=RUN, t=PACK)
+            return dst, src
 
-        def mix_w(c, h, experts):
-            group, i = place["w", c, h]
-            for e0 in range(0, EH, experts):
-                nc.scalar.copy(
-                    out=mixed[group][:, i, e0 * K : (e0 + experts) * K].rearrange(
-                        "p (e x r) t -> p e x t r", r=RUN, e=experts
-                    ),
-                    in_=w_raw[c, h][:, e0 : e0 + experts].rearrange("p e t (x r) -> p e x t r", r=RUN),
-                )
+        def gate_and_mix(c, h):
+            dst, src = g_views(c, h)
+            by_slot = gates[h][:].rearrange("p (x r) -> p x r", r=RUN).unsqueeze(2).to_broadcast([P, HALF // RUN, PACK, RUN])
+            nc.vector.tensor_tensor(dst, src, by_slot, MULT)
 
-        def quantise(group):
+        def quantise_g(c, s0, n):
             nc.vector.quantize_mx(
-                out=codes[group][:].bitcast(FP8X4),
-                scales=scales[group][:],
-                in_=mixed[group][:].rearrange("p i x t -> p (i x t)"),
+                out=g_codes[c][:, s0 : s0 + n].bitcast(FP8X4),
+                scales=g_scales[c][:, s0 : s0 + n],
+                in_=g_mixed[c][:, s0 * PACK : (s0 + n) * PACK],
             )
 
-        def multiply(c, e):
-            h, i = divmod(e, EH)
-            w_group, w_place = place["w", c, h]
-            g_group, g_place = place["g", c, h]
-            w_cols = slice(w_place * HALF + i * K, w_place * HALF + (i + 1) * K)
-            g_cols = slice(g_place * HALF + i * C, g_place * HALF + (i + 1) * C)
-            nc.tensor.matmul_mx(
-                out=acc[e][:],
-                lhsT=codes[w_group][:, w_cols].bitcast(FP8X4),
-                lhsT_scale=scales[w_group][:, w_cols],
-                rhs=codes[g_group][:, g_cols].bitcast(FP8X4),
-                rhs_scale=scales[g_group][:, g_cols],
-                start=(c == 0),
-                stop=(c == LAST),
-            )
-
-        def products(h):
-            experts = range(h * EH, (h + 1) * EH)
-            for c in range(LAST):
-                for e in experts:
-                    multiply(c, e)
-            for e in experts:
-                multiply(LAST, e)
-                nc.scalar.copy(out=slots[:, e * C : (e + 1) * C], in_=acc[e][:])
-
-        def scatter(h):
+        def prepare_expert(e):
             nc.vector.tensor_copy(
-                out=result[:].indirect(listed(h * HALF, HALF)), in_=slots[:, h * HALF : (h + 1) * HALF]
+                out=w_mixed[e][:].rearrange("p (c x r t) -> p x c t r", c=PASSES, r=RUN, t=PACK),
+                in_=w_raw[e][:].rearrange("p c (t x r) -> p x c t r", r=RUN, t=PACK),
             )
+
+        def prepare_expert_scalar(e):
+            nc.scalar.copy(
+                out=w_mixed[e][:].rearrange("p (c x r t) -> p c x t r", c=PASSES, r=RUN, t=PACK),
+                in_=w_raw[e][:].rearrange("p c (t x r) -> p c x t r", r=RUN, t=PACK),
+            )
+
+        def quantise_w(e):
+            nc.vector.quantize_mx(out=w_codes[e][:].bitcast(FP8X4), scales=w_scales[e][:], in_=w_mixed[e][:])
+
+        def finish(i):
+            e0, n = SCATTERS[i]
+            acc[i] = psum.tile([P, n * C], F32, tag=f"acc{i}", name=f"acc{i}")
+            for e in range(e0, e0 + n):
+                for c in range(PASSES):
+                    nc.tensor.matmul_mx(
+                        out=acc[i][:, (e - e0) * C : (e - e0 + 1) * C],
+                        lhsT=w_codes[e][:, c * K : (c + 1) * K].bitcast(FP8X4),
+                        lhsT_scale=w_scales[e][:, c * K : (c + 1) * K],
+                        rhs=g_codes[c][:, e * C : (e + 1) * C].bitcast(FP8X4),
+                        rhs_scale=g_scales[c][:, e * C : (e + 1) * C],
+                        start=(c == 0),
+                        stop=(c == LAST),
+                    )
+            cols = slice(e0 * C, (e0 + n) * C)
+            nc.scalar.copy(out=slots[:, cols], in_=acc[i][:])
+            nc.scalar.activation(result[:].indirect(listed(e0 * C, n * C)), slots[:, cols], COPY)
 
         load_window(0, 0)
         nc.sync.dma_start(offsets[:], offs)
-        for s0, n in HEAD:
-            nc.sync.dma_start(out=gates[:, s0 : s0 + n], in_=gate[0:P, s0 : s0 + n])
-        pairs = [(c, q) for c in range(PASSES) for q in range(PAIRS)]
-        loaded = 0
-        for c in range(PASSES):
-            for t in range(PACK):
-                if (c, t) == (0, 0):
-                    continue
-                load_window(c, t)
-                behind = 1 + EXTRA_PAIRS.get((c, t), 0) if c < LAST else 0
-                for pair in pairs[loaded : loaded + behind]:
-                    load_pair(*pair)
-                loaded = loaded + behind
-        for pair in pairs[loaded:]:
-            load_pair(*pair)
+        nc.sync.dma_start(out=gate_cols[:], in_=gate[0, :].rearrange("(h p j) -> p h j", p=P, j=PACK))
+        for t in range(1, PACK):
+            load_window(0, t)
+        for t in range(PACK):
+            load_window(1, t)
+        load_expert(0)
+        load_expert(1)
+        for t in range(PACK):
+            load_window(2, t)
+        for e in range(2, E):
+            load_expert(e)
 
-        gather_pass(0)
-        mix_w(0, 0, 2)
-        mix_w(0, 1, 2)
-        mix_g(0, 0)
-        mix_g(0, 1)
-        gather_pass(1)
-        quantise("w_pass0")
-        quantise("g_pass0")
-        mix_w(1, 0, EH)
-        mix_w(1, 1, 2)
-        mix_w(LAST, 0, 2)
-        mix_g(1, 0)
-        mix_g(1, 1)
-        gather_last(0)
-        quantise("w_half0")
-        mix_g(LAST, 0)
-        gather_last(1)
-        mix_w(LAST, 1, EH)
-        mix_g(LAST, 1)
-        quantise("g_pass1")
-        quantise("g_last0")
-        quantise("w_half1")
-        quantise("g_last1")
-        products(0)
-        products(1)
-        scatter(0)
-        scatter(1)
+        spread_gates()
+        gather_scalar(0, 0)
+        gather_vector(0, 1)
+        gate_and_mix(0, 1)
+        gate_and_mix(0, 0)
+        quantise_g(0, 0, S)
+        gather_scalar(1, 0)
+        gather_scalar(1, 1)
+        gate_and_mix(1, 0)
+        prepare_expert(0)
+        quantise_g(1, 0, HALF)
+        prepare_expert(1)
+        quantise_w(0)
+        quantise_w(1)
+        gate_and_mix(1, 1)
+        prepare_expert(2)
+        quantise_g(1, HALF, HALF)
+        quantise_w(2)
+        gather_scalar(2, 0)
+        gather_scalar(2, 1)
+        prepare_expert_scalar(4)
+        gate_and_mix(2, 0)
+        prepare_expert(3)
+        quantise_g(2, 0, HALF)
+        quantise_w(3)
+        finish(0)
+        finish(1)
+        gate_and_mix(2, 1)
+        quantise_w(4)
+        quantise_g(2, HALF, HALF)
+        finish(2)
+        prepare_expert(5)
+        prepare_expert(6)
+        quantise_w(5)
+        finish(3)
+        quantise_w(6)
+        finish(4)
+        prepare_expert(7)
+        quantise_w(7)
+        finish(5)
         nc.sync.dma_start(out=out, in_=result[:])

@@ -23,9 +23,10 @@ HALF = S // 2
 EH = E // 2
 LIST_ROWS = 16
 ALIGN = 256
-RUN = 2
+RUN = 4
+POOL = 96
 PLANES = PACK * HALF
-SCATTERS = ((0, 2), (2, 2), (4, 1), (5, 1), (6, 1), (7, 1))
+SCATTERS = ((0, 3), (3, 1), (4, 2), (6, 1), (7, 1))
 
 FLOPS = 2 * K * N * S
 BYTES = 4 * (N * T + E * N * K + K * T + S) + 2 * S
@@ -41,6 +42,7 @@ def tile_moe_bdx_lin_none_kernel(tc, dyT, w, gate, offs, out):
         identity = keep.tile([P, P], F32, align_bytes=ALIGN, name="identity")
         zero = keep.tile([P, 1], F32, name="zero")
         gate_cols = keep.tile([P, 2, PACK], F32, align_bytes=ALIGN, name="gate_cols")
+        pool_gates = keep.tile([P, 2, POOL], F32, align_bytes=ALIGN, name="pool_gates")
         gates = [psum.tile([P, HALF], F32, name=f"gates{h}") for h in range(2)]
         windows, gathered = {}, {}
         for c in range(PASSES):
@@ -48,7 +50,7 @@ def tile_moe_bdx_lin_none_kernel(tc, dyT, w, gate, offs, out):
                 if c > 0 and t == PACK - 1:
                     wide = keep.tile([P, T + PLANES], F32, align_bytes=ALIGN, name=f"win{c}{t}")
                     windows[c, t] = wide[:, 0:T]
-                    windows[c, "wide"] = wide[:]
+                    windows[c, "wide"] = wide[:, 0 : T + PLANES - (c - 1) * HALF]
                     gathered[0, c - 1] = wide[:, T : T + PLANES]
                     gathered[c, 1] = wide[:, T : T + PLANES]
                 else:
@@ -81,6 +83,8 @@ def tile_moe_bdx_lin_none_kernel(tc, dyT, w, gate, offs, out):
             for h in (1, 0):
                 for j in range(PACK):
                     nc.tensor.transpose(gates[h][:, j::PACK], gate_cols[:, h, j : j + 1].to_broadcast([P, P]), identity[:])
+                if j == PACK - 1:
+                    nc.vector.tensor_copy(out=pool_gates[:, h], in_=gates[h][:, 0:POOL])
 
         def load_expert(e):
             nc.sync.dma_start(out=w_raw[e][:], in_=w_rows[e])
@@ -91,24 +95,31 @@ def tile_moe_bdx_lin_none_kernel(tc, dyT, w, gate, offs, out):
         def plane(c, h, t):
             return gathered[c, h][:, t * HALF : (t + 1) * HALF]
 
-        def gather_scalar(c, h):
-            for t in range(PACK):
+        def gather_scalar(c, h, count=PACK):
+            for t in range(count):
                 win = windows[c, "wide"] if (c > 0 and h == 0 and t == PACK - 1) else windows[c, t]
                 nc.scalar.activation(plane(c, h, t), win.indirect(listed(h * HALF, HALF)), COPY)
 
-        def gather_vector(c, h):
-            for t in range(PACK):
+        def gather_vector(c, h, first=0):
+            for t in range(first, PACK):
                 nc.vector.tensor_copy(plane(c, h, t), windows[c, t].indirect(listed(h * HALF, HALF)))
 
-        def g_views(c, h):
-            dst = g_mixed[c][:, h * PLANES : (h + 1) * PLANES].rearrange("p (x r t) -> p x t r", r=RUN, t=PACK)
-            src = gathered[c, h].rearrange("p (t x r) -> p x t r", r=RUN, t=PACK)
-            return dst, src
-
         def gate_and_mix(c, h):
-            dst, src = g_views(c, h)
-            by_slot = gates[h][:].rearrange("p (x r) -> p x r", r=RUN).unsqueeze(2).to_broadcast([P, HALF // RUN, PACK, RUN])
-            nc.vector.tensor_tensor(dst, src, by_slot, MULT)
+            dst = g_mixed[c][:, h * PLANES : (h + 1) * PLANES].rearrange("p (s t) -> p s t", t=PACK)
+            src = gathered[c, h].rearrange("p (t s) -> p t s", t=PACK)
+            nc.gpsimd.tensor_tensor(
+                dst[:, 0:POOL],
+                src[:, :, 0:POOL].rearrange("p t s -> p s t"),
+                pool_gates[:, h].unsqueeze(2).to_broadcast([P, POOL, PACK]),
+                MULT,
+            )
+            by_slot = gates[h][:, POOL:HALF].rearrange("p (x r) -> p x r", r=RUN)
+            nc.vector.tensor_tensor(
+                dst[:, POOL:HALF].rearrange("p (x r) t -> p x t r", r=RUN),
+                src[:, :, POOL:HALF].rearrange("p t (x r) -> p x t r", r=RUN),
+                by_slot.unsqueeze(2).to_broadcast([P, (HALF - POOL) // RUN, PACK, RUN]),
+                MULT,
+            )
 
         def quantise_g(c, s0, n):
             nc.vector.quantize_mx(
@@ -117,22 +128,26 @@ def tile_moe_bdx_lin_none_kernel(tc, dyT, w, gate, offs, out):
                 in_=g_mixed[c][:, s0 * PACK : (s0 + n) * PACK],
             )
 
-        def prepare_expert(e):
+        def prepare_expert(e, c0=0, n=PASSES):
             nc.vector.tensor_copy(
-                out=w_mixed[e][:].rearrange("p (c x r t) -> p x c t r", c=PASSES, r=RUN, t=PACK),
-                in_=w_raw[e][:].rearrange("p c (t x r) -> p x c t r", r=RUN, t=PACK),
+                out=w_mixed[e][:, c0 * K_PASS : (c0 + n) * K_PASS].rearrange("p (c x r t) -> p x c t r", c=n, r=RUN, t=PACK),
+                in_=w_raw[e][:, c0 : c0 + n].rearrange("p c (t x r) -> p x c t r", r=RUN, t=PACK),
             )
 
-        def prepare_expert_scalar(e):
+        def prepare_expert_scalar(e, n):
             nc.scalar.copy(
-                out=w_mixed[e][:].rearrange("p (c x r t) -> p c x t r", c=PASSES, r=RUN, t=PACK),
-                in_=w_raw[e][:].rearrange("p c (t x r) -> p c x t r", r=RUN, t=PACK),
+                out=w_mixed[e][:, 0 : n * K_PASS].rearrange("p (c x r t) -> p c x t r", c=n, r=RUN, t=PACK),
+                in_=w_raw[e][:, 0:n].rearrange("p c (t x r) -> p c x t r", r=RUN, t=PACK),
             )
 
-        def quantise_w(e):
-            nc.vector.quantize_mx(out=w_codes[e][:].bitcast(FP8X4), scales=w_scales[e][:], in_=w_mixed[e][:])
+        def quantise_w(e, c0=0, n=PASSES):
+            nc.vector.quantize_mx(
+                out=w_codes[e][:, c0 * K : (c0 + n) * K].bitcast(FP8X4),
+                scales=w_scales[e][:, c0 * K : (c0 + n) * K],
+                in_=w_mixed[e][:, c0 * K_PASS : (c0 + n) * K_PASS],
+            )
 
-        def finish(i):
+        def finish(i, evacuate):
             e0, n = SCATTERS[i]
             acc[i] = psum.tile([P, n * C], F32, tag=f"acc{i}", name=f"acc{i}")
             for e in range(e0, e0 + n):
@@ -147,7 +162,7 @@ def tile_moe_bdx_lin_none_kernel(tc, dyT, w, gate, offs, out):
                         stop=(c == LAST),
                     )
             cols = slice(e0 * C, (e0 + n) * C)
-            nc.scalar.copy(out=slots[:, cols], in_=acc[i][:])
+            evacuate(out=slots[:, cols], in_=acc[i][:])
             nc.scalar.activation(result[:].indirect(listed(e0 * C, n * C)), slots[:, cols], COPY)
 
         load_window(0, 0)
@@ -177,31 +192,33 @@ def tile_moe_bdx_lin_none_kernel(tc, dyT, w, gate, offs, out):
         quantise_g(1, 0, HALF)
         prepare_expert(1)
         quantise_w(0)
-        quantise_w(1)
         gate_and_mix(1, 1)
-        prepare_expert(2)
+        quantise_w(1)
         quantise_g(1, HALF, HALF)
-        quantise_w(2)
         gather_scalar(2, 0)
-        gather_scalar(2, 1)
-        prepare_expert_scalar(4)
+        gather_vector(2, 1, PACK - 1)
+        gather_scalar(2, 1, PACK - 1)
+        prepare_expert_scalar(3, PASSES)
         gate_and_mix(2, 0)
-        prepare_expert(3)
+        prepare_expert(2)
         quantise_g(2, 0, HALF)
-        quantise_w(3)
-        finish(0)
-        finish(1)
+        quantise_w(2)
+        finish(0, nc.scalar.copy)
         gate_and_mix(2, 1)
-        quantise_w(4)
+        quantise_w(3)
+        finish(1, nc.scalar.copy)
         quantise_g(2, HALF, HALF)
-        finish(2)
+        prepare_expert(4)
         prepare_expert(5)
-        prepare_expert(6)
+        quantise_w(4)
         quantise_w(5)
-        finish(3)
+        finish(2, nc.scalar.copy)
+        prepare_expert(6)
+        prepare_expert(7, 0, LAST)
         quantise_w(6)
-        finish(4)
-        prepare_expert(7)
-        quantise_w(7)
-        finish(5)
+        prepare_expert(7, LAST, 1)
+        quantise_w(7, 0, LAST)
+        finish(3, nc.vector.tensor_copy)
+        quantise_w(7, LAST, 1)
+        finish(4, nc.vector.tensor_copy)
         nc.sync.dma_start(out=out, in_=result[:])

@@ -19,14 +19,16 @@ PACK = 4
 K_PASS = P * PACK
 PASSES = N // K_PASS
 LAST = PASSES - 1
+LAST_ROW = PACK - 1
 HALF = S // 2
-EH = E // 2
+PLANES = PACK * HALF
+W_COLS = PASSES * PACK * K
 LIST_ROWS = 16
 ALIGN = 256
+
 RUN = 4
 POOL = 96
-PLANES = PACK * HALF
-SCATTERS = ((0, 3), (3, 1), (4, 2), (6, 1), (7, 1))
+GROUPS = ((0, 3), (3, 1), (4, 2), (6, 1), (7, 1))
 
 FLOPS = 2 * K * N * S
 BYTES = 4 * (N * T + E * N * K + K * T + S) + 2 * S
@@ -44,31 +46,45 @@ def tile_moe_bdx_lin_none_kernel(tc, dyT, w, gate, offs, out):
         gate_cols = keep.tile([P, 2, PACK], F32, align_bytes=ALIGN, name="gate_cols")
         pool_gates = keep.tile([P, 2, POOL], F32, align_bytes=ALIGN, name="pool_gates")
         gates = [psum.tile([P, HALF], F32, name=f"gates{h}") for h in range(2)]
-        windows, gathered = {}, {}
+
+        windows, long_window, planes = {}, {}, {}
         for c in range(PASSES):
             for t in range(PACK):
-                if c > 0 and t == PACK - 1:
+                if c > 0 and t == LAST_ROW:
                     wide = keep.tile([P, T + PLANES], F32, align_bytes=ALIGN, name=f"win{c}{t}")
                     windows[c, t] = wide[:, 0:T]
-                    windows[c, "wide"] = wide[:, 0 : T + PLANES - (c - 1) * HALF]
-                    gathered[0, c - 1] = wide[:, T : T + PLANES]
-                    gathered[c, 1] = wide[:, T : T + PLANES]
+                    long_window[c] = wide[:, 0 : T + (PLANES - HALF if c == LAST else PLANES)]
+                    planes[0, c - 1] = wide[:, T : T + PLANES]
+                    planes[c, 1] = wide[:, T : T + PLANES]
                 else:
                     win = keep.tile([P, T], F32, align_bytes=ALIGN, name=f"win{c}{t}")
                     windows[c, t] = win[:]
             if c > 0:
-                first = keep.tile([P, PLANES], F32, align_bytes=ALIGN, name=f"gath{c}")
-                gathered[c, 0] = first[:]
-        w_raw = [keep.tile([P, PASSES, K_PASS], F32, align_bytes=ALIGN, name=f"wraw{e}") for e in range(E)]
-        w_mixed = [keep.tile([P, PASSES * K_PASS], BF16, align_bytes=ALIGN, name=f"wmixed{e}") for e in range(E)]
-        w_codes = [keep.tile([P, PASSES * K], U32, align_bytes=ALIGN, name=f"wcodes{e}") for e in range(E)]
-        w_scales = [keep.tile([P, PASSES * K], U8, align_bytes=ALIGN, name=f"wscales{e}") for e in range(E)]
-        g_mixed = [keep.tile([P, 2 * PLANES], BF16, align_bytes=ALIGN, name=f"gmixed{c}") for c in range(PASSES)]
-        g_codes = [keep.tile([P, S], U32, align_bytes=ALIGN, name=f"gcodes{c}") for c in range(PASSES)]
-        g_scales = [keep.tile([P, S], U8, align_bytes=ALIGN, name=f"gscales{c}") for c in range(PASSES)]
+                first = keep.tile([P, PLANES], F32, align_bytes=ALIGN, name=f"planes{c}")
+                planes[c, 0] = first[:]
+
+        both = keep.tile([P, 2 * PLANES], BF16, align_bytes=ALIGN, name="g_mixed0")
+        g_mixed = {(0, h): both[:, h * PLANES : (h + 1) * PLANES] for h in range(2)}
+        w_mixed = {}
+        lead = W_COLS - POOL * PACK
+        for c, e in ((1, 0), (LAST, 2)):
+            own = keep.tile([P, PLANES], BF16, align_bytes=ALIGN, name=f"g_mixed{c}")
+            shared = keep.tile([P, lead + PLANES], BF16, align_bytes=ALIGN, name=f"shared{c}")
+            g_mixed[c, 0] = own[:]
+            g_mixed[c, 1] = shared[:, lead : lead + PLANES]
+            w_mixed[e] = shared[:, 0:W_COLS]
+        for e in range(E):
+            if e not in w_mixed:
+                own = keep.tile([P, W_COLS], BF16, align_bytes=ALIGN, name=f"w_mixed{e}")
+                w_mixed[e] = own[:]
+
+        w_raw = [keep.tile([P, PASSES, PACK * K], F32, align_bytes=ALIGN, name=f"w_raw{e}") for e in range(E)]
+        w_codes = [keep.tile([P, PASSES * K], U32, align_bytes=ALIGN, name=f"w_codes{e}") for e in range(E)]
+        w_scales = [keep.tile([P, PASSES * K], U8, align_bytes=ALIGN, name=f"w_scales{e}") for e in range(E)]
+        g_codes = [keep.tile([P, S], U32, align_bytes=ALIGN, name=f"g_codes{c}") for c in range(PASSES)]
+        g_scales = [keep.tile([P, S], U8, align_bytes=ALIGN, name=f"g_scales{c}") for c in range(PASSES)]
         result = keep.tile([P, T], F32, align_bytes=ALIGN, name="result")
         slots = keep.tile([P, S], F32, align_bytes=ALIGN, name="slots")
-        acc = {}
 
         dy_rows = dyT.rearrange("(c p t) x -> c p t x", p=P, t=PACK)
         w_rows = w.rearrange("e (c p t) k -> e p c (t k)", p=P, t=PACK)
@@ -76,37 +92,39 @@ def tile_moe_bdx_lin_none_kernel(tc, dyT, w, gate, offs, out):
         def load_window(c, t):
             nc.sync.dma_start(out=windows[c, t], in_=dy_rows[c, :, t, :])
 
+        def load_expert(e):
+            parts = [(c, 1) for c in range(PASSES)] if e == E - 1 else [(0, LAST), (LAST, 1)]
+            for c0, n in parts:
+                nc.sync.dma_start(out=w_raw[e][:, c0 : c0 + n], in_=w_rows[e, :, c0 : c0 + n])
+
         def spread_gates():
             nc.vector.memset(zero[:], 0.0)
             nc.scalar.activation(identity[:], zero[:].to_broadcast([P, P]), COPY)
             make_identity(nc, identity[:], nomemset=True)
             for h in (1, 0):
                 for j in range(PACK):
-                    nc.tensor.transpose(gates[h][:, j::PACK], gate_cols[:, h, j : j + 1].to_broadcast([P, P]), identity[:])
-                if j == PACK - 1:
-                    nc.vector.tensor_copy(out=pool_gates[:, h], in_=gates[h][:, 0:POOL])
-
-        def load_expert(e):
-            nc.sync.dma_start(out=w_raw[e][:], in_=w_rows[e])
+                    column = gate_cols[:, h, j : j + 1].to_broadcast([P, P])
+                    nc.tensor.transpose(gates[h][:, j::PACK], column, identity[:])
+                nc.vector.tensor_copy(out=pool_gates[:, h], in_=gates[h][:, 0:POOL])
 
         def listed(s0, n):
             return offsets[:, s0 // LIST_ROWS : (s0 + n) // LIST_ROWS]
 
         def plane(c, h, t):
-            return gathered[c, h][:, t * HALF : (t + 1) * HALF]
+            return planes[c, h][:, t * HALF : (t + 1) * HALF]
 
-        def gather_scalar(c, h, count=PACK):
-            for t in range(count):
-                win = windows[c, "wide"] if (c > 0 and h == 0 and t == PACK - 1) else windows[c, t]
-                nc.scalar.activation(plane(c, h, t), win.indirect(listed(h * HALF, HALF)), COPY)
+        def gather_on_scalar(c, h, rows):
+            for t in rows:
+                window = long_window[c] if c > 0 and (h, t) == (0, LAST_ROW) else windows[c, t]
+                nc.scalar.activation(plane(c, h, t), window.indirect(listed(h * HALF, HALF)), COPY)
 
-        def gather_vector(c, h, first=0):
-            for t in range(first, PACK):
+        def gather_on_vector(c, h, rows):
+            for t in rows:
                 nc.vector.tensor_copy(plane(c, h, t), windows[c, t].indirect(listed(h * HALF, HALF)))
 
         def gate_and_mix(c, h):
-            dst = g_mixed[c][:, h * PLANES : (h + 1) * PLANES].rearrange("p (s t) -> p s t", t=PACK)
-            src = gathered[c, h].rearrange("p (t s) -> p t s", t=PACK)
+            dst = g_mixed[c, h].rearrange("p (s t) -> p s t", t=PACK)
+            src = planes[c, h].rearrange("p (t s) -> p t s", t=PACK)
             nc.gpsimd.tensor_tensor(
                 dst[:, 0:POOL],
                 src[:, :, 0:POOL].rearrange("p t s -> p s t"),
@@ -121,23 +139,26 @@ def tile_moe_bdx_lin_none_kernel(tc, dyT, w, gate, offs, out):
                 MULT,
             )
 
-        def quantise_g(c, s0, n):
+        def quantise_g(src, c, s0, n):
             nc.vector.quantize_mx(
-                out=g_codes[c][:, s0 : s0 + n].bitcast(FP8X4),
-                scales=g_scales[c][:, s0 : s0 + n],
-                in_=g_mixed[c][:, s0 * PACK : (s0 + n) * PACK],
+                out=g_codes[c][:, s0 : s0 + n].bitcast(FP8X4), scales=g_scales[c][:, s0 : s0 + n], in_=src
             )
 
-        def prepare_expert(e, c0=0, n=PASSES):
+        def quantise_half(c, h):
+            quantise_g(g_mixed[c, h], c, h * HALF, HALF)
+
+        def mix_on_vector(e, c0=0, n=PASSES):
             nc.vector.tensor_copy(
-                out=w_mixed[e][:, c0 * K_PASS : (c0 + n) * K_PASS].rearrange("p (c x r t) -> p x c t r", c=n, r=RUN, t=PACK),
+                out=w_mixed[e][:, c0 * K_PASS : (c0 + n) * K_PASS].rearrange(
+                    "p (c x r t) -> p x c t r", c=n, r=RUN, t=PACK
+                ),
                 in_=w_raw[e][:, c0 : c0 + n].rearrange("p c (t x r) -> p x c t r", r=RUN, t=PACK),
             )
 
-        def prepare_expert_scalar(e, n):
+        def mix_on_scalar(e):
             nc.scalar.copy(
-                out=w_mixed[e][:, 0 : n * K_PASS].rearrange("p (c x r t) -> p c x t r", c=n, r=RUN, t=PACK),
-                in_=w_raw[e][:, 0:n].rearrange("p c (t x r) -> p c x t r", r=RUN, t=PACK),
+                out=w_mixed[e].rearrange("p (c x r t) -> p c x t r", c=PASSES, r=RUN, t=PACK),
+                in_=w_raw[e][:].rearrange("p c (t x r) -> p c x t r", r=RUN, t=PACK),
             )
 
         def quantise_w(e, c0=0, n=PASSES):
@@ -147,13 +168,13 @@ def tile_moe_bdx_lin_none_kernel(tc, dyT, w, gate, offs, out):
                 in_=w_mixed[e][:, c0 * K_PASS : (c0 + n) * K_PASS],
             )
 
-        def finish(i, evacuate):
-            e0, n = SCATTERS[i]
-            acc[i] = psum.tile([P, n * C], F32, tag=f"acc{i}", name=f"acc{i}")
-            for e in range(e0, e0 + n):
+        def finish(group, empty_bank):
+            e0, count = GROUPS[group]
+            sums = psum.tile([P, count * C], F32, name=f"sums{group}")
+            for e in range(e0, e0 + count):
                 for c in range(PASSES):
                     nc.tensor.matmul_mx(
-                        out=acc[i][:, (e - e0) * C : (e - e0 + 1) * C],
+                        out=sums[:, (e - e0) * C : (e - e0 + 1) * C],
                         lhsT=w_codes[e][:, c * K : (c + 1) * K].bitcast(FP8X4),
                         lhsT_scale=w_scales[e][:, c * K : (c + 1) * K],
                         rhs=g_codes[c][:, e * C : (e + 1) * C].bitcast(FP8X4),
@@ -161,9 +182,9 @@ def tile_moe_bdx_lin_none_kernel(tc, dyT, w, gate, offs, out):
                         start=(c == 0),
                         stop=(c == LAST),
                     )
-            cols = slice(e0 * C, (e0 + n) * C)
-            evacuate(out=slots[:, cols], in_=acc[i][:])
-            nc.scalar.activation(result[:].indirect(listed(e0 * C, n * C)), slots[:, cols], COPY)
+            cols = slice(e0 * C, (e0 + count) * C)
+            empty_bank(out=slots[:, cols], in_=sums[:])
+            nc.scalar.activation(result[:].indirect(listed(e0 * C, count * C)), slots[:, cols], COPY)
 
         load_window(0, 0)
         nc.sync.dma_start(offsets[:], offs)
@@ -175,50 +196,53 @@ def tile_moe_bdx_lin_none_kernel(tc, dyT, w, gate, offs, out):
         load_expert(0)
         load_expert(1)
         for t in range(PACK):
-            load_window(2, t)
+            load_window(LAST, t)
         for e in range(2, E):
             load_expert(e)
 
         spread_gates()
-        gather_scalar(0, 0)
-        gather_vector(0, 1)
+        gather_on_scalar(0, 0, range(PACK))
+        gather_on_vector(0, 1, range(PACK))
         gate_and_mix(0, 1)
         gate_and_mix(0, 0)
-        quantise_g(0, 0, S)
-        gather_scalar(1, 0)
-        gather_scalar(1, 1)
+        quantise_g(both[:], 0, 0, S)
+
+        gather_on_scalar(1, 0, range(PACK))
+        gather_on_scalar(1, 1, range(PACK))
         gate_and_mix(1, 0)
-        prepare_expert(0)
-        quantise_g(1, 0, HALF)
-        prepare_expert(1)
+        mix_on_vector(0)
+        quantise_half(1, 0)
+        mix_on_vector(1)
         quantise_w(0)
         gate_and_mix(1, 1)
         quantise_w(1)
-        quantise_g(1, HALF, HALF)
-        gather_scalar(2, 0)
-        gather_vector(2, 1, PACK - 1)
-        gather_scalar(2, 1, PACK - 1)
-        prepare_expert_scalar(3, PASSES)
-        gate_and_mix(2, 0)
-        prepare_expert(2)
-        quantise_g(2, 0, HALF)
+        quantise_half(1, 1)
+
+        gather_on_scalar(LAST, 0, range(PACK))
+        gather_on_vector(LAST, 1, [LAST_ROW])
+        gather_on_scalar(LAST, 1, range(LAST_ROW))
+        mix_on_scalar(3)
+        gate_and_mix(LAST, 0)
+        mix_on_vector(2)
+        quantise_half(LAST, 0)
         quantise_w(2)
         finish(0, nc.scalar.copy)
-        gate_and_mix(2, 1)
+        mix_on_vector(4)
+        gate_and_mix(LAST, 1)
         quantise_w(3)
         finish(1, nc.scalar.copy)
-        quantise_g(2, HALF, HALF)
-        prepare_expert(4)
-        prepare_expert(5)
+        quantise_half(LAST, 1)
+
+        mix_on_vector(5)
         quantise_w(4)
         quantise_w(5)
         finish(2, nc.scalar.copy)
-        prepare_expert(6)
-        prepare_expert(7, 0, LAST)
+        mix_on_vector(6)
+        mix_on_vector(E - 1, 0, LAST)
         quantise_w(6)
-        prepare_expert(7, LAST, 1)
-        quantise_w(7, 0, LAST)
-        finish(3, nc.vector.tensor_copy)
-        quantise_w(7, LAST, 1)
+        finish(3, nc.scalar.copy)
+        mix_on_vector(E - 1, LAST, 1)
+        quantise_w(E - 1, 0, LAST)
+        quantise_w(E - 1, LAST, 1)
         finish(4, nc.vector.tensor_copy)
         nc.sync.dma_start(out=out, in_=result[:])

@@ -27,8 +27,8 @@ LIST_ROWS = 16
 ALIGN = 256
 
 RUN = 4
-POOL = 96
-GROUPS = ((0, 3), (3, 1), (4, 2), (6, 1), (7, 1))
+POOL = {(0, 0): HALF, (0, 1): 0, (1, 0): 256, (1, 1): 0, (2, 0): 128, (2, 1): 128}
+GROUPS = ((0, 2), (2, 2), (4, 2), (6, 1), (7, 1))
 
 FLOPS = 2 * K * N * S
 BYTES = 4 * (N * T + E * N * K + K * T + S) + 2 * S
@@ -44,45 +44,38 @@ def tile_moe_bdx_lin_none_kernel(tc, dyT, w, gate, offs, out):
         identity = keep.tile([P, P], F32, align_bytes=ALIGN, name="identity")
         zero = keep.tile([P, 1], F32, name="zero")
         gate_cols = keep.tile([P, 2, PACK], F32, align_bytes=ALIGN, name="gate_cols")
-        pool_gates = keep.tile([P, 2, POOL], F32, align_bytes=ALIGN, name="pool_gates")
+        pool_width = [max(POOL[c, h] for c in range(PASSES)) for h in range(2)]
+        pool_gates = [keep.tile([P, pool_width[h]], F32, align_bytes=ALIGN, name=f"pool_gates{h}") for h in range(2)]
         gates = [psum.tile([P, HALF], F32, name=f"gates{h}") for h in range(2)]
 
-        windows, long_window, planes = {}, {}, {}
+        long_window = keep.tile([P, T + PLANES], F32, align_bytes=ALIGN, name="long_window")
+        windows, planes = {(LAST, LAST_ROW): long_window[:, 0:T]}, {}
         for c in range(PASSES):
             for t in range(PACK):
-                if c > 0 and t == LAST_ROW:
-                    wide = keep.tile([P, T + PLANES], F32, align_bytes=ALIGN, name=f"win{c}{t}")
-                    windows[c, t] = wide[:, 0:T]
-                    long_window[c] = wide[:, 0 : T + (PLANES - HALF if c == LAST else PLANES)]
-                    planes[0, c - 1] = wide[:, T : T + PLANES]
-                    planes[c, 1] = wide[:, T : T + PLANES]
-                else:
+                if (c, t) not in windows:
                     win = keep.tile([P, T], F32, align_bytes=ALIGN, name=f"win{c}{t}")
                     windows[c, t] = win[:]
-            if c > 0:
-                first = keep.tile([P, PLANES], F32, align_bytes=ALIGN, name=f"planes{c}")
-                planes[c, 0] = first[:]
+        for c, h in ((0, 0), (0, 1), (1, 1), (LAST, 0)):
+            own = keep.tile([P, PLANES], F32, align_bytes=ALIGN, name=f"planes{c}{h}")
+            planes[c, h] = own[:]
+        planes[1, 0] = planes[LAST, 1] = long_window[:, T : T + PLANES]
 
-        both = keep.tile([P, 2 * PLANES], BF16, align_bytes=ALIGN, name="g_mixed0")
-        g_mixed = {(0, h): both[:, h * PLANES : (h + 1) * PLANES] for h in range(2)}
-        w_mixed = {}
-        lead = W_COLS - POOL * PACK
-        for c, e in ((1, 0), (LAST, 2)):
-            own = keep.tile([P, PLANES], BF16, align_bytes=ALIGN, name=f"g_mixed{c}")
-            shared = keep.tile([P, lead + PLANES], BF16, align_bytes=ALIGN, name=f"shared{c}")
-            g_mixed[c, 0] = own[:]
-            g_mixed[c, 1] = shared[:, lead : lead + PLANES]
-            w_mixed[e] = shared[:, 0:W_COLS]
-        for e in range(E):
-            if e not in w_mixed:
-                own = keep.tile([P, W_COLS], BF16, align_bytes=ALIGN, name=f"w_mixed{e}")
-                w_mixed[e] = own[:]
+        mixed = keep.tile([P, 4 * PLANES], BF16, align_bytes=ALIGN, name="mixed")
+        early = [mixed[:, 2 * h * PLANES : 2 * (h + 1) * PLANES] for h in range(2)]
+        g_mixed = {(c, h): early[h][:, c * PLANES : (c + 1) * PLANES] for c in range(LAST) for h in range(2)}
+        g_mixed[LAST, 0] = early[0][:, 0:PLANES]
+        g_mixed[LAST, 1] = early[1][:, 0:PLANES]
+        w_mixed = {e: mixed[:, PLANES + e * W_COLS : PLANES + (e + 1) * W_COLS] for e in range(2)}
+        w_mixed[2] = windows[LAST, LAST_ROW].bitcast(BF16)[:, 0:W_COLS]
+        w_mixed[3] = planes[LAST, 1].bitcast(BF16)[:, 0:W_COLS]
+        for e in range(4, E):
+            w_mixed[e] = early[1][:, (e % 2) * W_COLS : (e % 2 + 1) * W_COLS]
 
         w_raw = [keep.tile([P, PASSES, PACK * K], F32, align_bytes=ALIGN, name=f"w_raw{e}") for e in range(E)]
         w_codes = [keep.tile([P, PASSES * K], U32, align_bytes=ALIGN, name=f"w_codes{e}") for e in range(E)]
         w_scales = [keep.tile([P, PASSES * K], U8, align_bytes=ALIGN, name=f"w_scales{e}") for e in range(E)]
-        g_codes = [keep.tile([P, S], U32, align_bytes=ALIGN, name=f"g_codes{c}") for c in range(PASSES)]
-        g_scales = [keep.tile([P, S], U8, align_bytes=ALIGN, name=f"g_scales{c}") for c in range(PASSES)]
+        g_codes = [keep.tile([P, PASSES * HALF], U32, align_bytes=ALIGN, name=f"g_codes{h}") for h in range(2)]
+        g_scales = [keep.tile([P, PASSES * HALF], U8, align_bytes=ALIGN, name=f"g_scales{h}") for h in range(2)]
         result = keep.tile([P, T], F32, align_bytes=ALIGN, name="result")
         slots = keep.tile([P, S], F32, align_bytes=ALIGN, name="slots")
 
@@ -101,11 +94,11 @@ def tile_moe_bdx_lin_none_kernel(tc, dyT, w, gate, offs, out):
             nc.vector.memset(zero[:], 0.0)
             nc.scalar.activation(identity[:], zero[:].to_broadcast([P, P]), COPY)
             make_identity(nc, identity[:], nomemset=True)
-            for h in (1, 0):
+            for h in range(2):
                 for j in range(PACK):
                     column = gate_cols[:, h, j : j + 1].to_broadcast([P, P])
                     nc.tensor.transpose(gates[h][:, j::PACK], column, identity[:])
-                nc.vector.tensor_copy(out=pool_gates[:, h], in_=gates[h][:, 0:POOL])
+                nc.vector.tensor_copy(out=pool_gates[h][:], in_=gates[h][:, 0 : pool_width[h]])
 
         def listed(s0, n):
             return offsets[:, s0 // LIST_ROWS : (s0 + n) // LIST_ROWS]
@@ -115,7 +108,7 @@ def tile_moe_bdx_lin_none_kernel(tc, dyT, w, gate, offs, out):
 
         def gather_on_scalar(c, h, rows):
             for t in rows:
-                window = long_window[c] if c > 0 and (h, t) == (0, LAST_ROW) else windows[c, t]
+                window = long_window[:] if (c, h, t) == (LAST, 0, LAST_ROW) else windows[c, t]
                 nc.scalar.activation(plane(c, h, t), window.indirect(listed(h * HALF, HALF)), COPY)
 
         def gather_on_vector(c, h, rows):
@@ -123,29 +116,28 @@ def tile_moe_bdx_lin_none_kernel(tc, dyT, w, gate, offs, out):
                 nc.vector.tensor_copy(plane(c, h, t), windows[c, t].indirect(listed(h * HALF, HALF)))
 
         def gate_and_mix(c, h):
+            share = POOL[c, h]
             dst = g_mixed[c, h].rearrange("p (s t) -> p s t", t=PACK)
             src = planes[c, h].rearrange("p (t s) -> p t s", t=PACK)
-            nc.gpsimd.tensor_tensor(
-                dst[:, 0:POOL],
-                src[:, :, 0:POOL].rearrange("p t s -> p s t"),
-                pool_gates[:, h].unsqueeze(2).to_broadcast([P, POOL, PACK]),
-                MULT,
-            )
-            by_slot = gates[h][:, POOL:HALF].rearrange("p (x r) -> p x r", r=RUN)
-            nc.vector.tensor_tensor(
-                dst[:, POOL:HALF].rearrange("p (x r) t -> p x t r", r=RUN),
-                src[:, :, POOL:HALF].rearrange("p t (x r) -> p x t r", r=RUN),
-                by_slot.unsqueeze(2).to_broadcast([P, (HALF - POOL) // RUN, PACK, RUN]),
-                MULT,
-            )
+            if share > 0:
+                nc.gpsimd.tensor_tensor(
+                    dst[:, 0:share],
+                    src[:, :, 0:share].rearrange("p t s -> p s t"),
+                    pool_gates[h][:, 0:share].unsqueeze(2).to_broadcast([P, share, PACK]),
+                    MULT,
+                )
+            if share < HALF:
+                by_slot = gates[h][:, share:HALF].rearrange("p (x r) -> p x r", r=RUN)
+                nc.vector.tensor_tensor(
+                    dst[:, share:HALF].rearrange("p (x r) t -> p x t r", r=RUN),
+                    src[:, :, share:HALF].rearrange("p t (x r) -> p x t r", r=RUN),
+                    by_slot.unsqueeze(2).to_broadcast([P, (HALF - share) // RUN, PACK, RUN]),
+                    MULT,
+                )
 
-        def quantise_g(src, c, s0, n):
-            nc.vector.quantize_mx(
-                out=g_codes[c][:, s0 : s0 + n].bitcast(FP8X4), scales=g_scales[c][:, s0 : s0 + n], in_=src
-            )
-
-        def quantise_half(c, h):
-            quantise_g(g_mixed[c, h], c, h * HALF, HALF)
+        def quantise_g(src, h, c0, n):
+            cols = slice(c0 * HALF, (c0 + n) * HALF)
+            nc.vector.quantize_mx(out=g_codes[h][:, cols].bitcast(FP8X4), scales=g_scales[h][:, cols], in_=src)
 
         def mix_on_vector(e, c0=0, n=PASSES):
             nc.vector.tensor_copy(
@@ -157,8 +149,8 @@ def tile_moe_bdx_lin_none_kernel(tc, dyT, w, gate, offs, out):
 
         def mix_on_scalar(e):
             nc.scalar.copy(
-                out=w_mixed[e].rearrange("p (c x r t) -> p c x t r", c=PASSES, r=RUN, t=PACK),
-                in_=w_raw[e][:].rearrange("p c (t x r) -> p c x t r", r=RUN, t=PACK),
+                out=w_mixed[e].rearrange("p (c x r t) -> p x c t r", c=PASSES, r=RUN, t=PACK),
+                in_=w_raw[e][:].rearrange("p c (t x r) -> p x c t r", r=RUN, t=PACK),
             )
 
         def quantise_w(e, c0=0, n=PASSES):
@@ -172,13 +164,15 @@ def tile_moe_bdx_lin_none_kernel(tc, dyT, w, gate, offs, out):
             e0, count = GROUPS[group]
             sums = psum.tile([P, count * C], F32, name=f"sums{group}")
             for e in range(e0, e0 + count):
+                h, s0 = divmod(e * C, HALF)
                 for c in range(PASSES):
+                    cols = slice(c * HALF + s0, c * HALF + s0 + C)
                     nc.tensor.matmul_mx(
                         out=sums[:, (e - e0) * C : (e - e0 + 1) * C],
                         lhsT=w_codes[e][:, c * K : (c + 1) * K].bitcast(FP8X4),
                         lhsT_scale=w_scales[e][:, c * K : (c + 1) * K],
-                        rhs=g_codes[c][:, e * C : (e + 1) * C].bitcast(FP8X4),
-                        rhs_scale=g_scales[c][:, e * C : (e + 1) * C],
+                        rhs=g_codes[h][:, cols].bitcast(FP8X4),
+                        rhs_scale=g_scales[h][:, cols],
                         start=(c == 0),
                         stop=(c == LAST),
                     )
@@ -189,53 +183,46 @@ def tile_moe_bdx_lin_none_kernel(tc, dyT, w, gate, offs, out):
         load_window(0, 0)
         nc.sync.dma_start(offsets[:], offs)
         nc.sync.dma_start(out=gate_cols[:], in_=gate[0, :].rearrange("(h p j) -> p h j", p=P, j=PACK))
-        for t in range(1, PACK):
-            load_window(0, t)
-        for t in range(PACK):
-            load_window(1, t)
-        load_expert(0)
-        load_expert(1)
-        for t in range(PACK):
-            load_window(LAST, t)
-        for e in range(2, E):
+        for c in range(PASSES):
+            for t in range(PACK):
+                if (c, t) != (0, 0):
+                    load_window(c, t)
+        for e in range(E):
             load_expert(e)
 
         spread_gates()
         gather_on_scalar(0, 0, range(PACK))
         gather_on_vector(0, 1, range(PACK))
-        gate_and_mix(0, 1)
-        gate_and_mix(0, 0)
-        quantise_g(both[:], 0, 0, S)
-
         gather_on_scalar(1, 0, range(PACK))
-        gather_on_scalar(1, 1, range(PACK))
+        gather_on_vector(1, 1, range(LAST_ROW))
+        gather_on_scalar(1, 1, [LAST_ROW])
+        gate_and_mix(0, 0)
+        gate_and_mix(0, 1)
         gate_and_mix(1, 0)
-        mix_on_vector(0)
-        quantise_half(1, 0)
-        mix_on_vector(1)
-        quantise_w(0)
         gate_and_mix(1, 1)
-        quantise_w(1)
-        quantise_half(1, 1)
+        quantise_g(early[1], 1, 0, LAST)
+        quantise_g(early[0], 0, 0, LAST)
 
         gather_on_scalar(LAST, 0, range(PACK))
-        gather_on_vector(LAST, 1, [LAST_ROW])
-        gather_on_scalar(LAST, 1, range(LAST_ROW))
-        mix_on_scalar(3)
+        gather_on_scalar(LAST, 1, range(PACK))
+        mix_on_scalar(2)
         gate_and_mix(LAST, 0)
-        mix_on_vector(2)
-        quantise_half(LAST, 0)
-        quantise_w(2)
+        mix_on_vector(0)
+        quantise_g(g_mixed[LAST, 0], 0, LAST, 1)
+        mix_on_vector(1)
+        quantise_w(0)
+        quantise_w(1)
         finish(0, nc.scalar.copy)
-        mix_on_vector(4)
         gate_and_mix(LAST, 1)
+        mix_on_vector(3)
+        quantise_g(g_mixed[LAST, 1], 1, LAST, 1)
+        quantise_w(2)
         quantise_w(3)
+        mix_on_scalar(4)
         finish(1, nc.scalar.copy)
-        quantise_half(LAST, 1)
-
         mix_on_vector(5)
-        quantise_w(4)
         quantise_w(5)
+        quantise_w(4)
         finish(2, nc.scalar.copy)
         mix_on_vector(6)
         mix_on_vector(E - 1, 0, LAST)

@@ -28,6 +28,8 @@ ALIGN = 256
 
 RUN = 4
 POOL = {(0, 0): HALF, (0, 1): 0, (1, 0): 256, (1, 1): 0, (2, 0): 128, (2, 1): 128}
+WINDOW_LOADS = ((0, 0, 1), (0, 1, 1), (0, 2, 1), (0, 3, 1), (1, 0, 1), (1, 1, 1), (1, 2, 1), (1, 3, 1), (2, 0, 2), (2, 2, 2))
+W_PITCH = PACK * K + 64
 GROUPS = ((0, 2), (2, 2), (4, 2), (6, 1), (7, 1))
 
 FLOPS = 2 * K * N * S
@@ -48,13 +50,14 @@ def tile_moe_bdx_lin_none_kernel(tc, dyT, w, gate, offs, out):
         pool_gates = [keep.tile([P, pool_width[h]], F32, align_bytes=ALIGN, name=f"pool_gates{h}") for h in range(2)]
         gates = [psum.tile([P, HALF], F32, name=f"gates{h}") for h in range(2)]
 
-        long_window = keep.tile([P, T + PLANES], F32, align_bytes=ALIGN, name="long_window")
-        windows, planes = {(LAST, LAST_ROW): long_window[:, 0:T]}, {}
-        for c in range(PASSES):
-            for t in range(PACK):
-                if (c, t) not in windows:
-                    win = keep.tile([P, T], F32, align_bytes=ALIGN, name=f"win{c}{t}")
-                    windows[c, t] = win[:]
+        windows, loads, planes = {}, [], {}
+        for c, t0, n in WINDOW_LOADS:
+            spare = PLANES if (c, t0 + n) == (LAST, PACK) else 0
+            rows = keep.tile([P, n * T + spare], F32, align_bytes=ALIGN, name=f"win{c}{t0}")
+            loads.append((rows[:, 0 : n * T], c, t0, n))
+            for t in range(n):
+                windows[c, t0 + t] = rows[:, t * T : (t + 1) * T]
+        long_window = rows[:, (n - 1) * T : n * T + PLANES]
         for c, h in ((0, 0), (0, 1), (1, 1), (LAST, 0)):
             own = keep.tile([P, PLANES], F32, align_bytes=ALIGN, name=f"planes{c}{h}")
             planes[c, h] = own[:]
@@ -71,7 +74,8 @@ def tile_moe_bdx_lin_none_kernel(tc, dyT, w, gate, offs, out):
         for e in range(4, E):
             w_mixed[e] = early[1][:, (e % 2) * W_COLS : (e % 2 + 1) * W_COLS]
 
-        w_raw = [keep.tile([P, PASSES, PACK * K], F32, align_bytes=ALIGN, name=f"w_raw{e}") for e in range(E)]
+        w_raw = [keep.tile([P, PASSES, W_PITCH], F32, align_bytes=ALIGN, name=f"w_raw{e}") for e in range(E)]
+        w_raw = [padded[:, :, 0 : PACK * K] for padded in w_raw]
         w_codes = [keep.tile([P, PASSES * K], U32, align_bytes=ALIGN, name=f"w_codes{e}") for e in range(E)]
         w_scales = [keep.tile([P, PASSES * K], U8, align_bytes=ALIGN, name=f"w_scales{e}") for e in range(E)]
         g_codes = [keep.tile([P, PASSES * HALF], U32, align_bytes=ALIGN, name=f"g_codes{h}") for h in range(2)]
@@ -79,14 +83,14 @@ def tile_moe_bdx_lin_none_kernel(tc, dyT, w, gate, offs, out):
         result = keep.tile([P, T], F32, align_bytes=ALIGN, name="result")
         slots = keep.tile([P, S], F32, align_bytes=ALIGN, name="slots")
 
-        dy_rows = dyT.rearrange("(c p t) x -> c p t x", p=P, t=PACK)
+        dy_rows = dyT.rearrange("(c p t) x -> c p (t x)", p=P, t=PACK)
         w_rows = w.rearrange("e (c p t) k -> e p c (t k)", p=P, t=PACK)
 
-        def load_window(c, t):
-            nc.sync.dma_start(out=windows[c, t], in_=dy_rows[c, :, t, :])
+        def load_windows(rows, c, t0, n):
+            nc.sync.dma_start(out=rows, in_=dy_rows[c, :, t0 * T : (t0 + n) * T])
 
         def load_expert(e):
-            parts = [(c, 1) for c in range(PASSES)] if e == E - 1 else [(0, LAST), (LAST, 1)]
+            parts = {E - 2: [(0, LAST), (LAST, 1)], E - 1: [(c, 1) for c in range(PASSES)]}.get(e, [(0, PASSES)])
             for c0, n in parts:
                 nc.sync.dma_start(out=w_raw[e][:, c0 : c0 + n], in_=w_rows[e, :, c0 : c0 + n])
 
@@ -108,7 +112,7 @@ def tile_moe_bdx_lin_none_kernel(tc, dyT, w, gate, offs, out):
 
         def gather_on_scalar(c, h, rows):
             for t in rows:
-                window = long_window[:] if (c, h, t) == (LAST, 0, LAST_ROW) else windows[c, t]
+                window = long_window if (c, h, t) == (LAST, 0, LAST_ROW) else windows[c, t]
                 nc.scalar.activation(plane(c, h, t), window.indirect(listed(h * HALF, HALF)), COPY)
 
         def gather_on_vector(c, h, rows):
@@ -150,7 +154,7 @@ def tile_moe_bdx_lin_none_kernel(tc, dyT, w, gate, offs, out):
         def mix_on_scalar(e):
             nc.scalar.copy(
                 out=w_mixed[e].rearrange("p (c x r t) -> p x c t r", c=PASSES, r=RUN, t=PACK),
-                in_=w_raw[e][:].rearrange("p c (t x r) -> p x c t r", r=RUN, t=PACK),
+                in_=w_raw[e].rearrange("p c (t x r) -> p x c t r", r=RUN, t=PACK),
             )
 
         def quantise_w(e, c0=0, n=PASSES):
@@ -180,13 +184,11 @@ def tile_moe_bdx_lin_none_kernel(tc, dyT, w, gate, offs, out):
             empty_bank(out=slots[:, cols], in_=sums[:])
             nc.scalar.activation(result[:].indirect(listed(e0 * C, count * C)), slots[:, cols], COPY)
 
-        load_window(0, 0)
+        load_windows(*loads[0])
         nc.sync.dma_start(offsets[:], offs)
         nc.sync.dma_start(out=gate_cols[:], in_=gate[0, :].rearrange("(h p j) -> p h j", p=P, j=PACK))
-        for c in range(PASSES):
-            for t in range(PACK):
-                if (c, t) != (0, 0):
-                    load_window(c, t)
+        for load in loads[1:]:
+            load_windows(*load)
         for e in range(E):
             load_expert(e)
 

@@ -10,6 +10,7 @@ U16 = mybir.dt.uint16
 U8 = mybir.dt.uint8
 FP8X4 = mybir.dt.float8_e4m3fn_x4
 MULT = mybir.AluOpType.mult
+ADD = mybir.AluOpType.add
 COPY = mybir.ActivationFunctionType.Copy
 
 K, T, E, C, N = 128, 1024, 8, 128, 1536
@@ -27,10 +28,11 @@ LIST_ROWS = 16
 ALIGN = 256
 
 RUN = 4
-POOL = {(0, 0): HALF, (0, 1): 0, (1, 0): 256, (1, 1): 0, (2, 0): 128, (2, 1): 128}
+POOL = {(0, 0): HALF, (0, 1): 0, (1, 0): 192, (1, 1): 0, (2, 0): 0, (2, 1): 0}
 WINDOW_LOADS = ((0, 0, 1), (0, 1, 1), (0, 2, 1), (0, 3, 1), (1, 0, 1), (1, 1, 1), (1, 2, 1), (1, 3, 1), (2, 0, 2), (2, 2, 2))
 W_PITCH = PACK * K + 64
-GROUPS = ((0, 2), (2, 2), (4, 2), (6, 1), (7, 1))
+WEIGHT_LOADS = (3, 3, 3, 3, 2, 4, 2, 1, 1, 1, 1)
+GROUPS = ((0, 2), (2, 2), (4, 1), (5, 1), (6, 1), (7, 1))
 
 FLOPS = 2 * K * N * S
 BYTES = 4 * (N * T + E * N * K + K * T + S) + 2 * S
@@ -46,8 +48,7 @@ def tile_moe_bdx_lin_none_kernel(tc, dyT, w, gate, offs, out):
         identity = keep.tile([P, P], F32, align_bytes=ALIGN, name="identity")
         zero = keep.tile([P, 1], F32, name="zero")
         gate_cols = keep.tile([P, 2, PACK], F32, align_bytes=ALIGN, name="gate_cols")
-        pool_width = [max(POOL[c, h] for c in range(PASSES)) for h in range(2)]
-        pool_gates = [keep.tile([P, pool_width[h]], F32, align_bytes=ALIGN, name=f"pool_gates{h}") for h in range(2)]
+        pool_gates = keep.tile([P, HALF], F32, align_bytes=ALIGN, name="pool_gates")
         gates = [psum.tile([P, HALF], F32, name=f"gates{h}") for h in range(2)]
 
         windows, loads, planes = {}, [], {}
@@ -67,32 +68,46 @@ def tile_moe_bdx_lin_none_kernel(tc, dyT, w, gate, offs, out):
         early = [mixed[:, 2 * h * PLANES : 2 * (h + 1) * PLANES] for h in range(2)]
         g_mixed = {(c, h): early[h][:, c * PLANES : (c + 1) * PLANES] for c in range(LAST) for h in range(2)}
         g_mixed[LAST, 0] = early[0][:, 0:PLANES]
-        g_mixed[LAST, 1] = early[1][:, 0:PLANES]
         w_mixed = {e: mixed[:, PLANES + e * W_COLS : PLANES + (e + 1) * W_COLS] for e in range(2)}
+        g_mixed[LAST, 1] = mixed[:, W_COLS : W_COLS + PLANES]
         w_mixed[2] = windows[LAST, LAST_ROW].bitcast(BF16)[:, 0:W_COLS]
-        w_mixed[3] = planes[LAST, 1].bitcast(BF16)[:, 0:W_COLS]
-        for e in range(4, E):
-            w_mixed[e] = early[1][:, (e % 2) * W_COLS : (e % 2 + 1) * W_COLS]
+        w_mixed[3] = mixed[:, 2 * PLANES : 2 * PLANES + W_COLS]
+        w_mixed[4] = mixed[:, PLANES - W_COLS : PLANES]
+        w_mixed[5] = w_mixed[0]
+        w_mixed[6] = w_mixed[3]
+        w_mixed[7] = w_mixed[2]
 
-        w_raw = [keep.tile([P, PASSES, W_PITCH], F32, align_bytes=ALIGN, name=f"w_raw{e}") for e in range(E)]
-        w_raw = [padded[:, :, 0 : PACK * K] for padded in w_raw]
-        w_codes = [keep.tile([P, PASSES * K], U32, align_bytes=ALIGN, name=f"w_codes{e}") for e in range(E)]
-        w_scales = [keep.tile([P, PASSES * K], U8, align_bytes=ALIGN, name=f"w_scales{e}") for e in range(E)]
-        g_codes = [keep.tile([P, PASSES * HALF], U32, align_bytes=ALIGN, name=f"g_codes{h}") for h in range(2)]
-        g_scales = [keep.tile([P, PASSES * HALF], U8, align_bytes=ALIGN, name=f"g_scales{h}") for h in range(2)]
+        padded = keep.tile([P, E * PASSES, W_PITCH], F32, align_bytes=ALIGN, name="w_raw")
+        w_raw = [padded[:, e * PASSES : (e + 1) * PASSES, 0 : PACK * K] for e in range(E)]
+
+        def packed(words, name):
+            codes = keep.tile([P, words], U32, align_bytes=ALIGN, name=f"codes_{name}")
+            scales = keep.tile([P, words], U8, align_bytes=ALIGN, name=f"scales_{name}")
+            return codes, scales
+
+        def part(pair, start, words):
+            return pair[0][:, start : start + words], pair[1][:, start : start + words]
+
+        early_q = [packed(LAST * HALF, f"early{h}") for h in range(2)]
+        joint_q = packed(HALF + 2 * PASSES * K, "joint")
+        last_q = packed(HALF, "last")
+        g_q = {(c, h): part(early_q[h], c * HALF, HALF) for c in range(LAST) for h in range(2)}
+        g_q[LAST, 0] = part(joint_q, 0, HALF)
+        g_q[LAST, 1] = part(last_q, 0, HALF)
+        w_q = {e: part(joint_q, HALF + e * PASSES * K, PASSES * K) for e in range(2)}
+        for e in range(2, E):
+            w_q[e] = part(packed(PASSES * K, f"w{e}"), 0, PASSES * K)
         result = keep.tile([P, T], F32, align_bytes=ALIGN, name="result")
         slots = keep.tile([P, S], F32, align_bytes=ALIGN, name="slots")
 
         dy_rows = dyT.rearrange("(c p t) x -> c p (t x)", p=P, t=PACK)
-        w_rows = w.rearrange("e (c p t) k -> e p c (t k)", p=P, t=PACK)
+        w_rows = w.rearrange("e (c p t) k -> p (e c) (t k)", p=P, t=PACK)
 
         def load_windows(rows, c, t0, n):
             nc.sync.dma_start(out=rows, in_=dy_rows[c, :, t0 * T : (t0 + n) * T])
 
-        def load_expert(e):
-            parts = {E - 2: [(0, LAST), (LAST, 1)], E - 1: [(c, 1) for c in range(PASSES)]}.get(e, [(0, PASSES)])
-            for c0, n in parts:
-                nc.sync.dma_start(out=w_raw[e][:, c0 : c0 + n], in_=w_rows[e, :, c0 : c0 + n])
+        def load_weights(row, n):
+            nc.sync.dma_start(out=padded[:, row : row + n, 0 : PACK * K], in_=w_rows[:, row : row + n])
 
         def spread_gates():
             nc.vector.memset(zero[:], 0.0)
@@ -102,7 +117,7 @@ def tile_moe_bdx_lin_none_kernel(tc, dyT, w, gate, offs, out):
                 for j in range(PACK):
                     column = gate_cols[:, h, j : j + 1].to_broadcast([P, P])
                     nc.tensor.transpose(gates[h][:, j::PACK], column, identity[:])
-                nc.vector.tensor_copy(out=pool_gates[h][:], in_=gates[h][:, 0 : pool_width[h]])
+            nc.vector.tensor_copy(out=pool_gates[:], in_=gates[0][:])
 
         def listed(s0, n):
             return offsets[:, s0 // LIST_ROWS : (s0 + n) // LIST_ROWS]
@@ -127,7 +142,7 @@ def tile_moe_bdx_lin_none_kernel(tc, dyT, w, gate, offs, out):
                 nc.gpsimd.tensor_tensor(
                     dst[:, 0:share],
                     src[:, :, 0:share].rearrange("p t s -> p s t"),
-                    pool_gates[h][:, 0:share].unsqueeze(2).to_broadcast([P, share, PACK]),
+                    pool_gates[:, 0:share].unsqueeze(2).to_broadcast([P, share, PACK]),
                     MULT,
                 )
             if share < HALF:
@@ -139,9 +154,8 @@ def tile_moe_bdx_lin_none_kernel(tc, dyT, w, gate, offs, out):
                     MULT,
                 )
 
-        def quantise_g(src, h, c0, n):
-            cols = slice(c0 * HALF, (c0 + n) * HALF)
-            nc.vector.quantize_mx(out=g_codes[h][:, cols].bitcast(FP8X4), scales=g_scales[h][:, cols], in_=src)
+        def quantise(src, pair):
+            nc.vector.quantize_mx(out=pair[0].bitcast(FP8X4), scales=pair[1], in_=src)
 
         def mix_on_vector(e, c0=0, n=PASSES):
             nc.vector.tensor_copy(
@@ -157,12 +171,18 @@ def tile_moe_bdx_lin_none_kernel(tc, dyT, w, gate, offs, out):
                 in_=w_raw[e].rearrange("p c (t x r) -> p x c t r", r=RUN, t=PACK),
             )
 
-        def quantise_w(e, c0=0, n=PASSES):
-            nc.vector.quantize_mx(
-                out=w_codes[e][:, c0 * K : (c0 + n) * K].bitcast(FP8X4),
-                scales=w_scales[e][:, c0 * K : (c0 + n) * K],
-                in_=w_mixed[e][:, c0 * K_PASS : (c0 + n) * K_PASS],
+        def mix_on_pool(e):
+            nc.gpsimd.tensor_scalar(
+                w_mixed[e].rearrange("p (c k t) -> p c k t", c=PASSES, t=PACK),
+                w_raw[e].rearrange("p c (t k) -> p c k t", t=PACK),
+                1.0,
+                0.0,
+                MULT,
+                ADD,
             )
+
+        def quantise_w(e, c0=0, n=PASSES):
+            quantise(w_mixed[e][:, c0 * K_PASS : (c0 + n) * K_PASS], part(w_q[e], c0 * K, n * K))
 
         def finish(group, empty_bank):
             e0, count = GROUPS[group]
@@ -170,13 +190,14 @@ def tile_moe_bdx_lin_none_kernel(tc, dyT, w, gate, offs, out):
             for e in range(e0, e0 + count):
                 h, s0 = divmod(e * C, HALF)
                 for c in range(PASSES):
-                    cols = slice(c * HALF + s0, c * HALF + s0 + C)
+                    w_codes, w_scales = part(w_q[e], c * K, K)
+                    g_codes, g_scales = part(g_q[c, h], s0, C)
                     nc.tensor.matmul_mx(
                         out=sums[:, (e - e0) * C : (e - e0 + 1) * C],
-                        lhsT=w_codes[e][:, c * K : (c + 1) * K].bitcast(FP8X4),
-                        lhsT_scale=w_scales[e][:, c * K : (c + 1) * K],
-                        rhs=g_codes[h][:, cols].bitcast(FP8X4),
-                        rhs_scale=g_scales[h][:, cols],
+                        lhsT=w_codes.bitcast(FP8X4),
+                        lhsT_scale=w_scales,
+                        rhs=g_codes.bitcast(FP8X4),
+                        rhs_scale=g_scales,
                         start=(c == 0),
                         stop=(c == LAST),
                     )
@@ -189,8 +210,10 @@ def tile_moe_bdx_lin_none_kernel(tc, dyT, w, gate, offs, out):
         nc.sync.dma_start(out=gate_cols[:], in_=gate[0, :].rearrange("(h p j) -> p h j", p=P, j=PACK))
         for load in loads[1:]:
             load_windows(*load)
-        for e in range(E):
-            load_expert(e)
+        row = 0
+        for n in WEIGHT_LOADS:
+            load_weights(row, n)
+            row += n
 
         spread_gates()
         gather_on_scalar(0, 0, range(PACK))
@@ -202,36 +225,37 @@ def tile_moe_bdx_lin_none_kernel(tc, dyT, w, gate, offs, out):
         gate_and_mix(0, 1)
         gate_and_mix(1, 0)
         gate_and_mix(1, 1)
-        quantise_g(early[1], 1, 0, LAST)
-        quantise_g(early[0], 0, 0, LAST)
+        for h in range(2):
+            quantise(early[h], part(early_q[h], 0, LAST * HALF))
 
         gather_on_scalar(LAST, 0, range(PACK))
         gather_on_scalar(LAST, 1, range(PACK))
         mix_on_scalar(2)
         gate_and_mix(LAST, 0)
-        mix_on_vector(0)
-        quantise_g(g_mixed[LAST, 0], 0, LAST, 1)
-        mix_on_vector(1)
-        quantise_w(0)
-        quantise_w(1)
+        mix_on_pool(0)
+        mix_on_vector(1, 0, 1)
+        mix_on_vector(1, 1, LAST)
+        quantise(mixed[:, 0 : 2 * PLANES], part(joint_q, 0, 2 * HALF))
+        quantise_w(1, 1, LAST)
         finish(0, nc.scalar.copy)
         gate_and_mix(LAST, 1)
-        mix_on_vector(3)
-        quantise_g(g_mixed[LAST, 1], 1, LAST, 1)
+        mix_on_pool(3)
         quantise_w(2)
+        quantise(g_mixed[LAST, 1], g_q[LAST, 1])
         quantise_w(3)
-        mix_on_scalar(4)
         finish(1, nc.scalar.copy)
+        mix_on_vector(4)
         mix_on_vector(5)
-        quantise_w(5)
         quantise_w(4)
         finish(2, nc.scalar.copy)
         mix_on_vector(6)
+        quantise_w(5)
+        finish(3, nc.scalar.copy)
         mix_on_vector(E - 1, 0, LAST)
         quantise_w(6)
-        finish(3, nc.scalar.copy)
+        finish(4, nc.scalar.copy)
         mix_on_vector(E - 1, LAST, 1)
         quantise_w(E - 1, 0, LAST)
         quantise_w(E - 1, LAST, 1)
-        finish(4, nc.vector.tensor_copy)
+        finish(5, nc.vector.tensor_copy)
         nc.sync.dma_start(out=out, in_=result[:])

@@ -28,11 +28,11 @@ LIST_ROWS = 16
 ALIGN = 256
 
 RUN = 4
-POOL = {(0, 0): HALF, (0, 1): 0, (1, 0): 192, (1, 1): 0, (2, 0): 0, (2, 1): 0}
+POOL = {(0, 0): HALF, (0, 1): 0, (1, 0): 224, (1, 1): 0, (2, 0): 0, (2, 1): 0}
 WINDOW_LOADS = ((0, 0, 1), (0, 1, 1), (0, 2, 1), (0, 3, 1), (1, 0, 1), (1, 1, 1), (1, 2, 1), (1, 3, 1), (2, 0, 2), (2, 2, 2))
 W_PITCH = PACK * K + 64
 WEIGHT_LOADS = (3, 3, 3, 3, 2, 4, 2, 1, 1, 1, 1)
-GROUPS = ((0, 2), (2, 2), (4, 1), (5, 1), (6, 1), (7, 1))
+GROUPS = ((0, 2), (2, 2), (4, 2), (6, 1), (7, 1))
 
 FLOPS = 2 * K * N * S
 BYTES = 4 * (N * T + E * N * K + K * T + S) + 2 * S
@@ -247,15 +247,14 @@ def tile_moe_bdx_lin_none_kernel(tc, dyT, w, gate, offs, out):
         mix_on_vector(4)
         mix_on_vector(5)
         quantise_w(4)
+        quantise_w(5)
         finish(2, nc.scalar.copy)
         mix_on_vector(6)
-        quantise_w(5)
-        finish(3, nc.scalar.copy)
         mix_on_vector(E - 1, 0, LAST)
         quantise_w(6)
-        finish(4, nc.scalar.copy)
+        finish(3, nc.scalar.copy)
         mix_on_vector(E - 1, LAST, 1)
         quantise_w(E - 1, 0, LAST)
         quantise_w(E - 1, LAST, 1)
-        finish(5, nc.vector.tensor_copy)
+        finish(4, nc.vector.tensor_copy)
         nc.sync.dma_start(out=out, in_=result[:])

@@ -30,6 +30,7 @@ ALIGN = 256
 RUN = 4
 POOL = {(0, 0): HALF, (0, 1): 0, (1, 0): 224, (1, 1): 0, (2, 0): 0, (2, 1): 0}
 WINDOW_LOADS = ((0, 0, 1), (0, 1, 1), (0, 2, 1), (0, 3, 1), (1, 0, 1), (1, 1, 1), (1, 2, 1), (1, 3, 1), (2, 0, 2), (2, 2, 2))
+PLANE_PITCH = HALF + 64
 W_PITCH = PACK * K + 64
 WEIGHT_LOADS = (3, 3, 3, 3, 2, 4, 2, 1, 1, 1, 1)
 GROUPS = ((0, 2), (2, 2), (4, 2), (6, 1), (7, 1))
@@ -60,9 +61,9 @@ def tile_moe_bdx_lin_none_kernel(tc, dyT, w, gate, offs, out):
                 windows[c, t0 + t] = rows[:, t * T : (t + 1) * T]
         long_window = rows[:, (n - 1) * T : n * T + PLANES]
         for c, h in ((0, 0), (0, 1), (1, 1), (LAST, 0)):
-            own = keep.tile([P, PLANES], F32, align_bytes=ALIGN, name=f"planes{c}{h}")
-            planes[c, h] = own[:]
-        planes[1, 0] = planes[LAST, 1] = long_window[:, T : T + PLANES]
+            own = keep.tile([P, PACK, PLANE_PITCH], F32, align_bytes=ALIGN, name=f"planes{c}{h}")
+            planes[c, h] = own[:, :, 0:HALF]
+        planes[1, 0] = planes[LAST, 1] = long_window[:, T : T + PLANES].rearrange("p (t s) -> p t s", t=PACK)
 
         mixed = keep.tile([P, 4 * PLANES], BF16, align_bytes=ALIGN, name="mixed")
         early = [mixed[:, 2 * h * PLANES : 2 * (h + 1) * PLANES] for h in range(2)]
@@ -123,7 +124,7 @@ def tile_moe_bdx_lin_none_kernel(tc, dyT, w, gate, offs, out):
             return offsets[:, s0 // LIST_ROWS : (s0 + n) // LIST_ROWS]
 
         def plane(c, h, t):
-            return planes[c, h][:, t * HALF : (t + 1) * HALF]
+            return planes[c, h][:, t]
 
         def gather_on_scalar(c, h, rows):
             for t in rows:
@@ -137,7 +138,7 @@ def tile_moe_bdx_lin_none_kernel(tc, dyT, w, gate, offs, out):
         def gate_and_mix(c, h):
             share = POOL[c, h]
             dst = g_mixed[c, h].rearrange("p (s t) -> p s t", t=PACK)
-            src = planes[c, h].rearrange("p (t s) -> p t s", t=PACK)
+            src = planes[c, h]
             if share > 0:
                 nc.gpsimd.tensor_tensor(
                     dst[:, 0:share],

@@ -28,12 +28,9 @@ LIST_ROWS = 16
 ALIGN = 256
 
 RUN = 4
-POOL = {(0, 0): HALF, (0, 1): 0, (1, 0): 224, (1, 1): 0, (2, 0): 0, (2, 1): 0}
-WINDOW_LOADS = ((0, 0, 1), (0, 1, 1), (0, 2, 1), (0, 3, 1), (1, 0, 1), (1, 1, 1), (1, 2, 1), (1, 3, 1), (2, 0, 2), (2, 2, 2))
-PLANE_PITCH = HALF + 64
 W_PITCH = PACK * K + 64
-WEIGHT_LOADS = (3, 3, 3, 3, 2, 4, 2, 1, 1, 1, 1)
-GROUPS = ((0, 2), (2, 2), (4, 2), (6, 1), (7, 1))
+LAST_PASS_ROWS = (3, 0, 1, 2)
+GROUPS = ((0, 2), (2, 2), (4, 1), (5, 1), (6, 1), (7, 1))
 
 FLOPS = 2 * K * N * S
 BYTES = 4 * (N * T + E * N * K + K * T + S) + 2 * S
@@ -43,40 +40,51 @@ def tile_moe_bdx_lin_none_kernel(tc, dyT, w, gate, offs, out):
     nc = tc.nc
     with ExitStack() as ctx:
         keep = ctx.enter_context(tc.tile_pool(name="keep", bufs=1))
+        head = ctx.enter_context(tc.tile_pool(name="head", bufs=1))
         psum = ctx.enter_context(tc.psum_pool(name="psum", bufs=1))
 
         offsets = keep.tile([P, S // LIST_ROWS], U16, name="offsets")
         identity = keep.tile([P, P], F32, align_bytes=ALIGN, name="identity")
         zero = keep.tile([P, 1], F32, name="zero")
         gate_cols = keep.tile([P, 2, PACK], F32, align_bytes=ALIGN, name="gate_cols")
-        pool_gates = keep.tile([P, HALF], F32, align_bytes=ALIGN, name="pool_gates")
         gates = [psum.tile([P, HALF], F32, name=f"gates{h}") for h in range(2)]
 
-        windows, loads, planes = {}, [], {}
-        for c, t0, n in WINDOW_LOADS:
-            spare = PLANES if (c, t0 + n) == (LAST, PACK) else 0
-            rows = keep.tile([P, n * T + spare], F32, align_bytes=ALIGN, name=f"win{c}{t0}")
-            loads.append((rows[:, 0 : n * T], c, t0, n))
-            for t in range(n):
-                windows[c, t0 + t] = rows[:, t * T : (t + 1) * T]
-        long_window = rows[:, (n - 1) * T : n * T + PLANES]
-        for c, h in ((0, 0), (0, 1), (1, 1), (LAST, 0)):
-            own = keep.tile([P, PACK, PLANE_PITCH], F32, align_bytes=ALIGN, name=f"planes{c}{h}")
-            planes[c, h] = own[:, :, 0:HALF]
-        planes[1, 0] = planes[LAST, 1] = long_window[:, T : T + PLANES].rearrange("p (t s) -> p t s", t=PACK)
+        windows = {}
+        final_row = LAST_PASS_ROWS[-1]
+        for c in range(PASSES):
+            for t in range(PACK):
+                spare = PLANES if (c, t) == (LAST, final_row) else 0
+                if c == 0 and t < 2:
+                    rows = head.tile([P, T], F32, align_bytes=ALIGN, offset=4 * T * t, name=f"win{c}{t}")
+                else:
+                    rows = keep.tile([P, T + spare], F32, align_bytes=ALIGN, name=f"win{c}{t}")
+                windows[c, t] = rows[:, 0:T]
+                if spare > 0:
+                    long_window = rows[:, 0 : T + LAST_ROW * HALF]
+                    behind = rows[:, T : T + PLANES].rearrange("p (t s) -> p t s", t=PACK)
+        planes = {(0, 0): behind, (LAST, 1): behind}
+        for c, h in ((0, 1), (1, 0), (1, 1), (LAST, 0)):
+            own = keep.tile([P, PACK, HALF], F32, align_bytes=ALIGN, name=f"planes{c}{h}")
+            planes[c, h] = own[:]
+        fused_gates = planes[1, 1].rearrange("p t s -> p (t s)")[:, 5 * HALF // 2 : 7 * HALF // 2]
 
-        mixed = keep.tile([P, 4 * PLANES], BF16, align_bytes=ALIGN, name="mixed")
-        early = [mixed[:, 2 * h * PLANES : 2 * (h + 1) * PLANES] for h in range(2)]
+        early = [
+            head.tile([P, 2 * PLANES], BF16, align_bytes=ALIGN, offset=0, name="early0"),
+            keep.tile([P, 2 * PLANES], BF16, align_bytes=ALIGN, name="early1"),
+        ]
         g_mixed = {(c, h): early[h][:, c * PLANES : (c + 1) * PLANES] for c in range(LAST) for h in range(2)}
-        g_mixed[LAST, 0] = early[0][:, 0:PLANES]
-        w_mixed = {e: mixed[:, PLANES + e * W_COLS : PLANES + (e + 1) * W_COLS] for e in range(2)}
-        g_mixed[LAST, 1] = mixed[:, W_COLS : W_COLS + PLANES]
-        w_mixed[2] = windows[LAST, LAST_ROW].bitcast(BF16)[:, 0:W_COLS]
-        w_mixed[3] = mixed[:, 2 * PLANES : 2 * PLANES + W_COLS]
-        w_mixed[4] = mixed[:, PLANES - W_COLS : PLANES]
-        w_mixed[5] = w_mixed[0]
-        w_mixed[6] = w_mixed[3]
-        w_mixed[7] = w_mixed[2]
+
+        def reused(values):
+            return values.rearrange("p t s -> p (t s)").bitcast(BF16)
+
+        last_mixed = keep.tile([P, PLANES], BF16, align_bytes=ALIGN, name="last_mixed")
+        g_mixed[LAST, 0] = g_mixed[LAST, 1] = last_mixed[:]
+        w_tiles = [keep.tile([P, W_COLS], BF16, align_bytes=ALIGN, name=f"w_mixed{i}") for i in range(2)]
+        w_mixed = {0: windows[0, LAST_ROW].bitcast(BF16)[:, 0:W_COLS]}
+        w_mixed[1] = w_mixed[3] = w_mixed[4] = w_tiles[0][:]
+        w_mixed[2] = w_mixed[7] = w_tiles[1][:]
+        w_mixed[5] = reused(behind)[:, 0:W_COLS]
+        w_mixed[6] = reused(behind)[:, W_COLS : 2 * W_COLS]
 
         padded = keep.tile([P, E * PASSES, W_PITCH], F32, align_bytes=ALIGN, name="w_raw")
         w_raw = [padded[:, e * PASSES : (e + 1) * PASSES, 0 : PACK * K] for e in range(E)]
@@ -84,76 +92,66 @@ def tile_moe_bdx_lin_none_kernel(tc, dyT, w, gate, offs, out):
         def packed(words, name):
             codes = keep.tile([P, words], U32, align_bytes=ALIGN, name=f"codes_{name}")
             scales = keep.tile([P, words], U8, align_bytes=ALIGN, name=f"scales_{name}")
-            return codes, scales
+            return codes[:], scales[:]
 
         def part(pair, start, words):
             return pair[0][:, start : start + words], pair[1][:, start : start + words]
 
         early_q = [packed(LAST * HALF, f"early{h}") for h in range(2)]
-        joint_q = packed(HALF + 2 * PASSES * K, "joint")
-        last_q = packed(HALF, "last")
         g_q = {(c, h): part(early_q[h], c * HALF, HALF) for c in range(LAST) for h in range(2)}
-        g_q[LAST, 0] = part(joint_q, 0, HALF)
-        g_q[LAST, 1] = part(last_q, 0, HALF)
-        w_q = {e: part(joint_q, HALF + e * PASSES * K, PASSES * K) for e in range(2)}
-        for e in range(2, E):
-            w_q[e] = part(packed(PASSES * K, f"w{e}"), 0, PASSES * K)
+        for h in range(2):
+            g_q[LAST, h] = packed(HALF, f"last{h}")
+        w_q = [packed(PASSES * K, f"w{e}") for e in range(E)]
         result = keep.tile([P, T], F32, align_bytes=ALIGN, name="result")
         slots = keep.tile([P, S], F32, align_bytes=ALIGN, name="slots")
 
-        dy_rows = dyT.rearrange("(c p t) x -> c p (t x)", p=P, t=PACK)
+        dy_rows = dyT.rearrange("(c p t) x -> c p t x", p=P, t=PACK)
         w_rows = w.rearrange("e (c p t) k -> p (e c) (t k)", p=P, t=PACK)
 
-        def load_windows(rows, c, t0, n):
-            nc.sync.dma_start(out=rows, in_=dy_rows[c, :, t0 * T : (t0 + n) * T])
+        def load_window(c, t):
+            nc.sync.dma_start(out=windows[c, t], in_=dy_rows[c, :, t])
 
         def load_weights(row, n):
             nc.sync.dma_start(out=padded[:, row : row + n, 0 : PACK * K], in_=w_rows[:, row : row + n])
 
-        def spread_gates():
-            nc.vector.memset(zero[:], 0.0)
-            nc.scalar.activation(identity[:], zero[:].to_broadcast([P, P]), COPY)
-            make_identity(nc, identity[:], nomemset=True)
-            for h in range(2):
-                for j in range(PACK):
-                    column = gate_cols[:, h, j : j + 1].to_broadcast([P, P])
-                    nc.tensor.transpose(gates[h][:, j::PACK], column, identity[:])
-            nc.vector.tensor_copy(out=pool_gates[:], in_=gates[0][:])
+        def spread_gates(h):
+            for j in range(PACK):
+                column = gate_cols[:, h, j : j + 1].to_broadcast([P, P])
+                nc.tensor.transpose(gates[h][:, j::PACK], column, identity[:])
 
         def listed(s0, n):
             return offsets[:, s0 // LIST_ROWS : (s0 + n) // LIST_ROWS]
 
-        def plane(c, h, t):
-            return planes[c, h][:, t]
+        def gather_on_scalar(c, h, t):
+            window = long_window if (c, h, t) == (LAST, 0, final_row) else windows[c, t]
+            nc.scalar.activation(planes[c, h][:, t], window.indirect(listed(h * HALF, HALF)), COPY)
 
-        def gather_on_scalar(c, h, rows):
-            for t in rows:
-                window = long_window if (c, h, t) == (LAST, 0, LAST_ROW) else windows[c, t]
-                nc.scalar.activation(plane(c, h, t), window.indirect(listed(h * HALF, HALF)), COPY)
+        def gather_on_vector(c, h, t):
+            nc.vector.tensor_copy(planes[c, h][:, t], windows[c, t].indirect(listed(h * HALF, HALF)))
 
-        def gather_on_vector(c, h, rows):
-            for t in rows:
-                nc.vector.tensor_copy(plane(c, h, t), windows[c, t].indirect(listed(h * HALF, HALF)))
+        def gather_gated(c, h, t):
+            nc.vector.tensor_tensor(
+                planes[c, h][:, t], windows[c, t].indirect(listed(h * HALF, HALF)), fused_gates, MULT
+            )
 
-        def gate_and_mix(c, h):
-            share = POOL[c, h]
-            dst = g_mixed[c, h].rearrange("p (s t) -> p s t", t=PACK)
-            src = planes[c, h]
-            if share > 0:
-                nc.gpsimd.tensor_tensor(
-                    dst[:, 0:share],
-                    src[:, :, 0:share].rearrange("p t s -> p s t"),
-                    pool_gates[:, 0:share].unsqueeze(2).to_broadcast([P, share, PACK]),
-                    MULT,
-                )
-            if share < HALF:
-                by_slot = gates[h][:, share:HALF].rearrange("p (x r) -> p x r", r=RUN)
-                nc.vector.tensor_tensor(
-                    dst[:, share:HALF].rearrange("p (x r) t -> p x t r", r=RUN),
-                    src[:, :, share:HALF].rearrange("p t (x r) -> p x t r", r=RUN),
-                    by_slot.unsqueeze(2).to_broadcast([P, (HALF - share) // RUN, PACK, RUN]),
-                    MULT,
-                )
+        def gate_and_mix(c, h, s0=0, n=HALF):
+            by_slot = gates[h][:, s0 : s0 + n].rearrange("p (x r) -> p x r", r=RUN)
+            nc.vector.tensor_tensor(
+                g_mixed[c, h][:, s0 * PACK : (s0 + n) * PACK].rearrange("p (x r t) -> p x t r", r=RUN, t=PACK),
+                planes[c, h][:, :, s0 : s0 + n].rearrange("p t (x r) -> p x t r", r=RUN),
+                by_slot.unsqueeze(2).to_broadcast([P, n // RUN, PACK, RUN]),
+                MULT,
+            )
+
+        def mix_gated_on_pool(c, h):
+            nc.gpsimd.tensor_scalar(
+                g_mixed[c, h].rearrange("p (s t) -> p s t", t=PACK),
+                planes[c, h].rearrange("p t s -> p s t"),
+                1.0,
+                0.0,
+                MULT,
+                ADD,
+            )
 
         def quantise(src, pair):
             nc.vector.quantize_mx(out=pair[0].bitcast(FP8X4), scales=pair[1], in_=src)
@@ -164,12 +162,6 @@ def tile_moe_bdx_lin_none_kernel(tc, dyT, w, gate, offs, out):
                     "p (c x r t) -> p x c t r", c=n, r=RUN, t=PACK
                 ),
                 in_=w_raw[e][:, c0 : c0 + n].rearrange("p c (t x r) -> p x c t r", r=RUN, t=PACK),
-            )
-
-        def mix_on_scalar(e):
-            nc.scalar.copy(
-                out=w_mixed[e].rearrange("p (c x r t) -> p x c t r", c=PASSES, r=RUN, t=PACK),
-                in_=w_raw[e].rearrange("p c (t x r) -> p x c t r", r=RUN, t=PACK),
             )
 
         def mix_on_pool(e):
@@ -206,56 +198,80 @@ def tile_moe_bdx_lin_none_kernel(tc, dyT, w, gate, offs, out):
             empty_bank(out=slots[:, cols], in_=sums[:])
             nc.scalar.activation(result[:].indirect(listed(e0 * C, count * C)), slots[:, cols], COPY)
 
-        load_windows(*loads[0])
-        nc.sync.dma_start(offsets[:], offs)
         nc.sync.dma_start(out=gate_cols[:], in_=gate[0, :].rearrange("(h p j) -> p h j", p=P, j=PACK))
-        for load in loads[1:]:
-            load_windows(*load)
-        row = 0
-        for n in WEIGHT_LOADS:
+        load_window(0, 0)
+        nc.sync.dma_start(offsets[:], offs)
+        for t in range(1, PACK):
+            load_window(0, t)
+        for t in range(PACK):
+            load_window(1, t)
+        load_weights(0, PASSES)
+        load_weights(PASSES, PASSES)
+        load_window(LAST, LAST_PASS_ROWS[0])
+        load_weights(2 * PASSES, PASSES)
+        for t in LAST_PASS_ROWS[1:]:
+            load_window(LAST, t)
+        row = 3 * PASSES
+        for n in (3, 3, 4, 3, 2):
             load_weights(row, n)
             row += n
 
-        spread_gates()
-        gather_on_scalar(0, 0, range(PACK))
-        gather_on_vector(0, 1, range(PACK))
-        gather_on_scalar(1, 0, range(PACK))
-        gather_on_vector(1, 1, range(LAST_ROW))
-        gather_on_scalar(1, 1, [LAST_ROW])
-        gate_and_mix(0, 0)
-        gate_and_mix(0, 1)
-        gate_and_mix(1, 0)
-        gate_and_mix(1, 1)
-        for h in range(2):
-            quantise(early[h], part(early_q[h], 0, LAST * HALF))
+        nc.vector.memset(zero[:], 0.0)
+        nc.scalar.activation(identity[:], zero[:].to_broadcast([P, P]), COPY)
+        make_identity(nc, identity[:], nomemset=True)
+        spread_gates(1)
+        nc.vector.tensor_copy(out=fused_gates, in_=gates[1][:])
+        spread_gates(0)
 
-        gather_on_scalar(LAST, 0, range(PACK))
-        gather_on_scalar(LAST, 1, range(PACK))
-        mix_on_scalar(2)
-        gate_and_mix(LAST, 0)
+        for t in range(PACK):
+            gather_on_scalar(0, 0, t)
+            gather_gated(0, 1, t)
+        gate_and_mix(0, 0, 0, HALF // 2)
+        mix_gated_on_pool(0, 1)
+        for t in range(2):
+            gather_on_scalar(1, 0, t)
+            gather_on_scalar(1, 1, t)
+        for t in range(2, PACK):
+            gather_on_vector(1, 1, t)
+            gather_on_scalar(1, 0, t)
+        gate_and_mix(0, 0, HALF // 2, HALF // 2)
+        gate_and_mix(1, 1)
+        gate_and_mix(1, 0)
         mix_on_pool(0)
-        mix_on_vector(1, 0, 1)
-        mix_on_vector(1, 1, LAST)
-        quantise(mixed[:, 0 : 2 * PLANES], part(joint_q, 0, 2 * HALF))
-        quantise_w(1, 1, LAST)
-        finish(0, nc.scalar.copy)
-        gate_and_mix(LAST, 1)
+        mix_on_pool(1)
+        mix_on_pool(2)
+        quantise(early[1][:], early_q[1])
+        quantise(early[0][:], early_q[0])
+        quantise_w(0)
+        quantise_w(1)
+
+        gather_on_scalar(LAST, 0, LAST_PASS_ROWS[0])
+        gather_on_scalar(LAST, 1, LAST_PASS_ROWS[0])
+        for h in range(2):
+            for t in LAST_PASS_ROWS[1:]:
+                gather_on_scalar(LAST, h, t)
+        gate_and_mix(LAST, 0)
         mix_on_pool(3)
         quantise_w(2)
-        quantise(g_mixed[LAST, 1], g_q[LAST, 1])
+        quantise(g_mixed[LAST, 0], g_q[LAST, 0])
+        finish(0, nc.scalar.copy)
         quantise_w(3)
         finish(1, nc.scalar.copy)
-        mix_on_vector(4)
-        mix_on_vector(5)
+        gate_and_mix(LAST, 1)
+        mix_on_pool(4)
         quantise_w(4)
-        quantise_w(5)
+        quantise(g_mixed[LAST, 1], g_q[LAST, 1])
         finish(2, nc.scalar.copy)
-        mix_on_vector(6)
-        mix_on_vector(E - 1, 0, LAST)
-        quantise_w(6)
+        mix_on_vector(5)
+        mix_on_vector(6, 0, 1)
+        quantise_w(5)
         finish(3, nc.scalar.copy)
-        mix_on_vector(E - 1, LAST, 1)
-        quantise_w(E - 1, 0, LAST)
-        quantise_w(E - 1, LAST, 1)
-        finish(4, nc.vector.tensor_copy)
+        mix_on_vector(6, 1, LAST)
+        mix_on_vector(7, 0, 1)
+        quantise_w(6)
+        finish(4, nc.scalar.copy)
+        mix_on_vector(7, 1, LAST)
+        quantise_w(7, 0, 1)
+        quantise_w(7, 1, LAST)
+        finish(5, nc.vector.tensor_copy)
         nc.sync.dma_start(out=out, in_=result[:])

@@ -30,7 +30,7 @@ ALIGN = 256
 RUN = 4
 W_PITCH = PACK * K + 64
 LAST_PASS_ROWS = (3, 0, 1, 2)
-GROUPS = ((0, 2), (2, 2), (4, 1), (5, 1), (6, 1), (7, 1))
+GROUPS = ((0, 3), (3, 2), (5, 1), (6, 1), (7, 1))
 
 FLOPS = 2 * K * N * S
 BYTES = 4 * (N * T + E * N * K + K * T + S) + 2 * S
@@ -77,12 +77,13 @@ def tile_moe_bdx_lin_none_kernel(tc, dyT, w, gate, offs, out):
         def reused(values):
             return values.rearrange("p t s -> p (t s)").bitcast(BF16)
 
-        last_mixed = keep.tile([P, PLANES], BF16, align_bytes=ALIGN, name="last_mixed")
-        g_mixed[LAST, 0] = g_mixed[LAST, 1] = last_mixed[:]
-        w_tiles = [keep.tile([P, W_COLS], BF16, align_bytes=ALIGN, name=f"w_mixed{i}") for i in range(2)]
+        last_mixed = [keep.tile([P, PLANES], BF16, align_bytes=ALIGN, name=f"last_mixed{h}") for h in range(2)]
+        for h in range(2):
+            g_mixed[LAST, h] = last_mixed[h][:]
         w_mixed = {0: windows[0, LAST_ROW].bitcast(BF16)[:, 0:W_COLS]}
-        w_mixed[1] = w_mixed[3] = w_mixed[4] = w_tiles[0][:]
-        w_mixed[2] = w_mixed[7] = w_tiles[1][:]
+        w_mixed[1] = w_mixed[2] = w_mixed[7] = last_mixed[1][:, 0:W_COLS]
+        w_mixed[3] = early[1][:, 0:W_COLS]
+        w_mixed[4] = last_mixed[0][:, 0:W_COLS]
         w_mixed[5] = reused(behind)[:, 0:W_COLS]
         w_mixed[6] = reused(behind)[:, W_COLS : 2 * W_COLS]
 
@@ -164,6 +165,12 @@ def tile_moe_bdx_lin_none_kernel(tc, dyT, w, gate, offs, out):
                 in_=w_raw[e][:, c0 : c0 + n].rearrange("p c (t x r) -> p x c t r", r=RUN, t=PACK),
             )
 
+        def mix_on_scalar(e):
+            nc.scalar.copy(
+                out=w_mixed[e].rearrange("p (c x r t) -> p x c t r", c=PASSES, r=RUN, t=PACK),
+                in_=w_raw[e].rearrange("p c (t x r) -> p x c t r", r=RUN, t=PACK),
+            )
+
         def mix_on_pool(e):
             nc.gpsimd.tensor_scalar(
                 w_mixed[e].rearrange("p (c k t) -> p c k t", c=PASSES, t=PACK),
@@ -177,7 +184,7 @@ def tile_moe_bdx_lin_none_kernel(tc, dyT, w, gate, offs, out):
         def quantise_w(e, c0=0, n=PASSES):
             quantise(w_mixed[e][:, c0 * K_PASS : (c0 + n) * K_PASS], part(w_q[e], c0 * K, n * K))
 
-        def finish(group, empty_bank):
+        def multiply(group):
             e0, count = GROUPS[group]
             sums = psum.tile([P, count * C], F32, name=f"sums{group}")
             for e in range(e0, e0 + count):
@@ -194,6 +201,10 @@ def tile_moe_bdx_lin_none_kernel(tc, dyT, w, gate, offs, out):
                         start=(c == 0),
                         stop=(c == LAST),
                     )
+            return sums
+
+        def put_back(group, sums, empty_bank):
+            e0, count = GROUPS[group]
             cols = slice(e0 * C, (e0 + count) * C)
             empty_bank(out=slots[:, cols], in_=sums[:])
             nc.scalar.activation(result[:].indirect(listed(e0 * C, count * C)), slots[:, cols], COPY)
@@ -206,13 +217,12 @@ def tile_moe_bdx_lin_none_kernel(tc, dyT, w, gate, offs, out):
         for t in range(PACK):
             load_window(1, t)
         load_weights(0, PASSES)
-        load_weights(PASSES, PASSES)
         load_window(LAST, LAST_PASS_ROWS[0])
-        load_weights(2 * PASSES, PASSES)
+        load_weights(PASSES, PASSES)
         for t in LAST_PASS_ROWS[1:]:
             load_window(LAST, t)
-        row = 3 * PASSES
-        for n in (3, 3, 4, 3, 2):
+        row = 2 * PASSES
+        for n in (3, 3, 3, 4, 3, 2):
             load_weights(row, n)
             row += n
 
@@ -239,7 +249,6 @@ def tile_moe_bdx_lin_none_kernel(tc, dyT, w, gate, offs, out):
         gate_and_mix(1, 0)
         mix_on_pool(0)
         mix_on_pool(1)
-        mix_on_pool(2)
         quantise(early[1][:], early_q[1])
         quantise(early[0][:], early_q[0])
         quantise_w(0)
@@ -250,28 +259,30 @@ def tile_moe_bdx_lin_none_kernel(tc, dyT, w, gate, offs, out):
         for h in range(2):
             for t in LAST_PASS_ROWS[1:]:
                 gather_on_scalar(LAST, h, t)
+        mix_on_scalar(3)
         gate_and_mix(LAST, 0)
-        mix_on_pool(3)
+        mix_on_pool(2)
         quantise_w(2)
         quantise(g_mixed[LAST, 0], g_q[LAST, 0])
-        finish(0, nc.scalar.copy)
-        quantise_w(3)
-        finish(1, nc.scalar.copy)
+        put_back(0, multiply(0), nc.scalar.copy)
         gate_and_mix(LAST, 1)
         mix_on_pool(4)
-        quantise_w(4)
+        quantise_w(3)
         quantise(g_mixed[LAST, 1], g_q[LAST, 1])
-        finish(2, nc.scalar.copy)
+        quantise_w(4)
+        put_back(1, multiply(1), nc.scalar.copy)
         mix_on_vector(5)
         mix_on_vector(6, 0, 1)
         quantise_w(5)
-        finish(3, nc.scalar.copy)
+        sums = multiply(2)
         mix_on_vector(6, 1, LAST)
         mix_on_vector(7, 0, 1)
+        put_back(2, sums, nc.vector.tensor_copy)
         quantise_w(6)
-        finish(4, nc.scalar.copy)
+        sums = multiply(3)
         mix_on_vector(7, 1, LAST)
         quantise_w(7, 0, 1)
+        put_back(3, sums, nc.vector.tensor_copy)
         quantise_w(7, 1, LAST)
-        finish(5, nc.vector.tensor_copy)
+        put_back(4, multiply(4), nc.vector.tensor_copy)
         nc.sync.dma_start(out=out, in_=result[:])

@@ -54,8 +54,8 @@ def tile_moe_bdx_lin_none_kernel(tc, dyT, w, gate, offs, out):
         for c in range(PASSES):
             for t in range(PACK):
                 spare = PLANES if (c, t) == (LAST, final_row) else 0
-                if c == 0 and t < 2:
-                    rows = head.tile([P, T], F32, align_bytes=ALIGN, offset=4 * T * t, name=f"win{c}{t}")
+                if (c, t) == (0, LAST_ROW):
+                    rows = head.tile([P, T], F32, align_bytes=ALIGN, offset=0, name=f"win{c}{t}")
                 else:
                     rows = keep.tile([P, T + spare], F32, align_bytes=ALIGN, name=f"win{c}{t}")
                 windows[c, t] = rows[:, 0:T]
@@ -66,24 +66,23 @@ def tile_moe_bdx_lin_none_kernel(tc, dyT, w, gate, offs, out):
         for c, h in ((0, 1), (1, 0), (1, 1), (LAST, 0)):
             own = keep.tile([P, PACK, HALF], F32, align_bytes=ALIGN, name=f"planes{c}{h}")
             planes[c, h] = own[:]
-        fused_gates = planes[1, 1].rearrange("p t s -> p (t s)")[:, 5 * HALF // 2 : 7 * HALF // 2]
+        pool_gates = keep.tile([P, HALF], F32, align_bytes=ALIGN, name="pool_gates")
 
-        early = [
-            head.tile([P, 2 * PLANES], BF16, align_bytes=ALIGN, offset=0, name="early0"),
-            keep.tile([P, 2 * PLANES], BF16, align_bytes=ALIGN, name="early1"),
-        ]
+        early = [keep.tile([P, 2 * PLANES], BF16, align_bytes=ALIGN, name=f"early{h}") for h in range(2)]
         g_mixed = {(c, h): early[h][:, c * PLANES : (c + 1) * PLANES] for c in range(LAST) for h in range(2)}
 
         def reused(values):
             return values.rearrange("p t s -> p (t s)").bitcast(BF16)
 
-        last_mixed = [keep.tile([P, PLANES], BF16, align_bytes=ALIGN, name=f"last_mixed{h}") for h in range(2)]
-        for h in range(2):
-            g_mixed[LAST, h] = last_mixed[h][:]
-        w_mixed = {0: windows[0, LAST_ROW].bitcast(BF16)[:, 0:W_COLS]}
-        w_mixed[1] = w_mixed[2] = w_mixed[7] = last_mixed[1][:, 0:W_COLS]
+        late = keep.tile([P, PLANES + W_COLS], BF16, align_bytes=ALIGN, name="late")
+        over_window = head.tile([P, W_COLS], BF16, align_bytes=ALIGN, offset=0, name="w_mixed2")
+        own_w = keep.tile([P, W_COLS], BF16, align_bytes=ALIGN, name="w_mixed1")
+        g_mixed[LAST, 0] = late[:, PLANES // 2 : PLANES // 2 + PLANES]
+        g_mixed[LAST, 1] = late[:, 0:PLANES]
+        w_mixed = {0: windows[0, LAST_ROW].bitcast(BF16)[:, 0:W_COLS], 1: own_w[:], 2: over_window[:]}
         w_mixed[3] = early[1][:, 0:W_COLS]
-        w_mixed[4] = last_mixed[0][:, 0:W_COLS]
+        w_mixed[4] = late[:, PLANES : PLANES + W_COLS]
+        w_mixed[7] = late[:, 0:W_COLS]
         w_mixed[5] = reused(behind)[:, 0:W_COLS]
         w_mixed[6] = reused(behind)[:, W_COLS : 2 * W_COLS]
 
@@ -130,11 +129,6 @@ def tile_moe_bdx_lin_none_kernel(tc, dyT, w, gate, offs, out):
         def gather_on_vector(c, h, t):
             nc.vector.tensor_copy(planes[c, h][:, t], windows[c, t].indirect(listed(h * HALF, HALF)))
 
-        def gather_gated(c, h, t):
-            nc.vector.tensor_tensor(
-                planes[c, h][:, t], windows[c, t].indirect(listed(h * HALF, HALF)), fused_gates, MULT
-            )
-
         def gate_and_mix(c, h, s0=0, n=HALF):
             by_slot = gates[h][:, s0 : s0 + n].rearrange("p (x r) -> p x r", r=RUN)
             nc.vector.tensor_tensor(
@@ -144,14 +138,12 @@ def tile_moe_bdx_lin_none_kernel(tc, dyT, w, gate, offs, out):
                 MULT,
             )
 
-        def mix_gated_on_pool(c, h):
-            nc.gpsimd.tensor_scalar(
+        def gate_on_pool(c, h):
+            nc.gpsimd.tensor_tensor(
                 g_mixed[c, h].rearrange("p (s t) -> p s t", t=PACK),
                 planes[c, h].rearrange("p t s -> p s t"),
-                1.0,
-                0.0,
+                pool_gates[:].unsqueeze(2).to_broadcast([P, HALF, PACK]),
                 MULT,
-                ADD,
             )
 
         def quantise(src, pair):
@@ -209,9 +201,9 @@ def tile_moe_bdx_lin_none_kernel(tc, dyT, w, gate, offs, out):
             empty_bank(out=slots[:, cols], in_=sums[:])
             nc.scalar.activation(result[:].indirect(listed(e0 * C, count * C)), slots[:, cols], COPY)
 
-        nc.sync.dma_start(out=gate_cols[:], in_=gate[0, :].rearrange("(h p j) -> p h j", p=P, j=PACK))
         load_window(0, 0)
         nc.sync.dma_start(offsets[:], offs)
+        nc.sync.dma_start(out=gate_cols[:], in_=gate[0, :].rearrange("(h p j) -> p h j", p=P, j=PACK))
         for t in range(1, PACK):
             load_window(0, t)
         for t in range(PACK):
@@ -229,22 +221,21 @@ def tile_moe_bdx_lin_none_kernel(tc, dyT, w, gate, offs, out):
         nc.vector.memset(zero[:], 0.0)
         nc.scalar.activation(identity[:], zero[:].to_broadcast([P, P]), COPY)
         make_identity(nc, identity[:], nomemset=True)
-        spread_gates(1)
-        nc.vector.tensor_copy(out=fused_gates, in_=gates[1][:])
-        spread_gates(0)
+        for h in range(2):
+            spread_gates(h)
 
         for t in range(PACK):
             gather_on_scalar(0, 0, t)
-            gather_gated(0, 1, t)
-        gate_and_mix(0, 0, 0, HALF // 2)
-        mix_gated_on_pool(0, 1)
-        for t in range(2):
-            gather_on_scalar(1, 0, t)
-            gather_on_scalar(1, 1, t)
-        for t in range(2, PACK):
+            gather_on_vector(0, 1, t)
+        nc.vector.tensor_copy(out=pool_gates[:], in_=gates[0][:])
+        gate_on_pool(0, 0)
+        gate_and_mix(0, 1, 0, HALF // 2)
+        gather_on_scalar(1, 0, 0)
+        gather_on_scalar(1, 1, 0)
+        for t in range(1, PACK):
             gather_on_vector(1, 1, t)
             gather_on_scalar(1, 0, t)
-        gate_and_mix(0, 0, HALF // 2, HALF // 2)
+        gate_and_mix(0, 1, HALF // 2, HALF // 2)
         gate_and_mix(1, 1)
         gate_and_mix(1, 0)
         mix_on_pool(0)
@@ -262,8 +253,8 @@ def tile_moe_bdx_lin_none_kernel(tc, dyT, w, gate, offs, out):
         mix_on_scalar(3)
         gate_and_mix(LAST, 0)
         mix_on_pool(2)
-        quantise_w(2)
         quantise(g_mixed[LAST, 0], g_q[LAST, 0])
+        quantise_w(2)
         put_back(0, multiply(0), nc.scalar.copy)
         gate_and_mix(LAST, 1)
         mix_on_pool(4)
@@ -277,12 +268,12 @@ def tile_moe_bdx_lin_none_kernel(tc, dyT, w, gate, offs, out):
         sums = multiply(2)
         mix_on_vector(6, 1, LAST)
         mix_on_vector(7, 0, 1)
-        put_back(2, sums, nc.vector.tensor_copy)
+        put_back(2, sums, nc.scalar.copy)
         quantise_w(6)
         sums = multiply(3)
         mix_on_vector(7, 1, LAST)
         quantise_w(7, 0, 1)
-        put_back(3, sums, nc.vector.tensor_copy)
+        put_back(3, sums, nc.scalar.copy)
         quantise_w(7, 1, LAST)
         put_back(4, multiply(4), nc.vector.tensor_copy)
         nc.sync.dma_start(out=out, in_=result[:])

@@ -28,6 +28,7 @@ LIST_ROWS = 16
 ALIGN = 256
 
 RUN = 4
+SPLIT = 256
 W_PITCH = PACK * K + 64
 LAST_PASS_ROWS = (3, 0, 1, 2)
 GROUPS = ((0, 3), (3, 2), (5, 1), (6, 1), (7, 1))
@@ -122,12 +123,12 @@ def tile_moe_bdx_lin_none_kernel(tc, dyT, w, gate, offs, out):
         def listed(s0, n):
             return offsets[:, s0 // LIST_ROWS : (s0 + n) // LIST_ROWS]
 
-        def gather_on_scalar(c, h, t):
+        def gather_on_scalar(c, h, t, n=HALF):
             window = long_window if (c, h, t) == (LAST, 0, final_row) else windows[c, t]
-            nc.scalar.activation(planes[c, h][:, t], window.indirect(listed(h * HALF, HALF)), COPY)
+            nc.scalar.activation(planes[c, h][:, t, 0:n], window.indirect(listed(h * HALF, n)), COPY)
 
-        def gather_on_vector(c, h, t):
-            nc.vector.tensor_copy(planes[c, h][:, t], windows[c, t].indirect(listed(h * HALF, HALF)))
+        def gather_on_vector(c, h, t, s0=0):
+            nc.vector.tensor_copy(planes[c, h][:, t, s0:HALF], windows[c, t].indirect(listed(h * HALF + s0, HALF - s0)))
 
         def gate_and_mix(c, h, s0=0, n=HALF):
             by_slot = gates[h][:, s0 : s0 + n].rearrange("p (x r) -> p x r", r=RUN)
@@ -232,7 +233,10 @@ def tile_moe_bdx_lin_none_kernel(tc, dyT, w, gate, offs, out):
         gate_and_mix(0, 1, 0, HALF // 2)
         gather_on_scalar(1, 0, 0)
         gather_on_scalar(1, 1, 0)
-        for t in range(1, PACK):
+        gather_on_scalar(1, 0, 1)
+        gather_on_scalar(1, 1, 1, SPLIT)
+        gather_on_vector(1, 1, 1, SPLIT)
+        for t in range(2, PACK):
             gather_on_vector(1, 1, t)
             gather_on_scalar(1, 0, t)
         gate_and_mix(0, 1, HALF // 2, HALF // 2)

@@ -41,7 +41,7 @@ def tile_moe_bdx_lin_none_kernel(tc, dyT, w, gate, offs, out):
     nc = tc.nc
     with ExitStack() as ctx:
         keep = ctx.enter_context(tc.tile_pool(name="keep", bufs=1))
-        head = ctx.enter_context(tc.tile_pool(name="head", bufs=1))
+        tail = ctx.enter_context(tc.tile_pool(name="tail", bufs=1))
         psum = ctx.enter_context(tc.psum_pool(name="psum", bufs=1))
 
         offsets = keep.tile([P, S // LIST_ROWS], U16, name="offsets")
@@ -55,8 +55,8 @@ def tile_moe_bdx_lin_none_kernel(tc, dyT, w, gate, offs, out):
         for c in range(PASSES):
             for t in range(PACK):
                 spare = PLANES if (c, t) == (LAST, final_row) else 0
-                if (c, t) == (0, LAST_ROW):
-                    rows = head.tile([P, T], F32, align_bytes=ALIGN, offset=0, name=f"win{c}{t}")
+                if (c, t) == (LAST, 0):
+                    rows = tail.tile([P, T], F32, align_bytes=ALIGN, offset=0, name=f"win{c}{t}")
                 else:
                     rows = keep.tile([P, T + spare], F32, align_bytes=ALIGN, name=f"win{c}{t}")
                 windows[c, t] = rows[:, 0:T]
@@ -69,19 +69,22 @@ def tile_moe_bdx_lin_none_kernel(tc, dyT, w, gate, offs, out):
             planes[c, h] = own[:]
         pool_gates = keep.tile([P, HALF], F32, align_bytes=ALIGN, name="pool_gates")
 
-        early = [keep.tile([P, 2 * PLANES], BF16, align_bytes=ALIGN, name=f"early{h}") for h in range(2)]
-        g_mixed = {(c, h): early[h][:, c * PLANES : (c + 1) * PLANES] for c in range(LAST) for h in range(2)}
+        early = keep.tile([P, 2 * PLANES], BF16, align_bytes=ALIGN, name="early")
+        joint = keep.tile([P, PLANES + 2 * W_COLS], BF16, align_bytes=ALIGN, name="joint")
+        own = keep.tile([P, PLANES], BF16, align_bytes=ALIGN, name="mixed11")
+        g_mixed = {(c, 0): early[:, c * PLANES : (c + 1) * PLANES] for c in range(LAST)}
+        g_mixed[0, 1] = joint[:, 0:PLANES]
+        g_mixed[1, 1] = own[:]
 
         def reused(values):
             return values.rearrange("p t s -> p (t s)").bitcast(BF16)
 
         late = keep.tile([P, PLANES + W_COLS], BF16, align_bytes=ALIGN, name="late")
-        over_window = head.tile([P, W_COLS], BF16, align_bytes=ALIGN, offset=0, name="w_mixed2")
-        own_w = keep.tile([P, W_COLS], BF16, align_bytes=ALIGN, name="w_mixed1")
         g_mixed[LAST, 0] = late[:, PLANES // 2 : PLANES // 2 + PLANES]
         g_mixed[LAST, 1] = late[:, 0:PLANES]
-        w_mixed = {0: windows[0, LAST_ROW].bitcast(BF16)[:, 0:W_COLS], 1: own_w[:], 2: over_window[:]}
-        w_mixed[3] = early[1][:, 0:W_COLS]
+        w_mixed = {e: joint[:, PLANES + e * W_COLS : PLANES + (e + 1) * W_COLS] for e in range(2)}
+        w_mixed[2] = early[:, 0:W_COLS]
+        w_mixed[3] = joint[:, 0:W_COLS]
         w_mixed[4] = late[:, PLANES : PLANES + W_COLS]
         w_mixed[7] = late[:, 0:W_COLS]
         w_mixed[5] = reused(behind)[:, 0:W_COLS]
@@ -90,19 +93,26 @@ def tile_moe_bdx_lin_none_kernel(tc, dyT, w, gate, offs, out):
         padded = keep.tile([P, E * PASSES, W_PITCH], F32, align_bytes=ALIGN, name="w_raw")
         w_raw = [padded[:, e * PASSES : (e + 1) * PASSES, 0 : PACK * K] for e in range(E)]
 
-        def packed(words, name):
-            codes = keep.tile([P, words], U32, align_bytes=ALIGN, name=f"codes_{name}")
+        def packed(words, name, pool=keep, offset=None):
+            codes = pool.tile([P, words], U32, align_bytes=ALIGN, offset=offset, name=f"codes_{name}")
             scales = keep.tile([P, words], U8, align_bytes=ALIGN, name=f"scales_{name}")
             return codes[:], scales[:]
 
         def part(pair, start, words):
             return pair[0][:, start : start + words], pair[1][:, start : start + words]
 
-        early_q = [packed(LAST * HALF, f"early{h}") for h in range(2)]
-        g_q = {(c, h): part(early_q[h], c * HALF, HALF) for c in range(LAST) for h in range(2)}
+        early_q = packed(LAST * HALF, "early")
+        g_q = {(c, 0): part(early_q, c * HALF, HALF) for c in range(LAST)}
+        joint_q = packed(HALF + 2 * PASSES * K, "joint")
+        g_q[0, 1] = part(joint_q, 0, HALF)
+        g_q[1, 1] = packed(HALF, "g11", tail, 0)
         for h in range(2):
             g_q[LAST, h] = packed(HALF, f"last{h}")
-        w_q = [packed(PASSES * K, f"w{e}") for e in range(E)]
+        w_q = {e: part(joint_q, HALF + e * PASSES * K, PASSES * K) for e in range(2)}
+        for e in range(3, E):
+            w_q[e] = packed(PASSES * K, f"w{e}")
+        w_q[2] = packed(PASSES * K, "w2", tail, 4 * T)
+        filler = tail.tile([P, K_PASS], BF16, align_bytes=ALIGN, offset=4 * T, name="last_pass3")
         result = keep.tile([P, T], F32, align_bytes=ALIGN, name="result")
         slots = keep.tile([P, S], F32, align_bytes=ALIGN, name="slots")
 
@@ -158,10 +168,10 @@ def tile_moe_bdx_lin_none_kernel(tc, dyT, w, gate, offs, out):
                 in_=w_raw[e][:, c0 : c0 + n].rearrange("p c (t x r) -> p x c t r", r=RUN, t=PACK),
             )
 
-        def mix_on_scalar(e):
+        def mix_on_scalar(dst, e, c0, n):
             nc.scalar.copy(
-                out=w_mixed[e].rearrange("p (c x r t) -> p x c t r", c=PASSES, r=RUN, t=PACK),
-                in_=w_raw[e].rearrange("p c (t x r) -> p x c t r", r=RUN, t=PACK),
+                out=dst.rearrange("p (c x r t) -> p x c t r", c=n, r=RUN, t=PACK),
+                in_=w_raw[e][:, c0 : c0 + n].rearrange("p c (t x r) -> p x c t r", r=RUN, t=PACK),
             )
 
         def mix_on_pool(e):
@@ -196,11 +206,18 @@ def tile_moe_bdx_lin_none_kernel(tc, dyT, w, gate, offs, out):
                     )
             return sums
 
-        def put_back(group, sums, empty_bank):
+        def empty_bank(group, sums, copy):
+            e0, count = GROUPS[group]
+            copy(out=slots[:, e0 * C : (e0 + count) * C], in_=sums[:])
+
+        def scatter(group):
             e0, count = GROUPS[group]
             cols = slice(e0 * C, (e0 + count) * C)
-            empty_bank(out=slots[:, cols], in_=sums[:])
             nc.scalar.activation(result[:].indirect(listed(e0 * C, count * C)), slots[:, cols], COPY)
+
+        def put_back(group, sums, copy):
+            empty_bank(group, sums, copy)
+            scatter(group)
 
         load_window(0, 0)
         nc.sync.dma_start(offsets[:], offs)
@@ -230,39 +247,41 @@ def tile_moe_bdx_lin_none_kernel(tc, dyT, w, gate, offs, out):
             gather_on_vector(0, 1, t)
         nc.vector.tensor_copy(out=pool_gates[:], in_=gates[0][:])
         gate_on_pool(0, 0)
-        gate_and_mix(0, 1, 0, HALF // 2)
-        gather_on_scalar(1, 0, 0)
-        gather_on_scalar(1, 1, 0)
-        gather_on_scalar(1, 0, 1)
-        gather_on_scalar(1, 1, 1, SPLIT)
-        gather_on_vector(1, 1, 1, SPLIT)
-        for t in range(2, PACK):
-            gather_on_vector(1, 1, t)
+        gate_and_mix(0, 1)
+        for t in range(2):
             gather_on_scalar(1, 0, t)
-        gate_and_mix(0, 1, HALF // 2, HALF // 2)
-        gate_and_mix(1, 1)
+            gather_on_vector(1, 1, t)
+        gather_on_scalar(1, 0, 2)
+        gather_on_scalar(1, 1, 2, SPLIT)
+        gather_on_vector(1, 1, 2, SPLIT)
+        gather_on_scalar(1, 0, LAST_ROW)
+        gather_on_scalar(1, 1, LAST_ROW)
         gate_and_mix(1, 0)
+        gate_and_mix(1, 1)
         mix_on_pool(0)
         mix_on_pool(1)
-        quantise(early[1][:], early_q[1])
-        quantise(early[0][:], early_q[0])
-        quantise_w(0)
-        quantise_w(1)
+        quantise(joint[:, 0 : 2 * PLANES], part(joint_q, 0, 2 * HALF))
+        quantise(early[:], early_q)
+        quantise_w(1, 1, LAST)
 
         gather_on_scalar(LAST, 0, LAST_PASS_ROWS[0])
         gather_on_scalar(LAST, 1, LAST_PASS_ROWS[0])
         for h in range(2):
             for t in LAST_PASS_ROWS[1:]:
                 gather_on_scalar(LAST, h, t)
-        mix_on_scalar(3)
         gate_and_mix(LAST, 0)
         mix_on_pool(2)
+        quantise(g_mixed[1, 1], g_q[1, 1])
         quantise(g_mixed[LAST, 0], g_q[LAST, 0])
         quantise_w(2)
-        put_back(0, multiply(0), nc.scalar.copy)
+        mix_on_scalar(w_mixed[3][:, 0 : LAST * K_PASS], 3, 0, LAST)
+        empty_bank(0, multiply(0), nc.scalar.copy)
+        mix_on_scalar(filler[:], 3, LAST, 1)
+        scatter(0)
         gate_and_mix(LAST, 1)
         mix_on_pool(4)
-        quantise_w(3)
+        quantise_w(3, 0, LAST)
+        quantise(filler[:], part(w_q[3], LAST * K, K))
         quantise(g_mixed[LAST, 1], g_q[LAST, 1])
         quantise_w(4)
         put_back(1, multiply(1), nc.scalar.copy)

@@ -28,7 +28,7 @@ LIST_ROWS = 16
 ALIGN = 256
 
 RUN = 4
-SPLIT = 256
+SPLIT = 128
 W_PITCH = PACK * K + 64
 LAST_PASS_ROWS = (3, 0, 1, 2)
 GROUPS = ((0, 3), (3, 2), (5, 1), (6, 1), (7, 1))

@@ -28,7 +28,6 @@ LIST_ROWS = 16
 ALIGN = 256
 
 RUN = 4
-SPLIT = 128
 W_PITCH = PACK * K + 64
 LAST_PASS_ROWS = (3, 0, 1, 2)
 GROUPS = ((0, 3), (3, 2), (5, 1), (6, 1), (7, 1))
@@ -248,12 +247,9 @@ def tile_moe_bdx_lin_none_kernel(tc, dyT, w, gate, offs, out):
         nc.vector.tensor_copy(out=pool_gates[:], in_=gates[0][:])
         gate_on_pool(0, 0)
         gate_and_mix(0, 1)
-        for t in range(2):
+        for t in range(LAST_ROW):
             gather_on_scalar(1, 0, t)
             gather_on_vector(1, 1, t)
-        gather_on_scalar(1, 0, 2)
-        gather_on_scalar(1, 1, 2, SPLIT)
-        gather_on_vector(1, 1, 2, SPLIT)
         gather_on_scalar(1, 0, LAST_ROW)
         gather_on_scalar(1, 1, LAST_ROW)
         gate_and_mix(1, 0)

@@ -10,7 +10,6 @@ U16 = mybir.dt.uint16
 U8 = mybir.dt.uint8
 FP8X4 = mybir.dt.float8_e4m3fn_x4
 MULT = mybir.AluOpType.mult
-ADD = mybir.AluOpType.add
 COPY = mybir.ActivationFunctionType.Copy
 
 K, T, E, C, N = 128, 1024, 8, 128, 1536
@@ -30,6 +29,10 @@ ALIGN = 256
 RUN = 4
 W_PITCH = PACK * K + 64
 LAST_PASS_ROWS = (3, 0, 1, 2)
+SPLIT = 64
+SHARE = 96
+UNDER_ROWS6 = 2048
+PAIR = 2
 GROUPS = ((0, 3), (3, 2), (5, 1), (6, 1), (7, 1))
 
 FLOPS = 2 * K * N * S
@@ -46,7 +49,6 @@ def tile_moe_bdx_lin_none_kernel(tc, dyT, w, gate, offs, out):
         offsets = keep.tile([P, S // LIST_ROWS], U16, name="offsets")
         identity = keep.tile([P, P], F32, align_bytes=ALIGN, name="identity")
         zero = keep.tile([P, 1], F32, name="zero")
-        gate_cols = keep.tile([P, 2, PACK], F32, align_bytes=ALIGN, name="gate_cols")
         gates = [psum.tile([P, HALF], F32, name=f"gates{h}") for h in range(2)]
 
         windows = {}
@@ -55,42 +57,54 @@ def tile_moe_bdx_lin_none_kernel(tc, dyT, w, gate, offs, out):
             for t in range(PACK):
                 spare = PLANES if (c, t) == (LAST, final_row) else 0
                 if (c, t) == (LAST, 0):
-                    rows = tail.tile([P, T], F32, align_bytes=ALIGN, offset=0, name=f"win{c}{t}")
+                    rows = tail.tile([P, T], F32, align_bytes=ALIGN, offset=UNDER_ROWS6, name=f"win{c}{t}")
                 else:
                     rows = keep.tile([P, T + spare], F32, align_bytes=ALIGN, name=f"win{c}{t}")
                 windows[c, t] = rows[:, 0:T]
                 if spare > 0:
-                    long_window = rows[:, 0 : T + LAST_ROW * HALF]
+                    long_window = rows[:, 0 : T + final_row * HALF]
                     behind = rows[:, T : T + PLANES].rearrange("p (t s) -> p t s", t=PACK)
-        planes = {(0, 0): behind, (LAST, 1): behind}
-        for c, h in ((0, 1), (1, 0), (1, 1), (LAST, 0)):
+        planes = {(0, 1): behind, (LAST, 1): behind}
+        for c, h in ((0, 0), (1, 0), (1, 1), (LAST, 0)):
             own = keep.tile([P, PACK, HALF], F32, align_bytes=ALIGN, name=f"planes{c}{h}")
             planes[c, h] = own[:]
+        gate_cols = planes[0, 0][:, PAIR:PACK, 0:PACK]
         pool_gates = keep.tile([P, HALF], F32, align_bytes=ALIGN, name="pool_gates")
 
         early = keep.tile([P, 2 * PLANES], BF16, align_bytes=ALIGN, name="early")
-        joint = keep.tile([P, PLANES + 2 * W_COLS], BF16, align_bytes=ALIGN, name="joint")
-        own = keep.tile([P, PLANES], BF16, align_bytes=ALIGN, name="mixed11")
-        g_mixed = {(c, 0): early[:, c * PLANES : (c + 1) * PLANES] for c in range(LAST)}
-        g_mixed[0, 1] = joint[:, 0:PLANES]
-        g_mixed[1, 1] = own[:]
+        pooled = keep.tile([P, 2 * PLANES], BF16, align_bytes=ALIGN, name="pooled")
+        late = keep.tile([P, PLANES + W_COLS], BF16, align_bytes=ALIGN, name="late")
+        g_mixed = {(c, 1): early[:, c * PLANES : (c + 1) * PLANES] for c in range(LAST)}
+        for c in range(LAST):
+            g_mixed[c, 0] = pooled[:, c * PLANES : (c + 1) * PLANES]
+        g_mixed[LAST, 0] = late[:, PLANES // 2 : PLANES // 2 + PLANES]
+        g_mixed[LAST, 1] = late[:, 0:PLANES]
 
         def reused(values):
             return values.rearrange("p t s -> p (t s)").bitcast(BF16)
 
-        late = keep.tile([P, PLANES + W_COLS], BF16, align_bytes=ALIGN, name="late")
-        g_mixed[LAST, 0] = late[:, PLANES // 2 : PLANES // 2 + PLANES]
-        g_mixed[LAST, 1] = late[:, 0:PLANES]
-        w_mixed = {e: joint[:, PLANES + e * W_COLS : PLANES + (e + 1) * W_COLS] for e in range(2)}
-        w_mixed[2] = early[:, 0:W_COLS]
-        w_mixed[3] = joint[:, 0:W_COLS]
-        w_mixed[4] = late[:, PLANES : PLANES + W_COLS]
-        w_mixed[7] = late[:, 0:W_COLS]
-        w_mixed[5] = reused(behind)[:, 0:W_COLS]
-        w_mixed[6] = reused(behind)[:, W_COLS : 2 * W_COLS]
+        first = keep.tile([P, 2 * W_COLS], BF16, align_bytes=ALIGN, name="rows0")
+        third = keep.tile([P, 2 * K_PASS], BF16, align_bytes=ALIGN, name="rows9")
+        filler = tail.tile([P, K_PASS], BF16, align_bytes=ALIGN, offset=0, name="row11")
+        runs = {
+            0: first[:],
+            6: early[:, 0:W_COLS],
+            9: third[:],
+            11: filler[:],
+            12: late[:, PLANES : PLANES + W_COLS],
+            15: reused(behind)[:, 0 : 2 * W_COLS],
+            21: late[:, 0:W_COLS],
+        }
+
+        def mixed(row, n):
+            start = max(r for r in runs if r <= row)
+            return runs[start][:, (row - start) * K_PASS : (row - start + n) * K_PASS]
 
         padded = keep.tile([P, E * PASSES, W_PITCH], F32, align_bytes=ALIGN, name="w_raw")
-        w_raw = [padded[:, e * PASSES : (e + 1) * PASSES, 0 : PACK * K] for e in range(E)]
+
+
+        def raw(row, n):
+            return padded[:, row : row + n, 0 : PACK * K]
 
         def packed(words, name, pool=keep, offset=None):
             codes = pool.tile([P, words], U32, align_bytes=ALIGN, offset=offset, name=f"codes_{name}")
@@ -101,17 +115,21 @@ def tile_moe_bdx_lin_none_kernel(tc, dyT, w, gate, offs, out):
             return pair[0][:, start : start + words], pair[1][:, start : start + words]
 
         early_q = packed(LAST * HALF, "early")
-        g_q = {(c, 0): part(early_q, c * HALF, HALF) for c in range(LAST)}
-        joint_q = packed(HALF + 2 * PASSES * K, "joint")
-        g_q[0, 1] = part(joint_q, 0, HALF)
-        g_q[1, 1] = packed(HALF, "g11", tail, 0)
+        g_q = {(c, 1): part(early_q, c * HALF, HALF) for c in range(LAST)}
+        pooled_q = packed(LAST * HALF, "pooled")
+        for c in range(LAST):
+            g_q[c, 0] = part(pooled_q, c * HALF, HALF)
         for h in range(2):
             g_q[LAST, h] = packed(HALF, f"last{h}")
-        w_q = {e: part(joint_q, HALF + e * PASSES * K, PASSES * K) for e in range(2)}
-        for e in range(3, E):
-            w_q[e] = packed(PASSES * K, f"w{e}")
-        w_q[2] = packed(PASSES * K, "w2", tail, 4 * T)
-        filler = tail.tile([P, K_PASS], BF16, align_bytes=ALIGN, offset=4 * T, name="last_pass3")
+        runs_q = {e * PASSES: packed(PASSES * K, f"w{e}") for e in range(3, E)}
+        runs_q[0] = packed(4 * K, "rows0", tail, UNDER_ROWS6)
+        runs_q[4] = packed(2 * K, "rows4")
+        runs_q[6] = packed(3 * K, "rows6", tail, 0)
+
+        def w_q(row, n):
+            start = max(r for r in runs_q if r <= row)
+            return part(runs_q[start], (row - start) * K, n * K)
+
         result = keep.tile([P, T], F32, align_bytes=ALIGN, name="result")
         slots = keep.tile([P, S], F32, align_bytes=ALIGN, name="slots")
 
@@ -122,7 +140,7 @@ def tile_moe_bdx_lin_none_kernel(tc, dyT, w, gate, offs, out):
             nc.sync.dma_start(out=windows[c, t], in_=dy_rows[c, :, t])
 
         def load_weights(row, n):
-            nc.sync.dma_start(out=padded[:, row : row + n, 0 : PACK * K], in_=w_rows[:, row : row + n])
+            nc.sync.dma_start(out=raw(row, n), in_=w_rows[:, row : row + n])
 
         def spread_gates(h):
             for j in range(PACK):
@@ -148,43 +166,31 @@ def tile_moe_bdx_lin_none_kernel(tc, dyT, w, gate, offs, out):
                 MULT,
             )
 
-        def gate_on_pool(c, h):
+        def gate_on_pool(c, h, t0, n=HALF):
             nc.gpsimd.tensor_tensor(
-                g_mixed[c, h].rearrange("p (s t) -> p s t", t=PACK),
-                planes[c, h].rearrange("p t s -> p s t"),
-                pool_gates[:].unsqueeze(2).to_broadcast([P, HALF, PACK]),
+                g_mixed[c, h].rearrange("p (s t) -> p s t", t=PACK)[:, 0:n, t0 : t0 + PAIR],
+                planes[c, h][:, t0 : t0 + PAIR, 0:n].rearrange("p t s -> p s t"),
+                pool_gates[:, 0:n].unsqueeze(2).to_broadcast([P, n, PAIR]),
                 MULT,
             )
 
         def quantise(src, pair):
             nc.vector.quantize_mx(out=pair[0].bitcast(FP8X4), scales=pair[1], in_=src)
 
-        def mix_on_vector(e, c0=0, n=PASSES):
-            nc.vector.tensor_copy(
-                out=w_mixed[e][:, c0 * K_PASS : (c0 + n) * K_PASS].rearrange(
-                    "p (c x r t) -> p x c t r", c=n, r=RUN, t=PACK
-                ),
-                in_=w_raw[e][:, c0 : c0 + n].rearrange("p c (t x r) -> p x c t r", r=RUN, t=PACK),
+        def mix(copy, row, n):
+            copy(
+                out=mixed(row, n).rearrange("p (c x r t) -> p x c t r", c=n, r=RUN, t=PACK),
+                in_=raw(row, n).rearrange("p c (t x r) -> p x c t r", r=RUN, t=PACK),
             )
 
-        def mix_on_scalar(dst, e, c0, n):
-            nc.scalar.copy(
-                out=dst.rearrange("p (c x r t) -> p x c t r", c=n, r=RUN, t=PACK),
-                in_=w_raw[e][:, c0 : c0 + n].rearrange("p c (t x r) -> p x c t r", r=RUN, t=PACK),
+        def mix_on_pool(row, n):
+            nc.gpsimd.tensor_copy(
+                out=mixed(row, n).rearrange("p (c k t) -> p c k t", c=n, t=PACK),
+                in_=raw(row, n).rearrange("p c (t k) -> p c k t", t=PACK),
             )
 
-        def mix_on_pool(e):
-            nc.gpsimd.tensor_scalar(
-                w_mixed[e].rearrange("p (c k t) -> p c k t", c=PASSES, t=PACK),
-                w_raw[e].rearrange("p c (t k) -> p c k t", t=PACK),
-                1.0,
-                0.0,
-                MULT,
-                ADD,
-            )
-
-        def quantise_w(e, c0=0, n=PASSES):
-            quantise(w_mixed[e][:, c0 * K_PASS : (c0 + n) * K_PASS], part(w_q[e], c0 * K, n * K))
+        def quantise_w(row, n):
+            quantise(mixed(row, n), w_q(row, n))
 
         def multiply(group):
             e0, count = GROUPS[group]
@@ -192,7 +198,7 @@ def tile_moe_bdx_lin_none_kernel(tc, dyT, w, gate, offs, out):
             for e in range(e0, e0 + count):
                 h, s0 = divmod(e * C, HALF)
                 for c in range(PASSES):
-                    w_codes, w_scales = part(w_q[e], c * K, K)
+                    w_codes, w_scales = w_q(e * PASSES + c, 1)
                     g_codes, g_scales = part(g_q[c, h], s0, C)
                     nc.tensor.matmul_mx(
                         out=sums[:, (e - e0) * C : (e - e0 + 1) * C],
@@ -218,9 +224,11 @@ def tile_moe_bdx_lin_none_kernel(tc, dyT, w, gate, offs, out):
             empty_bank(group, sums, copy)
             scatter(group)
 
+        on_vector, on_scalar = nc.vector.tensor_copy, nc.scalar.copy
+
         load_window(0, 0)
         nc.sync.dma_start(offsets[:], offs)
-        nc.sync.dma_start(out=gate_cols[:], in_=gate[0, :].rearrange("(h p j) -> p h j", p=P, j=PACK))
+        nc.sync.dma_start(out=gate_cols, in_=gate[0, :].rearrange("(h p j) -> p h j", p=P, j=PACK))
         for t in range(1, PACK):
             load_window(0, t)
         for t in range(PACK):
@@ -242,57 +250,66 @@ def tile_moe_bdx_lin_none_kernel(tc, dyT, w, gate, offs, out):
             spread_gates(h)
 
         for t in range(PACK):
-            gather_on_scalar(0, 0, t)
-            gather_on_vector(0, 1, t)
-        nc.vector.tensor_copy(out=pool_gates[:], in_=gates[0][:])
-        gate_on_pool(0, 0)
+            gather_on_scalar(0, 1, t)
+            if t == PAIR:
+                nc.vector.tensor_copy(out=pool_gates[:], in_=gates[0][:])
+                gate_on_pool(0, 0, 0)
+            gather_on_vector(0, 0, t)
+        gate_on_pool(0, 0, PAIR)
         gate_and_mix(0, 1)
-        for t in range(LAST_ROW):
+        for t in range(PAIR):
             gather_on_scalar(1, 0, t)
             gather_on_vector(1, 1, t)
+        gate_on_pool(1, 0, 0, SHARE)
+        gather_on_scalar(1, 0, 2)
+        gather_on_scalar(1, 1, 2, SPLIT)
+        gather_on_vector(1, 1, 2, SPLIT)
         gather_on_scalar(1, 0, LAST_ROW)
         gather_on_scalar(1, 1, LAST_ROW)
-        gate_and_mix(1, 0)
+        gate_on_pool(1, 0, PAIR, SHARE)
+        gate_and_mix(1, 0, SHARE, HALF - SHARE)
         gate_and_mix(1, 1)
-        mix_on_pool(0)
-        mix_on_pool(1)
-        quantise(joint[:, 0 : 2 * PLANES], part(joint_q, 0, 2 * HALF))
+        mix_on_pool(0, PASSES)
+        mix_on_pool(PASSES, PASSES)
+        quantise(pooled[:], pooled_q)
         quantise(early[:], early_q)
-        quantise_w(1, 1, LAST)
+        quantise_w(4, 2)
 
         gather_on_scalar(LAST, 0, LAST_PASS_ROWS[0])
         gather_on_scalar(LAST, 1, LAST_PASS_ROWS[0])
-        for h in range(2):
-            for t in LAST_PASS_ROWS[1:]:
-                gather_on_scalar(LAST, h, t)
+        for t in LAST_PASS_ROWS[1:]:
+            gather_on_scalar(LAST, 0, t)
+        gather_on_scalar(LAST, 1, final_row)
+        for t in LAST_PASS_ROWS[1:-1]:
+            gather_on_scalar(LAST, 1, t)
         gate_and_mix(LAST, 0)
-        mix_on_pool(2)
-        quantise(g_mixed[1, 1], g_q[1, 1])
+        mix_on_pool(6, 3)
+        quantise_w(0, 4)
         quantise(g_mixed[LAST, 0], g_q[LAST, 0])
-        quantise_w(2)
-        mix_on_scalar(w_mixed[3][:, 0 : LAST * K_PASS], 3, 0, LAST)
-        empty_bank(0, multiply(0), nc.scalar.copy)
-        mix_on_scalar(filler[:], 3, LAST, 1)
+        quantise_w(6, 3)
+        mix(on_scalar, 9, 2)
+        empty_bank(0, multiply(0), on_scalar)
+        mix(on_scalar, 11, 1)
         scatter(0)
         gate_and_mix(LAST, 1)
-        mix_on_pool(4)
-        quantise_w(3, 0, LAST)
-        quantise(filler[:], part(w_q[3], LAST * K, K))
+        mix_on_pool(12, 3)
+        quantise_w(9, 2)
+        quantise_w(11, 1)
         quantise(g_mixed[LAST, 1], g_q[LAST, 1])
-        quantise_w(4)
-        put_back(1, multiply(1), nc.scalar.copy)
-        mix_on_vector(5)
-        mix_on_vector(6, 0, 1)
-        quantise_w(5)
+        quantise_w(12, 3)
+        put_back(1, multiply(1), on_scalar)
+        mix(on_vector, 15, 3)
+        mix(on_vector, 18, 1)
+        quantise_w(15, 3)
         sums = multiply(2)
-        mix_on_vector(6, 1, LAST)
-        mix_on_vector(7, 0, 1)
-        put_back(2, sums, nc.scalar.copy)
-        quantise_w(6)
+        mix(on_vector, 19, 2)
+        mix(on_vector, 21, 1)
+        put_back(2, sums, on_scalar)
+        quantise_w(18, 3)
         sums = multiply(3)
-        mix_on_vector(7, 1, LAST)
-        quantise_w(7, 0, 1)
-        put_back(3, sums, nc.scalar.copy)
-        quantise_w(7, 1, LAST)
-        put_back(4, multiply(4), nc.vector.tensor_copy)
+        mix(on_vector, 22, 2)
+        quantise_w(21, 1)
+        put_back(3, sums, on_scalar)
+        quantise_w(22, 2)
+        put_back(4, multiply(4), on_vector)
         nc.sync.dma_start(out=out, in_=result[:])

@@ -29,7 +29,6 @@ ALIGN = 256
 RUN = 4
 W_PITCH = PACK * K + 64
 LAST_PASS_ROWS = (3, 0, 1, 2)
-SPLIT = 64
 SHARE = 96
 UNDER_ROWS6 = 2048
 PAIR = 2
@@ -262,8 +261,7 @@ def tile_moe_bdx_lin_none_kernel(tc, dyT, w, gate, offs, out):
             gather_on_vector(1, 1, t)
         gate_on_pool(1, 0, 0, SHARE)
         gather_on_scalar(1, 0, 2)
-        gather_on_scalar(1, 1, 2, SPLIT)
-        gather_on_vector(1, 1, 2, SPLIT)
+        gather_on_vector(1, 1, 2)
         gather_on_scalar(1, 0, LAST_ROW)
         gather_on_scalar(1, 1, LAST_ROW)
         gate_on_pool(1, 0, PAIR, SHARE)

from contextlib import ExitStack

import concourse.mybir as mybir
from concourse.masks import make_identity

F32 = mybir.dt.float32
BF16 = mybir.dt.bfloat16
U32 = mybir.dt.uint32
U16 = mybir.dt.uint16
U8 = mybir.dt.uint8
FP8X4 = mybir.dt.float8_e4m3fn_x4
MULT = mybir.AluOpType.mult
COPY = mybir.ActivationFunctionType.Copy

K, T, E, C, N = 128, 1024, 8, 128, 1536
S = E * C
P = 128
PACK = 4
K_PASS = P * PACK
PASSES = N // K_PASS
LAST = PASSES - 1
LAST_ROW = PACK - 1
HALF = S // 2
PLANES = PACK * HALF
W_COLS = PASSES * PACK * K
LIST_ROWS = 16
ALIGN = 256

RUN = 4
W_PITCH = PACK * K + 64
LAST_PASS_ROWS = (3, 0, 1, 2)
SHARE = 96
UNDER_ROWS6 = 2048
PAIR = 2
GROUPS = ((0, 3), (3, 2), (5, 1), (6, 1), (7, 1))

FLOPS = 2 * K * N * S
BYTES = 4 * (N * T + E * N * K + K * T + S) + 2 * S


def tile_moe_bdx_lin_none_kernel(tc, dyT, w, gate, offs, out):
    nc = tc.nc
    with ExitStack() as ctx:
        keep = ctx.enter_context(tc.tile_pool(name="keep", bufs=1))
        tail = ctx.enter_context(tc.tile_pool(name="tail", bufs=1))
        psum = ctx.enter_context(tc.psum_pool(name="psum", bufs=1))

        offsets = keep.tile([P, S // LIST_ROWS], U16, name="offsets")
        identity = keep.tile([P, P], F32, align_bytes=ALIGN, name="identity")
        zero = keep.tile([P, 1], F32, name="zero")
        gates = [psum.tile([P, HALF], F32, name=f"gates{h}") for h in range(2)]

        windows = {}
        final_row = LAST_PASS_ROWS[-1]
        for c in range(PASSES):
            for t in range(PACK):
                spare = PLANES if (c, t) == (LAST, final_row) else 0
                if (c, t) == (LAST, 0):
                    rows = tail.tile([P, T], F32, align_bytes=ALIGN, offset=UNDER_ROWS6, name=f"win{c}{t}")
                else:
                    rows = keep.tile([P, T + spare], F32, align_bytes=ALIGN, name=f"win{c}{t}")
                windows[c, t] = rows[:, 0:T]
                if spare > 0:
                    long_window = rows[:, 0 : T + final_row * HALF]
                    behind = rows[:, T : T + PLANES].rearrange("p (t s) -> p t s", t=PACK)
        planes = {(0, 1): behind, (LAST, 1): behind}
        for c, h in ((0, 0), (1, 0), (1, 1), (LAST, 0)):
            own = keep.tile([P, PACK, HALF], F32, align_bytes=ALIGN, name=f"planes{c}{h}")
            planes[c, h] = own[:]
        gate_cols = planes[0, 0][:, PAIR:PACK, 0:PACK]
        pool_gates = keep.tile([P, HALF], F32, align_bytes=ALIGN, name="pool_gates")

        early = keep.tile([P, 2 * PLANES], BF16, align_bytes=ALIGN, name="early")
        pooled = keep.tile([P, 2 * PLANES], BF16, align_bytes=ALIGN, name="pooled")
        late = keep.tile([P, PLANES + W_COLS], BF16, align_bytes=ALIGN, name="late")
        g_mixed = {(c, 1): early[:, c * PLANES : (c + 1) * PLANES] for c in range(LAST)}
        for c in range(LAST):
            g_mixed[c, 0] = pooled[:, c * PLANES : (c + 1) * PLANES]
        g_mixed[LAST, 0] = late[:, PLANES // 2 : PLANES // 2 + PLANES]
        g_mixed[LAST, 1] = late[:, 0:PLANES]

        def reused(values):
            return values.rearrange("p t s -> p (t s)").bitcast(BF16)

        first = keep.tile([P, 2 * W_COLS], BF16, align_bytes=ALIGN, name="rows0")
        third = keep.tile([P, 2 * K_PASS], BF16, align_bytes=ALIGN, name="rows9")
        filler = tail.tile([P, K_PASS], BF16, align_bytes=ALIGN, offset=0, name="row11")
        runs = {
            0: first[:],
            6: early[:, 0:W_COLS],
            9: third[:],
            11: filler[:],
            12: late[:, PLANES : PLANES + W_COLS],
            15: reused(behind)[:, 0 : 2 * W_COLS],
            21: late[:, 0:W_COLS],
        }

        def mixed(row, n):
            start = max(r for r in runs if r <= row)
            return runs[start][:, (row - start) * K_PASS : (row - start + n) * K_PASS]

        padded = keep.tile([P, E * PASSES, W_PITCH], F32, align_bytes=ALIGN, name="w_raw")


        def raw(row, n):
            return padded[:, row : row + n, 0 : PACK * K]

        def packed(words, name, pool=keep, offset=None):
            codes = pool.tile([P, words], U32, align_bytes=ALIGN, offset=offset, name=f"codes_{name}")
            scales = keep.tile([P, words], U8, align_bytes=ALIGN, name=f"scales_{name}")
            return codes[:], scales[:]

        def part(pair, start, words):
            return pair[0][:, start : start + words], pair[1][:, start : start + words]

        early_q = packed(LAST * HALF, "early")
        g_q = {(c, 1): part(early_q, c * HALF, HALF) for c in range(LAST)}
        pooled_q = packed(LAST * HALF, "pooled")
        for c in range(LAST):
            g_q[c, 0] = part(pooled_q, c * HALF, HALF)
        for h in range(2):
            g_q[LAST, h] = packed(HALF, f"last{h}")
        runs_q = {e * PASSES: packed(PASSES * K, f"w{e}") for e in range(3, E)}
        runs_q[0] = packed(4 * K, "rows0", tail, UNDER_ROWS6)
        runs_q[4] = packed(2 * K, "rows4")
        runs_q[6] = packed(3 * K, "rows6", tail, 0)

        def w_q(row, n):
            start = max(r for r in runs_q if r <= row)
            return part(runs_q[start], (row - start) * K, n * K)

        result = keep.tile([P, T], F32, align_bytes=ALIGN, name="result")
        slots = keep.tile([P, S], F32, align_bytes=ALIGN, name="slots")

        dy_rows = dyT.rearrange("(c p t) x -> c p t x", p=P, t=PACK)
        w_rows = w.rearrange("e (c p t) k -> p (e c) (t k)", p=P, t=PACK)

        def load_window(c, t):
            nc.sync.dma_start(out=windows[c, t], in_=dy_rows[c, :, t])

        def load_weights(row, n):
            nc.sync.dma_start(out=raw(row, n), in_=w_rows[:, row : row + n])

        def spread_gates(h):
            for j in range(PACK):
                column = gate_cols[:, h, j : j + 1].to_broadcast([P, P])
                nc.tensor.transpose(gates[h][:, j::PACK], column, identity[:])

        def listed(s0, n):
            return offsets[:, s0 // LIST_ROWS : (s0 + n) // LIST_ROWS]

        def gather_on_scalar(c, h, t, n=HALF):
            window = long_window if (c, h, t) == (LAST, 0, final_row) else windows[c, t]
            nc.scalar.activation(planes[c, h][:, t, 0:n], window.indirect(listed(h * HALF, n)), COPY)

        def gather_on_vector(c, h, t, s0=0):
            nc.vector.tensor_copy(planes[c, h][:, t, s0:HALF], windows[c, t].indirect(listed(h * HALF + s0, HALF - s0)))

        def gate_and_mix(c, h, s0=0, n=HALF):
            by_slot = gates[h][:, s0 : s0 + n].rearrange("p (x r) -> p x r", r=RUN)
            nc.vector.tensor_tensor(
                g_mixed[c, h][:, s0 * PACK : (s0 + n) * PACK].rearrange("p (x r t) -> p x t r", r=RUN, t=PACK),
                planes[c, h][:, :, s0 : s0 + n].rearrange("p t (x r) -> p x t r", r=RUN),
                by_slot.unsqueeze(2).to_broadcast([P, n // RUN, PACK, RUN]),
                MULT,
            )

        def gate_on_pool(c, h, t0, n=HALF):
            nc.gpsimd.tensor_tensor(
                g_mixed[c, h].rearrange("p (s t) -> p s t", t=PACK)[:, 0:n, t0 : t0 + PAIR],
                planes[c, h][:, t0 : t0 + PAIR, 0:n].rearrange("p t s -> p s t"),
                pool_gates[:, 0:n].unsqueeze(2).to_broadcast([P, n, PAIR]),
                MULT,
            )

        def quantise(src, pair):
            nc.vector.quantize_mx(out=pair[0].bitcast(FP8X4), scales=pair[1], in_=src)

        def mix(copy, row, n):
            copy(
                out=mixed(row, n).rearrange("p (c x r t) -> p x c t r", c=n, r=RUN, t=PACK),
                in_=raw(row, n).rearrange("p c (t x r) -> p x c t r", r=RUN, t=PACK),
            )

        def mix_on_pool(row, n):
            nc.gpsimd.tensor_copy(
                out=mixed(row, n).rearrange("p (c k t) -> p c k t", c=n, t=PACK),
                in_=raw(row, n).rearrange("p c (t k) -> p c k t", t=PACK),
            )

        def quantise_w(row, n):
            quantise(mixed(row, n), w_q(row, n))

        def multiply(group):
            e0, count = GROUPS[group]
            sums = psum.tile([P, count * C], F32, name=f"sums{group}")
            for e in range(e0, e0 + count):
                h, s0 = divmod(e * C, HALF)
                for c in range(PASSES):
                    w_codes, w_scales = w_q(e * PASSES + c, 1)
                    g_codes, g_scales = part(g_q[c, h], s0, C)
                    nc.tensor.matmul_mx(
                        out=sums[:, (e - e0) * C : (e - e0 + 1) * C],
                        lhsT=w_codes.bitcast(FP8X4),
                        lhsT_scale=w_scales,
                        rhs=g_codes.bitcast(FP8X4),
                        rhs_scale=g_scales,
                        start=(c == 0),
                        stop=(c == LAST),
                    )
            return sums

        def empty_bank(group, sums, copy):
            e0, count = GROUPS[group]
            copy(out=slots[:, e0 * C : (e0 + count) * C], in_=sums[:])

        def scatter(group):
            e0, count = GROUPS[group]
            cols = slice(e0 * C, (e0 + count) * C)
            nc.scalar.activation(result[:].indirect(listed(e0 * C, count * C)), slots[:, cols], COPY)

        def put_back(group, sums, copy):
            empty_bank(group, sums, copy)
            scatter(group)

        on_vector, on_scalar = nc.vector.tensor_copy, nc.scalar.copy

        load_window(0, 0)
        nc.sync.dma_start(offsets[:], offs)
        nc.sync.dma_start(out=gate_cols, in_=gate[0, :].rearrange("(h p j) -> p h j", p=P, j=PACK))
        for t in range(1, PACK):
            load_window(0, t)
        for t in range(PACK):
            load_window(1, t)
        load_weights(0, PASSES)
        load_window(LAST, LAST_PASS_ROWS[0])
        load_weights(PASSES, PASSES)
        for t in LAST_PASS_ROWS[1:]:
            load_window(LAST, t)
        row = 2 * PASSES
        for n in (3, 3, 3, 4, 3, 2):
            load_weights(row, n)
            row += n

        nc.vector.memset(zero[:], 0.0)
        nc.scalar.activation(identity[:], zero[:].to_broadcast([P, P]), COPY)
        make_identity(nc, identity[:], nomemset=True)
        for h in range(2):
            spread_gates(h)

        for t in range(PACK):
            gather_on_scalar(0, 1, t)
            if t == PAIR:
                nc.vector.tensor_copy(out=pool_gates[:], in_=gates[0][:])
                gate_on_pool(0, 0, 0)
            gather_on_vector(0, 0, t)
        gate_on_pool(0, 0, PAIR)
        gate_and_mix(0, 1)
        for t in range(PAIR):
            gather_on_scalar(1, 0, t)
            gather_on_vector(1, 1, t)
        gate_on_pool(1, 0, 0, SHARE)
        gather_on_scalar(1, 0, 2)
        gather_on_vector(1, 1, 2)
        gather_on_scalar(1, 0, LAST_ROW)
        gather_on_scalar(1, 1, LAST_ROW)
        gate_on_pool(1, 0, PAIR, SHARE)
        gate_and_mix(1, 0, SHARE, HALF - SHARE)
        gate_and_mix(1, 1)
        mix_on_pool(0, PASSES)
        mix_on_pool(PASSES, PASSES)
        quantise(pooled[:], pooled_q)
        quantise(early[:], early_q)
        quantise_w(4, 2)

        gather_on_scalar(LAST, 0, LAST_PASS_ROWS[0])
        gather_on_scalar(LAST, 1, LAST_PASS_ROWS[0])
        for t in LAST_PASS_ROWS[1:]:
            gather_on_scalar(LAST, 0, t)
        gather_on_scalar(LAST, 1, final_row)
        for t in LAST_PASS_ROWS[1:-1]:
            gather_on_scalar(LAST, 1, t)
        gate_and_mix(LAST, 0)
        mix_on_pool(6, 3)
        quantise_w(0, 4)
        quantise(g_mixed[LAST, 0], g_q[LAST, 0])
        quantise_w(6, 3)
        mix(on_scalar, 9, 2)
        empty_bank(0, multiply(0), on_scalar)
        mix(on_scalar, 11, 1)
        scatter(0)
        gate_and_mix(LAST, 1)
        mix_on_pool(12, 3)
        quantise_w(9, 2)
        quantise_w(11, 1)
        quantise(g_mixed[LAST, 1], g_q[LAST, 1])
        quantise_w(12, 3)
        put_back(1, multiply(1), on_scalar)
        mix(on_vector, 15, 3)
        mix(on_vector, 18, 1)
        quantise_w(15, 3)
        sums = multiply(2)
        mix(on_vector, 19, 2)
        mix(on_vector, 21, 1)
        put_back(2, sums, on_scalar)
        quantise_w(18, 3)
        sums = multiply(3)
        mix(on_vector, 22, 2)
        quantise_w(21, 1)
        put_back(3, sums, on_scalar)
        quantise_w(22, 2)
        put_back(4, multiply(4), on_vector)
        nc.sync.dma_start(out=out, in_=result[:])
